import numpy as np
import ml_dtypes


def mxq(x, axis, fmt="e4m3"):
    dtype, down = {"e4m3": (ml_dtypes.float8_e4m3fn, 7), "e5m2": (ml_dtypes.float8_e5m2, 14)}[fmt]
    v = np.moveaxis(np.asarray(x, np.float32).astype(ml_dtypes.bfloat16).astype(np.float64), axis, -1)
    blocks = v.reshape(v.shape[:-1] + (-1, 32))
    amax = np.abs(blocks).max(-1, keepdims=True)
    byte = np.maximum(np.where(amax > 0, np.frexp(amax)[1] - 1 + 127, 0) - down, 1)
    scale = np.exp2(byte - 127.0)
    codes = (blocks / scale).astype(np.float32).astype(dtype).astype(np.float64)
    return np.moveaxis((codes * scale).reshape(v.shape), -1, axis)


WIDE = False


def mx_kscale(k):
    if not WIDE:
        return np.ones(k)
    levels = np.array([10, -10, 5, -5, 0])
    if k % 512:
        return np.exp2(np.random.permutation(np.resize(levels, k // 32))).repeat(32)
    a = np.empty((k // 512, 16))
    for p in range(k // 512):
        a[p, :8] = np.random.permutation(np.resize(levels, 8))
        for g in range(8):
            far = levels[np.abs(levels - a[p, g]) >= 10]
            a[p, g + 8] = far[np.random.randint(len(far))]
    return np.exp2(a.ravel()).repeat(32)


BF16 = ml_dtypes.bfloat16


def bf(x):
    return np.asarray(x, np.float32).astype(BF16)


def f64(x):
    return np.asarray(x).astype(np.float64)


E2M1 = np.array([0.0, 0.5, 1.0, 1.5, 2.0, 3.0, 4.0, 6.0, -0.0, -0.5, -1.0, -1.5, -2.0, -3.0, -4.0, -6.0])


def pack_weight(w, fmt):
    k, n = w.shape
    w = f64(bf(w)).reshape(k // 32, 32, n)
    amax = np.abs(w).max(1)
    if fmt == "e4m3":
        byte = np.frexp(amax)[1] - 1 + 127 - 7
    else:
        mant, ex = np.frexp(amax / 6.0)
        byte = np.where(mant > 0.5, ex, ex - 1) + 127
    byte = np.clip(np.where(amax > 0, byte, 1), 1, 254)
    scaled = (w * np.exp2(127.0 - byte)[:, None, :]).reshape(k, n).astype(np.float32)
    by_word = np.ascontiguousarray(scaled.reshape(k // 512, 128, 4, n).transpose(0, 1, 3, 2))
    if fmt == "e4m3":
        words = by_word.astype(ml_dtypes.float8_e4m3fn).view(np.uint8)
    else:
        c = by_word.astype(ml_dtypes.float4_e2m1fn).view(np.uint8) & 0xF
        words = c[..., 0::2] | (c[..., 1::2] << 4)
    return np.ascontiguousarray(words), np.ascontiguousarray(byte.astype(np.uint8).reshape(k // 512, 16, n))


def unpack_weight(words, scales, fmt):
    g, p, n, _ = words.shape
    if fmt == "e4m3":
        vals = np.ascontiguousarray(words).view(ml_dtypes.float8_e4m3fn).astype(np.float64)
    else:
        nib = np.empty((g, p, n, 4), np.uint8)
        nib[..., 0::2] = words & 0xF
        nib[..., 1::2] = words >> 4
        vals = E2M1[nib]
    vals = vals * np.repeat(np.exp2(scales.astype(np.float64) - 127.0), 8, axis=1)[..., None]
    return vals.transpose(0, 1, 3, 2).reshape(g * 512, n)
def pack4(w):
    words, scales = pack_weight(w, "e2m1")
    return words.reshape(words.shape[0], 128, -1), scales


def unpack4(words, scales):
    return unpack_weight(words.reshape(words.shape[0], 128, -1, 2), scales, "e2m1")


M, R, B = 2048, 1024, 512

E_MIN = 0.5


def draw0():
    s, t = mx_kscale(R), mx_kscale(M)
    phi = np.random.standard_normal((M, R)) * s * t[:, None]
    coef = np.random.standard_normal((R, B)) / np.sqrt(R) / s[:, None]
    energy = np.sqrt(E_MIN ** 2 + np.random.standard_normal((M, B)) ** 2)
    v = np.random.standard_normal((M, M)) / np.sqrt(M) / t[:, None]
    v_words, v_scales = pack4(v)
    return {"phi": bf(phi),
            "coef": bf(coef),
            "energy": bf(energy),
            "v_words": v_words,
            "v_scales": v_scales}


def core(phi, coef, energy, v_words, v_scales):
    gap = mxq(f64(phi), 1, "e4m3") @ mxq(f64(coef), 0, "e4m3")
    e = f64(energy)
    h = gap * np.tanh(e) / e
    v = unpack4(v_words, v_scales)
    return v.T @ mxq(h, 0, "e4m3")


def e4m3fn_bytes(y):
    return np.clip(np.asarray(y, np.float64), -448.0, 448.0).astype(np.float32).astype(ml_dtypes.float8_e4m3fn).view(np.uint8)


def e4m3fn_values(b):
    return np.asarray(b, np.uint8).view(ml_dtypes.float8_e4m3fn).astype(np.float64)


def setup_inputs():
    d = draw0()
    x0 = np.asarray(d['coef']).astype(np.float64)
    s = (np.max(np.abs(x0), axis=(1,), keepdims=True) / 448.0).astype(np.float32)
    out = {}
    for k, v in d.items():
        if k == 'coef':
            out['coef_bytes'] = e4m3fn_bytes(x0 / s.astype(np.float64))
            out['coef_scale'] = s
        else:
            out[k] = v
    return out


def reference(phi, coef_bytes, coef_scale, energy, v_words, v_scales):
    return core(phi, e4m3fn_values(coef_bytes) * coef_scale.astype(np.float64), energy, v_words, v_scales)

@@ -1,0 +1,430 @@
+from contextlib import ExitStack
+
+import concourse.mybir as mybir
+from concourse.masks import make_identity
+
+M, R, B = 2048, 1024, 512
+FLOPS = 2 * M * R * B + 2 * M * M * B
+
+F32 = mybir.dt.float32
+BF16 = mybir.dt.bfloat16
+U32 = mybir.dt.uint32
+I32 = mybir.dt.int32
+U8 = mybir.dt.uint8
+FP8 = mybir.dt.float8_e4m3fn
+FP8X4 = mybir.dt.float8_e4m3fn_x4
+FP4X4 = mybir.dt.float4_e2m1fn_x4
+ACT = mybir.ActivationFunctionType
+MULT = mybir.AluOpType.mult
+
+P = 128
+G = M // 512
+PASSES = R // 512
+NC = 128
+CH = B // NC
+
+
+def tile_bcs_gap_step_s13_kernel(tc, phi, coef_bytes, coef_scale, energy, v_words, v_scales, out):
+    nc = tc.nc
+    with ExitStack() as ctx:
+        keep = ctx.enter_context(tc.tile_pool(name="keep", bufs=1))
+        stage = ctx.enter_context(tc.tile_pool(name="stage", bufs=3))
+        ps_x = ctx.enter_context(tc.psum_pool(name="ps_x", bufs=8))
+
+        en = keep.tile([P, G, 4, B], BF16, name="en", align_bytes=64)
+        ph = keep.tile([P, G, 4, R], BF16, name="ph", align_bytes=64)
+        cb = keep.tile([P, PASSES, 4, B], U8, name="cb", align_bytes=64)
+        cs = keep.tile([P, PASSES, 4], F32, name="cs", align_bytes=64)
+        vw = keep.tile([P, G, 2 * M], U8, name="vw", align_bytes=64)
+        vs = keep.tile([P, G, M], U8, name="vs", align_bytes=64)
+
+        phi_v = phi.rearrange("(g p t) k -> g p t k", p=P, t=4)
+        en_v = energy.rearrange("(g p t) n -> g p t n", p=P, t=4)
+        cb_v = coef_bytes.rearrange("(g p t) n -> p g (t n)", p=P, t=4)
+        cs_v = coef_scale.rearrange("(g p t) o -> p g (t o)", p=P, t=4)
+        out_v = out.rearrange("(q i p) (c n) -> q c p i n", i=4, p=P, n=NC)
+
+        def load_en(g):
+            nc.sync.dma_start(out=en[:, g, :, :], in_=en_v[g])
+
+        def load_phi(g, t0, t1):
+            nc.sync.dma_start(out=ph[:, g, t0:t1, :], in_=phi_v[g][:, t0:t1, :])
+
+        def load_cb(k):
+            nc.sync.dma_start(out=cb[:, k, :, :].rearrange("p t n -> p (t n)"), in_=cb_v[:, k, :])
+
+        warm = keep.tile([P, 1], F32, name="warm")
+        nc.vector.memset(warm[:], 1.0)
+        nc.scalar.activation(out=warm[:], in_=warm[:], func=ACT.Abs_reciprocal_sqrt)
+        ident = keep.tile([P, P], F32, name="ident", align_bytes=64)
+        make_identity(nc, ident[:])
+        nc.gpsimd.memset(vs[:].rearrange("p g n -> p (g n)").bitcast(U32), 0)
+
+        nc.sync.dma_start(out=cs[:], in_=cs_v)
+        load_cb(0)
+        load_en(0)
+        load_cb(1)
+        load_phi(0, 0, 2)
+        load_phi(0, 2, 4)
+        load_en(1)
+        load_phi(1, 0, 2)
+        load_en(2)
+        load_phi(1, 2, 4)
+        load_en(3)
+        load_phi(2, 0, 2)
+        load_phi(2, 2, 4)
+        load_phi(3, 0, 2)
+        load_phi(3, 2, 4)
+        for quad in range(4):
+            nc.sync.dma_start(
+                out=vs[32 * quad : 32 * quad + 4, :, :].bitcast(I32),
+                in_=v_scales[:, 4 * quad : 4 * quad + 4, :].rearrange("g r n -> r g n").bitcast(I32),
+            )
+        for g in range(G):
+            nc.sync.dma_start(out=vw[:, g, :], in_=v_words[g])
+
+        cc = keep.tile([P, PASSES, B], U32, name="cc", align_bytes=64)
+        csc = keep.tile([P, PASSES, B], U8, name="csc", align_bytes=64)
+        wide = keep.tile([P, PASSES, 4, B], BF16, name="wide", align_bytes=64)
+        cgrp = keep.tile([P, PASSES, B, 4], BF16, name="cgrp", align_bytes=64)
+        qr = keep.tile([P, G * 4, B], F32, name="qr", align_bytes=64)
+        pc = keep.tile([P, G * 4, PASSES, P], U32, name="pc", align_bytes=64)
+        psc = keep.tile([P, G * 4, PASSES, P], U8, name="psc", align_bytes=64)
+
+        def coef_widen(k, on_scalar):
+            for t in range(4):
+                if on_scalar:
+                    nc.scalar.activation(out=wide[:, k, t, :], in_=cb[:, k, t, :].bitcast(FP8), func=ACT.Copy, scale=cs[:, k, t : t + 1])
+                else:
+                    nc.vector.tensor_scalar(
+                        out=wide[:, k, t, :], in0=cb[:, k, t, :].bitcast(FP8), scalar1=cs[:, k, t : t + 1], scalar2=None, op0=MULT
+                    )
+
+        def coef_interleave(k):
+            nc.vector.tensor_copy(
+                out=cgrp[:, k, :, :].rearrange("p (c i) t -> p c t i", i=4),
+                in_=wide[:, k, :, :].rearrange("p t (c i) -> p c t i", i=4),
+            )
+
+        def coef_quant(k):
+            nc.vector.quantize_mx(
+                out=cc[:, k, :].bitcast(FP8X4), scales=csc[:, k, :], in_=cgrp[:, k, :, :].rearrange("p n t -> p (n t)")
+            )
+
+        split = 2 * NC
+
+        def ars(g, a):
+            if a == 0:
+                nc.scalar.activation(out=qr[:, 4 * g : 4 * g + 4, :split], in_=en[:, g, :, :split], func=ACT.Abs_reciprocal_sqrt)
+            else:
+                nc.scalar.activation(
+                    out=qr[:, 8 * g : 8 * g + 8, split:],
+                    in_=en[:, 2 * g : 2 * g + 2, :, split:].rearrange("p g t n -> p (g t) n"),
+                    func=ACT.Abs_reciprocal_sqrt,
+                )
+
+        banks = {}
+        groups = {}
+
+        def transposes(j):
+            g, t = divmod(j, 4)
+            bank = ps_x.tile([P, PASSES, 2, P], F32, name="bank", tag="x")
+            words = ph[:, g, t, :].bitcast(F32)
+            for k in range(PASSES):
+                for u in range(2):
+                    nc.tensor.transpose(bank[:, k, u, :], words[:, 256 * k + u : 256 * (k + 1) : 2], ident[:])
+            banks[j] = bank
+
+        def evacuate(j, on_scalar):
+            grp = stage.tile([P, PASSES, P, 4], BF16, name="grp", tag="grp", bufs=6, align_bytes=64)
+            dst = grp[:].rearrange("p k r t -> p (k r t)").bitcast(F32).rearrange("p (k r u) -> p k r u", k=PASSES, u=2)
+            src = banks[j][:].rearrange("p k u r -> p k r u")
+            if on_scalar:
+                nc.scalar.copy(out=dst, in_=src)
+            else:
+                nc.vector.tensor_copy(out=dst, in_=src)
+            groups[j] = grp
+
+        def quant_phi(j):
+            nc.vector.quantize_mx(
+                out=pc[:, j, :, :].rearrange("p k r -> p (k r)").bitcast(FP8X4),
+                scales=psc[:, j, :, :].rearrange("p k r -> p (k r)"),
+                in_=groups[j][:].rearrange("p k r t -> p (k r t)"),
+            )
+
+        gbanks = {}
+
+        def mm1(g, c):
+            bank = ps_x.tile([P, 4, NC], F32, name="gbank", tag="x")
+            cols = slice(c * NC, (c + 1) * NC)
+            for t in range(4):
+                for k in range(PASSES):
+                    nc.tensor.matmul_mx(
+                        out=bank[:, t, :],
+                        lhsT=pc[:, 4 * g + t, k, :].bitcast(FP8X4),
+                        lhsT_scale=psc[:, 4 * g + t, k, :],
+                        rhs=cc[:, k, cols].bitcast(FP8X4),
+                        rhs_scale=csc[:, k, cols],
+                        start=(k == 0),
+                        stop=(k == PASSES - 1),
+                    )
+            gbanks[g, c] = bank
+
+        th = {}
+        hcodes = {}
+        hscales = {}
+        hgrp = {}
+
+        def square(g, c, on_scalar):
+            r = qr[:, 4 * g : 4 * g + 4, c * NC : (c + 1) * NC]
+            if on_scalar:
+                nc.scalar.activation(out=r, in_=r, func=ACT.Square)
+            else:
+                nc.vector.tensor_tensor(out=r, in0=r, in1=r, op=MULT)
+
+        def tanh(g, c):
+            if c not in th:
+                th[c] = stage.tile([P, G * 4, NC], F32, name="th", tag="th", bufs=3, align_bytes=64)
+            nc.scalar.activation(out=th[c][:, 4 * g : 4 * g + 4, :], in_=en[:, g, :, c * NC : (c + 1) * NC], func=ACT.Tanh)
+
+        def weights_mult(g, c, on_gpsimd=False):
+            rows = slice(4 * g, 4 * g + 4)
+            cols = slice(c * NC, (c + 1) * NC)
+            eng = nc.gpsimd if on_gpsimd else nc.vector
+            eng.tensor_tensor(out=th[c][:, rows, :], in0=th[c][:, rows, :], in1=qr[:, rows, cols], op=MULT)
+
+        def make_h(g, c):
+            hg = stage.tile([P, NC, 4], BF16, name="hg", tag="hg", bufs=4, align_bytes=64)
+            nc.vector.tensor_tensor(
+                out=hg[:].rearrange("p (c i) t -> p c t i", i=4),
+                in0=gbanks[g, c][:].rearrange("p t (c i) -> p c t i", i=4),
+                in1=th[c][:, 4 * g : 4 * g + 4, :].rearrange("p t (c i) -> p c t i", i=4),
+                op=MULT,
+            )
+            hgrp[g, c] = hg
+
+        def quant_h(g, c):
+            if c not in hcodes:
+                hcodes[c] = stage.tile([P, G, NC], U32, name="hc", tag="hc", bufs=3, align_bytes=64)
+                hscales[c] = stage.tile([P, G, NC], U8, name="hs", tag="hs", bufs=3, align_bytes=64)
+            nc.vector.quantize_mx(
+                out=hcodes[c][:, g, :].bitcast(FP8X4),
+                scales=hscales[c][:, g, :],
+                in_=hgrp[g, c][:].rearrange("p n t -> p (n t)"),
+            )
+
+        obanks = {}
+
+        def mm2(q, c):
+            bank = ps_x.tile([P, 4, NC], F32, name="obank", tag="x")
+            for i in range(4):
+                tile_i = 4 * q + i
+                for g in range(G):
+                    nc.tensor.matmul_mx(
+                        out=bank[:, i, :],
+                        lhsT=vw[:, g, 256 * tile_i : 256 * (tile_i + 1)].bitcast(FP4X4),
+                        lhsT_scale=vs[:, g, P * tile_i : P * (tile_i + 1)],
+                        rhs=hcodes[c][:, g, :].bitcast(FP8X4),
+                        rhs_scale=hscales[c][:, g, :],
+                        start=(g == 0),
+                        stop=(g == G - 1),
+                    )
+            obanks[q, c] = bank
+
+        def store(q, c, on_scalar):
+            o = stage.tile([P, 4, NC], F32, name="o", tag="o", bufs=4, align_bytes=64)
+            if on_scalar:
+                nc.scalar.copy(out=o[:], in_=obanks[q, c][:])
+            else:
+                nc.vector.tensor_copy(out=o[:], in_=obanks[q, c][:])
+            nc.sync.dma_start(out=out_v[q, c], in_=o[:])
+
+        with tc.manual_schedule():
+            coef_widen(0, True)
+            coef_widen(1, False)
+            ars(0, 0)
+            transposes(0)
+            coef_interleave(0)
+            transposes(1)
+            evacuate(0, True)
+            transposes(2)
+            evacuate(1, True)
+            coef_interleave(1)
+            transposes(3)
+            evacuate(2, True)
+            ars(1, 0)
+            evacuate(3, False)
+            transposes(4)
+            coef_quant(1)
+            square(0, 0, True)
+            transposes(5)
+            quant_phi(2)
+            evacuate(4, True)
+            coef_quant(0)
+            ars(2, 0)
+            quant_phi(1)
+            quant_phi(0)
+            transposes(6)
+            quant_phi(3)
+            evacuate(5, True)
+            quant_phi(4)
+            transposes(7)
+            square(2, 0, False)
+            square(1, 0, True)
+            mm1(0, 1)
+            quant_phi(5)
+            ars(3, 0)
+            evacuate(7, False)
+            mm1(0, 0)
+            evacuate(6, False)
+            transposes(9)
+            square(1, 1, True)
+            quant_phi(7)
+            quant_phi(6)
+            tanh(0, 0)
+            transposes(8)
+            evacuate(9, False)
+            transposes(10)
+            evacuate(8, False)
+            transposes(11)
+            quant_phi(9)
+            transposes(12)
+            quant_phi(8)
+            evacuate(11, False)
+            transposes(13)
+            evacuate(10, True)
+            weights_mult(0, 0, True)
+            evacuate(12, False)
+            transposes(15)
+            square(3, 0, True)
+            evacuate(13, False)
+            transposes(14)
+            tanh(3, 0)
+            mm1(1, 0)
+            quant_phi(12)
+            evacuate(15, True)
+            quant_phi(10)
+            make_h(0, 0)
+            weights_mult(3, 0, True)
+            evacuate(14, True)
+            mm1(1, 1)
+            tanh(1, 0)
+            mm1(1, 2)
+            quant_h(0, 0)
+            tanh(2, 0)
+            mm1(0, 2)
+            quant_phi(15)
+            quant_phi(13)
+            tanh(0, 1)
+            mm1(1, 3)
+            quant_phi(11)
+            quant_phi(14)
+            tanh(1, 1)
+            mm1(2, 0)
+            weights_mult(1, 0, False)
+            tanh(3, 1)
+            weights_mult(2, 0, False)
+            mm1(3, 0)
+            square(2, 1, True)
+            make_h(1, 0)
+            weights_mult(1, 1, True)
+            square(0, 1, True)
+            make_h(2, 0)
+            mm1(3, 1)
+            square(3, 1, True)
+            make_h(3, 0)
+            weights_mult(0, 1, True)
+            mm1(2, 1)
+            tanh(2, 1)
+            make_h(1, 1)
+            mm1(2, 2)
+            ars(0, 1)
+            quant_h(3, 0)
+            quant_h(1, 0)
+            mm1(3, 2)
+            quant_h(2, 0)
+            make_h(0, 1)
+            weights_mult(2, 1, True)
+            mm2(2, 0)
+            quant_h(0, 1)
+            quant_h(1, 1)
+            make_h(2, 1)
+            weights_mult(3, 1, True)
+            store(2, 0, False)
+            mm2(3, 0)
+            quant_h(2, 1)
+            make_h(3, 1)
+            ars(1, 1)
+            square(0, 2, False)
+            mm2(0, 0)
+            square(1, 2, False)
+            quant_h(3, 1)
+            store(3, 0, False)
+            mm2(1, 0)
+            store(0, 0, True)
+            square(3, 2, False)
+            tanh(1, 2)
+            square(2, 2, False)
+            mm2(2, 1)
+            store(1, 0, False)
+            square(2, 3, False)
+            mm2(1, 1)
+            square(1, 3, False)
+            tanh(0, 2)
+            weights_mult(1, 2, False)
+            tanh(3, 2)
+            weights_mult(0, 2, False)
+            mm2(3, 1)
+            tanh(2, 2)
+            make_h(1, 2)
+            weights_mult(3, 2, True)
+            store(1, 1, True)
+            make_h(0, 2)
+            store(2, 1, True)
+            mm2(0, 1)
+            store(3, 1, False)
+            weights_mult(2, 2, True)
+            square(0, 3, True)
+            make_h(3, 2)
+            square(3, 3, True)
+            mm1(0, 3)
+            quant_h(0, 2)
+            store(0, 1, True)
+            quant_h(1, 2)
+            make_h(2, 2)
+            mm1(2, 3)
+            tanh(0, 3)
+            quant_h(3, 2)
+            mm1(3, 3)
+            quant_h(2, 2)
+            tanh(2, 3)
+            weights_mult(0, 3, False)
+            mm2(0, 2)
+            tanh(3, 3)
+            weights_mult(2, 3, False)
+            tanh(1, 3)
+            make_h(0, 3)
+            weights_mult(3, 3, True)
+            mm2(1, 2)
+            make_h(2, 3)
+            store(0, 2, True)
+            quant_h(0, 3)
+            quant_h(2, 3)
+            make_h(3, 3)
+            weights_mult(1, 3, True)
+            mm2(3, 2)
+            store(1, 2, True)
+            quant_h(3, 3)
+            make_h(1, 3)
+            mm2(2, 2)
+            store(3, 2, True)
+            quant_h(1, 3)
+            mm2(0, 3)
+            store(2, 2, True)
+            mm2(1, 3)
+            store(0, 3, True)
+            mm2(3, 3)
+            store(1, 3, True)
+            mm2(2, 3)
+            store(3, 3, True)
+            store(2, 3, True)

@@ -18,413 +18,291 @@ ACT = mybir.ActivationFunctionType
 MULT = mybir.AluOpType.mult
 
 P = 128
+PACK = 4
 G = M // 512
 PASSES = R // 512
 NC = 128
 CH = B // NC
+TILES = M // P
+EARLY = 4
+FIRST_EVAC = 1
 
 
 def tile_bcs_gap_step_s13_kernel(tc, phi, coef_bytes, coef_scale, energy, v_words, v_scales, out):
     nc = tc.nc
     with ExitStack() as ctx:
         keep = ctx.enter_context(tc.tile_pool(name="keep", bufs=1))
-        stage = ctx.enter_context(tc.tile_pool(name="stage", bufs=3))
-        ps_x = ctx.enter_context(tc.psum_pool(name="ps_x", bufs=8))
+        stage = ctx.enter_context(tc.tile_pool(name="stage", bufs=2))
+        psum = ctx.enter_context(tc.psum_pool(name="psum", bufs=2))
+        ctx.enter_context(tc.manual_schedule())
 
-        en = keep.tile([P, G, 4, B], BF16, name="en", align_bytes=64)
-        ph = keep.tile([P, G, 4, R], BF16, name="ph", align_bytes=64)
-        cb = keep.tile([P, PASSES, 4, B], U8, name="cb", align_bytes=64)
-        cs = keep.tile([P, PASSES, 4], F32, name="cs", align_bytes=64)
-        vw = keep.tile([P, G, 2 * M], U8, name="vw", align_bytes=64)
+        en = [keep.tile([P, PACK, B], BF16, name="en%d" % g, align_bytes=64) for g in range(G)]
+        ph = [keep.tile([P, 2, R], BF16, name="ph%d" % j, align_bytes=64) for j in range(2 * G)]
+        cb = [keep.tile([P, PACK * B], U8, name="cb%d" % k, align_bytes=64) for k in range(PASSES)]
+        cs = keep.tile([P, PASSES, PACK], F32, name="cs", align_bytes=64)
+        vw = [keep.tile([P, 2 * M], U8, name="vw%d" % g, align_bytes=64) for g in range(G)]
         vs = keep.tile([P, G, M], U8, name="vs", align_bytes=64)
-
-        phi_v = phi.rearrange("(g p t) k -> g p t k", p=P, t=4)
-        en_v = energy.rearrange("(g p t) n -> g p t n", p=P, t=4)
-        cb_v = coef_bytes.rearrange("(g p t) n -> p g (t n)", p=P, t=4)
-        cs_v = coef_scale.rearrange("(g p t) o -> p g (t o)", p=P, t=4)
-        out_v = out.rearrange("(q i p) (c n) -> q c p i n", i=4, p=P, n=NC)
-
-        def load_en(g):
-            nc.sync.dma_start(out=en[:, g, :, :], in_=en_v[g])
-
-        def load_phi(g, t0, t1):
-            nc.sync.dma_start(out=ph[:, g, t0:t1, :], in_=phi_v[g][:, t0:t1, :])
-
-        def load_cb(k):
-            nc.sync.dma_start(out=cb[:, k, :, :].rearrange("p t n -> p (t n)"), in_=cb_v[:, k, :])
-
-        warm = keep.tile([P, 1], F32, name="warm")
-        nc.vector.memset(warm[:], 1.0)
-        nc.scalar.activation(out=warm[:], in_=warm[:], func=ACT.Abs_reciprocal_sqrt)
         ident = keep.tile([P, P], F32, name="ident", align_bytes=64)
+
+        phi_v = phi.rearrange("(g p t) k -> g p t k", p=P, t=PACK)
+        en_v = energy.rearrange("(g p t) n -> g p t n", p=P, t=PACK)
+        cb_v = coef_bytes.rearrange("(g p t) n -> g p (t n)", p=P, t=PACK)
+        cs_v = coef_scale.rearrange("(g p t) o -> p g (t o)", p=P, t=PACK)
+        out_v = out.rearrange("(i p) n -> i p n", p=P)
+
+        def load_en(g, t0, t1):
+            nc.sync.dma_start(out=en[g][:, t0:t1, :], in_=en_v[g][:, t0:t1, :])
+
+        def load_phi(j):
+            g, half = divmod(j, 2)
+            nc.sync.dma_start(out=ph[j][:], in_=phi_v[g][:, 2 * half : 2 * half + 2, :])
+
+        def load_v(g):
+            nc.sync.dma_start(out=vw[g][:], in_=v_words[g])
+
         make_identity(nc, ident[:])
-        nc.gpsimd.memset(vs[:].rearrange("p g n -> p (g n)").bitcast(U32), 0)
+        nc.vector.memset(vs[:].rearrange("p g n -> p (g n)").bitcast(I32), 0)
 
         nc.sync.dma_start(out=cs[:], in_=cs_v)
-        load_cb(0)
-        load_en(0)
-        load_cb(1)
-        load_phi(0, 0, 2)
-        load_phi(0, 2, 4)
-        load_en(1)
-        load_phi(1, 0, 2)
-        load_en(2)
-        load_phi(1, 2, 4)
-        load_en(3)
-        load_phi(2, 0, 2)
-        load_phi(2, 2, 4)
-        load_phi(3, 0, 2)
-        load_phi(3, 2, 4)
+        nc.sync.dma_start(out=cb[0][:], in_=cb_v[0])
+        load_en(0, 0, 2)
+        nc.sync.dma_start(out=cb[1][:], in_=cb_v[1])
+        load_en(0, 2, 4)
+        load_en(1, 0, 4)
+        load_phi(0)
+        load_en(2, 0, 4)
+        load_phi(1)
+        load_en(3, 0, 4)
+        for j in range(2, 7):
+            load_phi(j)
         for quad in range(4):
             nc.sync.dma_start(
                 out=vs[32 * quad : 32 * quad + 4, :, :].bitcast(I32),
                 in_=v_scales[:, 4 * quad : 4 * quad + 4, :].rearrange("g r n -> r g n").bitcast(I32),
             )
+        load_phi(7)
         for g in range(G):
-            nc.sync.dma_start(out=vw[:, g, :], in_=v_words[g])
+            load_v(g)
 
         cc = keep.tile([P, PASSES, B], U32, name="cc", align_bytes=64)
         csc = keep.tile([P, PASSES, B], U8, name="csc", align_bytes=64)
-        wide = keep.tile([P, PASSES, 4, B], BF16, name="wide", align_bytes=64)
-        cgrp = keep.tile([P, PASSES, B, 4], BF16, name="cgrp", align_bytes=64)
-        qr = keep.tile([P, G * 4, B], F32, name="qr", align_bytes=64)
-        pc = keep.tile([P, G * 4, PASSES, P], U32, name="pc", align_bytes=64)
-        psc = keep.tile([P, G * 4, PASSES, P], U8, name="psc", align_bytes=64)
+        wide = [keep.tile([P, PACK, B], BF16, name="wide%d" % k, align_bytes=64) for k in range(PASSES)]
+        cgrp = [keep.tile([P, B, PACK], BF16, name="cgrp%d" % k, align_bytes=64) for k in range(PASSES)]
+        weight = [keep.tile([P, PACK, B], F32, name="weight%d" % g, align_bytes=64) for g in range(G)]
+        pc = [keep.tile([P, PACK, PASSES, P], U32, name="pc%d" % g, align_bytes=64) for g in range(G)]
+        psc = [keep.tile([P, PACK, PASSES, P], U8, name="psc%d" % g, align_bytes=64) for g in range(G)]
+        hc = [keep.tile([P, B], U32, name="hc%d" % g, align_bytes=64) for g in range(G)]
+        hs = [keep.tile([P, B], U8, name="hs%d" % g, align_bytes=64) for g in range(G)]
 
-        def coef_widen(k, on_scalar):
-            for t in range(4):
-                if on_scalar:
-                    nc.scalar.activation(out=wide[:, k, t, :], in_=cb[:, k, t, :].bitcast(FP8), func=ACT.Copy, scale=cs[:, k, t : t + 1])
-                else:
-                    nc.vector.tensor_scalar(
-                        out=wide[:, k, t, :], in0=cb[:, k, t, :].bitcast(FP8), scalar1=cs[:, k, t : t + 1], scalar2=None, op0=MULT
-                    )
+        def coef_widen(k):
+            for t in range(PACK):
+                nc.vector.tensor_scalar(
+                    out=wide[k][:, t, :],
+                    in0=cb[k][:, t * B : (t + 1) * B].bitcast(FP8),
+                    scalar1=cs[:, k, t : t + 1],
+                    scalar2=None,
+                    op0=MULT,
+                )
 
         def coef_interleave(k):
             nc.vector.tensor_copy(
-                out=cgrp[:, k, :, :].rearrange("p (c i) t -> p c t i", i=4),
-                in_=wide[:, k, :, :].rearrange("p t (c i) -> p c t i", i=4),
+                out=cgrp[k][:].rearrange("p (c i) t -> p c t i", i=4),
+                in_=wide[k][:].rearrange("p t (c i) -> p c t i", i=4),
             )
 
         def coef_quant(k):
-            nc.vector.quantize_mx(
-                out=cc[:, k, :].bitcast(FP8X4), scales=csc[:, k, :], in_=cgrp[:, k, :, :].rearrange("p n t -> p (n t)")
-            )
+            nc.vector.quantize_mx(out=cc[:, k, :].bitcast(FP8X4), scales=csc[:, k, :], in_=cgrp[k][:].rearrange("p n t -> p (n t)"))
 
-        split = 2 * NC
+        def tanh(g, t0, t1):
+            nc.scalar.activation(out=weight[g][:, t0:t1, :], in_=en[g][:, t0:t1, :], func=ACT.Tanh)
 
-        def ars(g, a):
-            if a == 0:
-                nc.scalar.activation(out=qr[:, 4 * g : 4 * g + 4, :split], in_=en[:, g, :, :split], func=ACT.Abs_reciprocal_sqrt)
-            else:
-                nc.scalar.activation(
-                    out=qr[:, 8 * g : 8 * g + 8, split:],
-                    in_=en[:, 2 * g : 2 * g + 2, :, split:].rearrange("p g t n -> p (g t) n"),
-                    func=ACT.Abs_reciprocal_sqrt,
-                )
+        inv = {}
 
-        banks = {}
-        groups = {}
+        def inv_sqrt(u):
+            g, c = divmod(u, CH)
+            inv[u] = stage.tile([P, PACK, NC], F32, name="inv", tag="inv", bufs=6, align_bytes=64)
+            nc.scalar.activation(out=inv[u][:], in_=en[g][:, :, c * NC : (c + 1) * NC], func=ACT.Abs_reciprocal_sqrt)
+
+        def square(u):
+            nc.scalar.activation(out=inv[u][:], in_=inv[u][:], func=ACT.Square)
+
+        turned = {}
+        grouped = {}
 
         def transposes(j):
-            g, t = divmod(j, 4)
-            bank = ps_x.tile([P, PASSES, 2, P], F32, name="bank", tag="x")
-            words = ph[:, g, t, :].bitcast(F32)
+            bank = psum.tile([P, PASSES, 2, P], F32, name="tbank", tag="bank%d" % (2 + j % 6), bufs=1)
+            words = ph[j // 2][:, j % 2, :].bitcast(F32)
             for k in range(PASSES):
                 for u in range(2):
                     nc.tensor.transpose(bank[:, k, u, :], words[:, 256 * k + u : 256 * (k + 1) : 2], ident[:])
-            banks[j] = bank
+            turned[j] = bank
 
         def evacuate(j, on_scalar):
-            grp = stage.tile([P, PASSES, P, 4], BF16, name="grp", tag="grp", bufs=6, align_bytes=64)
-            dst = grp[:].rearrange("p k r t -> p (k r t)").bitcast(F32).rearrange("p (k r u) -> p k r u", k=PASSES, u=2)
-            src = banks[j][:].rearrange("p k u r -> p k r u")
+            g, t = divmod(j, PACK)
+            if t == 0:
+                grouped[g] = stage.tile([P, PACK, PASSES * P * PACK], BF16, name="grp", tag="grp", bufs=2, align_bytes=64)
+            dst = grouped[g][:, t, :].bitcast(F32).rearrange("p (k r u) -> p k r u", k=PASSES, u=2)
+            src = turned[j][:].rearrange("p k u r -> p k r u")
             if on_scalar:
                 nc.scalar.copy(out=dst, in_=src)
             else:
                 nc.vector.tensor_copy(out=dst, in_=src)
-            groups[j] = grp
 
-        def quant_phi(j):
+        def quant_phi(g):
             nc.vector.quantize_mx(
-                out=pc[:, j, :, :].rearrange("p k r -> p (k r)").bitcast(FP8X4),
-                scales=psc[:, j, :, :].rearrange("p k r -> p (k r)"),
-                in_=groups[j][:].rearrange("p k r t -> p (k r t)"),
+                out=pc[g][:].rearrange("p t k r -> p (t k r)").bitcast(FP8X4),
+                scales=psc[g][:].rearrange("p t k r -> p (t k r)"),
+                in_=grouped[g][:].rearrange("p t x -> p (t x)"),
             )
 
-        gbanks = {}
+        gaps = {}
 
-        def mm1(g, c):
-            bank = ps_x.tile([P, 4, NC], F32, name="gbank", tag="x")
+        def mm1(u):
+            g, c = divmod(u, CH)
+            bank = psum.tile([P, PACK, NC], F32, name="gbank", tag="bank%d" % (u % 2), bufs=1)
             cols = slice(c * NC, (c + 1) * NC)
-            for t in range(4):
+            for t in range(PACK):
                 for k in range(PASSES):
                     nc.tensor.matmul_mx(
                         out=bank[:, t, :],
-                        lhsT=pc[:, 4 * g + t, k, :].bitcast(FP8X4),
-                        lhsT_scale=psc[:, 4 * g + t, k, :],
+                        lhsT=pc[g][:, t, k, :].bitcast(FP8X4),
+                        lhsT_scale=psc[g][:, t, k, :],
                         rhs=cc[:, k, cols].bitcast(FP8X4),
                         rhs_scale=csc[:, k, cols],
                         start=(k == 0),
                         stop=(k == PASSES - 1),
                     )
-            gbanks[g, c] = bank
+            gaps[u] = bank
 
-        th = {}
-        hcodes = {}
-        hscales = {}
         hgrp = {}
 
-        def square(g, c, on_scalar):
-            r = qr[:, 4 * g : 4 * g + 4, c * NC : (c + 1) * NC]
-            if on_scalar:
-                nc.scalar.activation(out=r, in_=r, func=ACT.Square)
-            else:
-                nc.vector.tensor_tensor(out=r, in0=r, in1=r, op=MULT)
-
-        def tanh(g, c):
-            if c not in th:
-                th[c] = stage.tile([P, G * 4, NC], F32, name="th", tag="th", bufs=3, align_bytes=64)
-            nc.scalar.activation(out=th[c][:, 4 * g : 4 * g + 4, :], in_=en[:, g, :, c * NC : (c + 1) * NC], func=ACT.Tanh)
-
-        def weights_mult(g, c, on_gpsimd=False):
-            rows = slice(4 * g, 4 * g + 4)
+        def divide(u):
+            g, c = divmod(u, CH)
             cols = slice(c * NC, (c + 1) * NC)
-            eng = nc.gpsimd if on_gpsimd else nc.vector
-            eng.tensor_tensor(out=th[c][:, rows, :], in0=th[c][:, rows, :], in1=qr[:, rows, cols], op=MULT)
+            nc.vector.tensor_tensor(out=weight[g][:, :, cols], in0=weight[g][:, :, cols], in1=inv[u][:], op=MULT)
 
-        def make_h(g, c):
-            hg = stage.tile([P, NC, 4], BF16, name="hg", tag="hg", bufs=4, align_bytes=64)
+        def make_h(u):
+            g, c = divmod(u, CH)
+            if c == 0:
+                hgrp[g] = stage.tile([P, B, PACK], BF16, name="hg", tag="hg", bufs=2, align_bytes=64)
+            cols = slice(c * NC, (c + 1) * NC)
             nc.vector.tensor_tensor(
-                out=hg[:].rearrange("p (c i) t -> p c t i", i=4),
-                in0=gbanks[g, c][:].rearrange("p t (c i) -> p c t i", i=4),
-                in1=th[c][:, 4 * g : 4 * g + 4, :].rearrange("p t (c i) -> p c t i", i=4),
+                out=hgrp[g][:, cols, :].rearrange("p (c i) t -> p c t i", i=2),
+                in0=gaps[u][:].rearrange("p t (c i) -> p c t i", i=2),
+                in1=weight[g][:, :, cols].rearrange("p t (c i) -> p c t i", i=2),
                 op=MULT,
             )
-            hgrp[g, c] = hg
 
-        def quant_h(g, c):
-            if c not in hcodes:
-                hcodes[c] = stage.tile([P, G, NC], U32, name="hc", tag="hc", bufs=3, align_bytes=64)
-                hscales[c] = stage.tile([P, G, NC], U8, name="hs", tag="hs", bufs=3, align_bytes=64)
+        def quant_h(g, c0, c1):
+            cols = slice(c0 * NC, c1 * NC)
             nc.vector.quantize_mx(
-                out=hcodes[c][:, g, :].bitcast(FP8X4),
-                scales=hscales[c][:, g, :],
-                in_=hgrp[g, c][:].rearrange("p n t -> p (n t)"),
+                out=hc[g][:, cols].bitcast(FP8X4),
+                scales=hs[g][:, cols],
+                in_=hgrp[g][:, cols, :].rearrange("p n t -> p (n t)"),
             )
 
-        obanks = {}
+        sums = {}
 
-        def mm2(q, c):
-            bank = ps_x.tile([P, 4, NC], F32, name="obank", tag="x")
-            for i in range(4):
-                tile_i = 4 * q + i
-                for g in range(G):
-                    nc.tensor.matmul_mx(
-                        out=bank[:, i, :],
-                        lhsT=vw[:, g, 256 * tile_i : 256 * (tile_i + 1)].bitcast(FP4X4),
-                        lhsT_scale=vs[:, g, P * tile_i : P * (tile_i + 1)],
-                        rhs=hcodes[c][:, g, :].bitcast(FP8X4),
-                        rhs_scale=hscales[c][:, g, :],
-                        start=(g == 0),
-                        stop=(g == G - 1),
-                    )
-            obanks[q, c] = bank
+        def mm2(i, g):
+            if g == 0:
+                slot = i % 8
+                slot = 2 + (slot + 4) % 6 if slot < 6 else slot - 6
+                sums[i] = psum.tile([P, B], F32, name="obank", tag="bank%d" % slot, bufs=1)
+            nc.tensor.matmul_mx(
+                out=sums[i][:],
+                lhsT=vw[g][:, 2 * P * i : 2 * P * (i + 1)].bitcast(FP4X4),
+                lhsT_scale=vs[:, g, P * i : P * (i + 1)],
+                rhs=hc[g][:].bitcast(FP8X4),
+                rhs_scale=hs[g][:],
+                start=(g == 0),
+                stop=(g == G - 1),
+            )
 
-        def store(q, c, on_scalar):
-            o = stage.tile([P, 4, NC], F32, name="o", tag="o", bufs=4, align_bytes=64)
-            if on_scalar:
-                nc.scalar.copy(out=o[:], in_=obanks[q, c][:])
+        def store(i):
+            o = stage.tile([P, B], F32, name="o", tag="o", bufs=12, align_bytes=64)
+            if i % 2 == 0:
+                nc.scalar.copy(out=o[:], in_=sums[i][:])
             else:
-                nc.vector.tensor_copy(out=o[:], in_=obanks[q, c][:])
-            nc.sync.dma_start(out=out_v[q, c], in_=o[:])
+                nc.vector.tensor_copy(out=o[:], in_=sums[i][:])
+            nc.sync.dma_start(out=out_v[i], in_=o[:])
 
-        with tc.manual_schedule():
-            coef_widen(0, True)
-            coef_widen(1, False)
-            ars(0, 0)
-            transposes(0)
-            coef_interleave(0)
-            transposes(1)
-            evacuate(0, True)
-            transposes(2)
-            evacuate(1, True)
-            coef_interleave(1)
-            transposes(3)
-            evacuate(2, True)
-            ars(1, 0)
-            evacuate(3, False)
-            transposes(4)
-            coef_quant(1)
-            square(0, 0, True)
-            transposes(5)
-            quant_phi(2)
-            evacuate(4, True)
-            coef_quant(0)
-            ars(2, 0)
-            quant_phi(1)
-            quant_phi(0)
-            transposes(6)
-            quant_phi(3)
-            evacuate(5, True)
-            quant_phi(4)
-            transposes(7)
-            square(2, 0, False)
-            square(1, 0, True)
-            mm1(0, 1)
-            quant_phi(5)
-            ars(3, 0)
-            evacuate(7, False)
-            mm1(0, 0)
-            evacuate(6, False)
-            transposes(9)
-            square(1, 1, True)
-            quant_phi(7)
-            quant_phi(6)
-            tanh(0, 0)
-            transposes(8)
-            evacuate(9, False)
-            transposes(10)
-            evacuate(8, False)
-            transposes(11)
-            quant_phi(9)
-            transposes(12)
-            quant_phi(8)
-            evacuate(11, False)
-            transposes(13)
-            evacuate(10, True)
-            weights_mult(0, 0, True)
-            evacuate(12, False)
-            transposes(15)
-            square(3, 0, True)
-            evacuate(13, False)
-            transposes(14)
-            tanh(3, 0)
-            mm1(1, 0)
-            quant_phi(12)
-            evacuate(15, True)
-            quant_phi(10)
-            make_h(0, 0)
-            weights_mult(3, 0, True)
-            evacuate(14, True)
-            mm1(1, 1)
-            tanh(1, 0)
-            mm1(1, 2)
-            quant_h(0, 0)
-            tanh(2, 0)
-            mm1(0, 2)
-            quant_phi(15)
-            quant_phi(13)
-            tanh(0, 1)
-            mm1(1, 3)
-            quant_phi(11)
-            quant_phi(14)
-            tanh(1, 1)
-            mm1(2, 0)
-            weights_mult(1, 0, False)
-            tanh(3, 1)
-            weights_mult(2, 0, False)
-            mm1(3, 0)
-            square(2, 1, True)
-            make_h(1, 0)
-            weights_mult(1, 1, True)
-            square(0, 1, True)
-            make_h(2, 0)
-            mm1(3, 1)
-            square(3, 1, True)
-            make_h(3, 0)
-            weights_mult(0, 1, True)
-            mm1(2, 1)
-            tanh(2, 1)
-            make_h(1, 1)
-            mm1(2, 2)
-            ars(0, 1)
-            quant_h(3, 0)
-            quant_h(1, 0)
-            mm1(3, 2)
-            quant_h(2, 0)
-            make_h(0, 1)
-            weights_mult(2, 1, True)
-            mm2(2, 0)
-            quant_h(0, 1)
-            quant_h(1, 1)
-            make_h(2, 1)
-            weights_mult(3, 1, True)
-            store(2, 0, False)
-            mm2(3, 0)
-            quant_h(2, 1)
-            make_h(3, 1)
-            ars(1, 1)
-            square(0, 2, False)
-            mm2(0, 0)
-            square(1, 2, False)
-            quant_h(3, 1)
-            store(3, 0, False)
-            mm2(1, 0)
-            store(0, 0, True)
-            square(3, 2, False)
-            tanh(1, 2)
-            square(2, 2, False)
-            mm2(2, 1)
-            store(1, 0, False)
-            square(2, 3, False)
-            mm2(1, 1)
-            square(1, 3, False)
-            tanh(0, 2)
-            weights_mult(1, 2, False)
-            tanh(3, 2)
-            weights_mult(0, 2, False)
-            mm2(3, 1)
-            tanh(2, 2)
-            make_h(1, 2)
-            weights_mult(3, 2, True)
-            store(1, 1, True)
-            make_h(0, 2)
-            store(2, 1, True)
-            mm2(0, 1)
-            store(3, 1, False)
-            weights_mult(2, 2, True)
-            square(0, 3, True)
-            make_h(3, 2)
-            square(3, 3, True)
-            mm1(0, 3)
-            quant_h(0, 2)
-            store(0, 1, True)
-            quant_h(1, 2)
-            make_h(2, 2)
-            mm1(2, 3)
-            tanh(0, 3)
-            quant_h(3, 2)
-            mm1(3, 3)
-            quant_h(2, 2)
-            tanh(2, 3)
-            weights_mult(0, 3, False)
-            mm2(0, 2)
-            tanh(3, 3)
-            weights_mult(2, 3, False)
-            tanh(1, 3)
-            make_h(0, 3)
-            weights_mult(3, 3, True)
-            mm2(1, 2)
-            make_h(2, 3)
-            store(0, 2, True)
-            quant_h(0, 3)
-            quant_h(2, 3)
-            make_h(3, 3)
-            weights_mult(1, 3, True)
-            mm2(3, 2)
-            store(1, 2, True)
-            quant_h(3, 3)
-            make_h(1, 3)
-            mm2(2, 2)
-            store(3, 2, True)
-            quant_h(1, 3)
-            mm2(0, 3)
-            store(2, 2, True)
-            mm2(1, 3)
-            store(0, 3, True)
-            mm2(3, 3)
-            store(1, 3, True)
-            mm2(2, 3)
-            store(3, 3, True)
-            store(2, 3, True)
+        tanh(0, 0, 2)
+        tanh(0, 2, 4)
+        for g in range(1, G):
+            tanh(g, 0, 4)
+        for k in range(PASSES):
+            coef_widen(k)
+        for k in range(PASSES):
+            coef_interleave(k)
+        for j in range(6):
+            transposes(j)
+        coef_quant(0)
+        for j in range(PACK):
+            evacuate(j, False)
+        coef_quant(1)
+        quant_phi(0)
+        transposes(6)
+        transposes(7)
+        mm1(0)
+        mm1(1)
+        transposes(8)
+        transposes(9)
+        for j in range(PACK, 2 * PACK):
+            evacuate(j, False)
+            transposes(j + 6)
+        inv_sqrt(0)
+        inv_sqrt(1)
+        square(0)
+        inv_sqrt(2)
+        square(1)
+        quant_phi(1)
+        divide(0)
+
+        units = G * CH
+        done = [0] * 6
+        for u in range(units):
+            g, c = divmod(u, CH)
+            if u + 3 < units:
+                inv_sqrt(u + 3)
+            if u + 2 < units:
+                square(u + 2)
+            if FIRST_EVAC <= u < FIRST_EVAC + 2 * PACK:
+                evacuate(2 * PACK + u - FIRST_EVAC, u >= FIRST_EVAC + 2)
+            if u + 1 < units:
+                divide(u + 1)
+            if c == 0 and g > 0:
+                quant_h(g - 1, 0, CH)
+            if u == units - 2:
+                quant_h(g, 0, 2)
+            make_h(u)
+            if u == FIRST_EVAC + PACK:
+                quant_phi(2)
+            if u == FIRST_EVAC + 2 * PACK:
+                quant_phi(3)
+            if u + 2 < units:
+                mm1(u + 2)
+            if u == FIRST_EVAC + 2:
+                transposes(14)
+                transposes(15)
+            left = 2 if u < units - CH else 3
+            for i in range(6):
+                while left and done[i] < g and u >= FIRST_EVAC + 3 + i:
+                    mm2(i, done[i])
+                    done[i] = done[i] + 1
+                    left = left - 1
+            if u >= units - 2:
+                for gg in range(G - 1):
+                    mm2(6 + u - (units - 2), gg)
+        quant_h(G - 1, 2, 3)
+        quant_h(G - 1, 3, 4)
+
+        for i in range(6):
+            for g in range(done[i], G - 1):
+                mm2(i, g)
+        for i in range(8):
+            mm2(i, G - 1)
+            store(i)
+        for i in range(8, TILES):
+            for g in range(G):
+                mm2(i, g)
+            store(i)

@@ -24,12 +24,23 @@ PASSES = R // 512
 NC = 128
 CH = B // NC
 TILES = M // P
-EARLY = 4
-FIRST_EVAC = 1
+QUAD = 4
+UNITS = G * CH
+IL = 4
+ORDER = [(0, 0), (1, 0), (0, 1), (2, 0), (1, 1), (3, 0), (2, 1), (3, 1)] + [(g, c) for c in (2, 3) for g in range(G)]
+EV_V = (8, 12)
+QUANT_AT = {2: 1, 3: 3}
+ST_V = ()
+JOBS = 4
+AHEAD = (4, 5)
+QH_FIRST = False
+SPLIT = 12
+SERIAL = 12
 
 
 def tile_bcs_gap_step_s13_kernel(tc, phi, coef_bytes, coef_scale, energy, v_words, v_scales, out):
     nc = tc.nc
+    order = ORDER
     with ExitStack() as ctx:
         keep = ctx.enter_context(tc.tile_pool(name="keep", bufs=1))
         stage = ctx.enter_context(tc.tile_pool(name="stage", bufs=2))
@@ -48,7 +59,7 @@ def tile_bcs_gap_step_s13_kernel(tc, phi, coef_bytes, coef_scale, energy, v_word
         en_v = energy.rearrange("(g p t) n -> g p t n", p=P, t=PACK)
         cb_v = coef_bytes.rearrange("(g p t) n -> g p (t n)", p=P, t=PACK)
         cs_v = coef_scale.rearrange("(g p t) o -> p g (t o)", p=P, t=PACK)
-        out_v = out.rearrange("(i p) n -> i p n", p=P)
+        out_v = out.rearrange("(i p) (c n) -> c p i n", p=P, n=NC)
 
         def load_en(g, t0, t1):
             nc.sync.dma_start(out=en[g][:, t0:t1, :], in_=en_v[g][:, t0:t1, :])
@@ -73,14 +84,13 @@ def tile_bcs_gap_step_s13_kernel(tc, phi, coef_bytes, coef_scale, energy, v_word
         load_en(2, 0, 4)
         load_phi(1)
         load_en(3, 0, 4)
-        for j in range(2, 7):
+        for j in range(2, 2 * G):
             load_phi(j)
         for quad in range(4):
             nc.sync.dma_start(
                 out=vs[32 * quad : 32 * quad + 4, :, :].bitcast(I32),
                 in_=v_scales[:, 4 * quad : 4 * quad + 4, :].rearrange("g r n -> r g n").bitcast(I32),
             )
-        load_phi(7)
         for g in range(G):
             load_v(g)
 
@@ -119,7 +129,7 @@ def tile_bcs_gap_step_s13_kernel(tc, phi, coef_bytes, coef_scale, energy, v_word
         inv = {}
 
         def inv_sqrt(u):
-            g, c = divmod(u, CH)
+            g, c = order[u]
             inv[u] = stage.tile([P, PACK, NC], F32, name="inv", tag="inv", bufs=6, align_bytes=64)
             nc.scalar.activation(out=inv[u][:], in_=en[g][:, :, c * NC : (c + 1) * NC], func=ACT.Abs_reciprocal_sqrt)
 
@@ -130,7 +140,7 @@ def tile_bcs_gap_step_s13_kernel(tc, phi, coef_bytes, coef_scale, energy, v_word
         grouped = {}
 
         def transposes(j):
-            bank = psum.tile([P, PASSES, 2, P], F32, name="tbank", tag="bank%d" % (2 + j % 6), bufs=1)
+            bank = psum.tile([P, PASSES, 2, P], F32, name="tbank", tag="bank%d" % (2 + (j + 4) % 6), bufs=1)
             words = ph[j // 2][:, j % 2, :].bitcast(F32)
             for k in range(PASSES):
                 for u in range(2):
@@ -158,7 +168,7 @@ def tile_bcs_gap_step_s13_kernel(tc, phi, coef_bytes, coef_scale, energy, v_word
         gaps = {}
 
         def mm1(u):
-            g, c = divmod(u, CH)
+            g, c = order[u]
             bank = psum.tile([P, PACK, NC], F32, name="gbank", tag="bank%d" % (u % 2), bufs=1)
             cols = slice(c * NC, (c + 1) * NC)
             for t in range(PACK):
@@ -177,54 +187,59 @@ def tile_bcs_gap_step_s13_kernel(tc, phi, coef_bytes, coef_scale, energy, v_word
         hgrp = {}
 
         def divide(u):
-            g, c = divmod(u, CH)
+            g, c = order[u]
             cols = slice(c * NC, (c + 1) * NC)
             nc.vector.tensor_tensor(out=weight[g][:, :, cols], in0=weight[g][:, :, cols], in1=inv[u][:], op=MULT)
 
         def make_h(u):
-            g, c = divmod(u, CH)
-            if c == 0:
-                hgrp[g] = stage.tile([P, B, PACK], BF16, name="hg", tag="hg", bufs=2, align_bytes=64)
+            g, c = order[u]
+            hgrp[u] = stage.tile([P, NC, PACK], BF16, name="hg", tag="hg", bufs=3, align_bytes=64)
             cols = slice(c * NC, (c + 1) * NC)
             nc.vector.tensor_tensor(
-                out=hgrp[g][:, cols, :].rearrange("p (c i) t -> p c t i", i=2),
-                in0=gaps[u][:].rearrange("p t (c i) -> p c t i", i=2),
-                in1=weight[g][:, :, cols].rearrange("p t (c i) -> p c t i", i=2),
+                out=hgrp[u][:].rearrange("p (c i) t -> p c t i", i=IL),
+                in0=gaps[u][:].rearrange("p t (c i) -> p c t i", i=IL),
+                in1=weight[g][:, :, cols].rearrange("p t (c i) -> p c t i", i=IL),
                 op=MULT,
             )
 
-        def quant_h(g, c0, c1):
-            cols = slice(c0 * NC, c1 * NC)
+        def quant_h(u):
+            g, c = order[u]
+            cols = slice(c * NC, (c + 1) * NC)
             nc.vector.quantize_mx(
                 out=hc[g][:, cols].bitcast(FP8X4),
                 scales=hs[g][:, cols],
-                in_=hgrp[g][:, cols, :].rearrange("p n t -> p (n t)"),
+                in_=hgrp[u][:].rearrange("p n t -> p (n t)"),
             )
 
+        parts = [(c, i0, QUAD) for c in range(CH) for i0 in range(0, TILES, QUAD)]
+        parts = parts[:-1] + [(CH - 1, TILES - QUAD, 2), (CH - 1, TILES - 2, 2)]
         sums = {}
 
-        def mm2(i, g):
+        def mm2(n, g):
+            c, i0, count = parts[n]
             if g == 0:
-                slot = i % 8
-                slot = 2 + (slot + 4) % 6 if slot < 6 else slot - 6
-                sums[i] = psum.tile([P, B], F32, name="obank", tag="bank%d" % slot, bufs=1)
-            nc.tensor.matmul_mx(
-                out=sums[i][:],
-                lhsT=vw[g][:, 2 * P * i : 2 * P * (i + 1)].bitcast(FP4X4),
-                lhsT_scale=vs[:, g, P * i : P * (i + 1)],
-                rhs=hc[g][:].bitcast(FP8X4),
-                rhs_scale=hs[g][:],
-                start=(g == 0),
-                stop=(g == G - 1),
-            )
+                sums[n] = psum.tile([P, count, NC], F32, name="obank", tag="bank%d" % (2 + (2 + n) % 6), bufs=1)
+            cols = slice(c * NC, (c + 1) * NC)
+            for k in range(count):
+                i = i0 + k
+                nc.tensor.matmul_mx(
+                    out=sums[n][:, k, :],
+                    lhsT=vw[g][:, 2 * P * i : 2 * P * (i + 1)].bitcast(FP4X4),
+                    lhsT_scale=vs[:, g, P * i : P * (i + 1)],
+                    rhs=hc[g][:, cols].bitcast(FP8X4),
+                    rhs_scale=hs[g][:, cols],
+                    start=(g == 0 and k == 0),
+                    stop=(g == G - 1 and k == count - 1),
+                )
 
-        def store(i):
-            o = stage.tile([P, B], F32, name="o", tag="o", bufs=12, align_bytes=64)
-            if i % 2 == 0:
-                nc.scalar.copy(out=o[:], in_=sums[i][:])
+        def store(n, on_scalar):
+            c, i0, count = parts[n]
+            o = stage.tile([P, count, NC], F32, name="o", tag="o", bufs=6, align_bytes=64)
+            if on_scalar:
+                nc.scalar.copy(out=o[:], in_=sums[n][:])
             else:
-                nc.vector.tensor_copy(out=o[:], in_=sums[i][:])
-            nc.sync.dma_start(out=out_v[i], in_=o[:])
+                nc.vector.tensor_copy(out=o[:], in_=sums[n][:])
+            nc.sync.dma_start(out=out_v[c][:, i0 : i0 + count, :], in_=o[:])
 
         tanh(0, 0, 2)
         tanh(0, 2, 4)
@@ -243,66 +258,73 @@ def tile_bcs_gap_step_s13_kernel(tc, phi, coef_bytes, coef_scale, energy, v_word
         quant_phi(0)
         transposes(6)
         transposes(7)
-        mm1(0)
-        mm1(1)
         transposes(8)
         transposes(9)
         for j in range(PACK, 2 * PACK):
             evacuate(j, False)
-            transposes(j + 6)
+            if j + 6 < SPLIT:
+                transposes(j + 6)
         inv_sqrt(0)
         inv_sqrt(1)
         square(0)
         inv_sqrt(2)
         square(1)
         quant_phi(1)
+        mm1(0)
+        mm1(1)
+        for j in range(SPLIT, 2 * PACK + 6):
+            transposes(j)
         divide(0)
 
-        units = G * CH
-        done = [0] * 6
-        for u in range(units):
-            g, c = divmod(u, CH)
-            if u + 3 < units:
-                inv_sqrt(u + 3)
-            if u + 2 < units:
-                square(u + 2)
-            if FIRST_EVAC <= u < FIRST_EVAC + 2 * PACK:
-                evacuate(2 * PACK + u - FIRST_EVAC, u >= FIRST_EVAC + 2)
-            if u + 1 < units:
+        todo = [(n, g) for n in range(len(parts)) for g in range(G)]
+        full = []
+        stored = []
+        emptied = 2 * PACK
+        roots = 3
+        for u in range(UNITS + 1):
+            pair = range(emptied, min(emptied + 2, TILES))
+            for j in pair:
+                evacuate(j, j not in EV_V)
+                emptied = j + 1
+            for j in pair:
+                if j + 6 < TILES:
+                    transposes(j + 6)
+            for n in range(2 if u in AHEAD else 1):
+                if roots < UNITS:
+                    inv_sqrt(roots)
+                if roots - 1 < UNITS:
+                    square(roots - 1)
+                roots = roots + 1
+            if u > 0 and QH_FIRST:
+                quant_h(u - 1)
+            if u + 1 < UNITS:
                 divide(u + 1)
-            if c == 0 and g > 0:
-                quant_h(g - 1, 0, CH)
-            if u == units - 2:
-                quant_h(g, 0, 2)
-            make_h(u)
-            if u == FIRST_EVAC + PACK:
-                quant_phi(2)
-            if u == FIRST_EVAC + 2 * PACK:
-                quant_phi(3)
-            if u + 2 < units:
+            if u > 0 and not QH_FIRST:
+                quant_h(u - 1)
+            if u < UNITS:
+                make_h(u)
+            for g in range(2, G):
+                if u == QUANT_AT[g]:
+                    quant_phi(g)
+            if u + 2 < UNITS:
                 mm1(u + 2)
-            if u == FIRST_EVAC + 2:
-                transposes(14)
-                transposes(15)
-            left = 2 if u < units - CH else 3
-            for i in range(6):
-                while left and done[i] < g and u >= FIRST_EVAC + 3 + i:
-                    mm2(i, done[i])
-                    done[i] = done[i] + 1
+            for n in full:
+                store(n, n not in ST_V)
+                stored.append(n)
+            full = []
+            left = JOBS if u < UNITS else len(todo)
+            for n, g in list(todo):
+                c = parts[n][0]
+                free = emptied > TILES - 6 + n if n < 6 else n - 6 in stored
+                turn = n <= SERIAL or (n - 1, G - 1) not in todo
+                if left and order.index((g, c)) < u and free and turn and (g == 0 or (n, g - 1) not in todo):
+                    mm2(n, g)
+                    todo.remove((n, g))
                     left = left - 1
-            if u >= units - 2:
-                for gg in range(G - 1):
-                    mm2(6 + u - (units - 2), gg)
-        quant_h(G - 1, 2, 3)
-        quant_h(G - 1, 3, 4)
-
-        for i in range(6):
-            for g in range(done[i], G - 1):
-                mm2(i, g)
-        for i in range(8):
-            mm2(i, G - 1)
-            store(i)
-        for i in range(8, TILES):
-            for g in range(G):
-                mm2(i, g)
-            store(i)
+                    if g == G - 1:
+                        if u == UNITS:
+                            store(n, n % 2 == 0)
+                            stored.append(n)
+                        else:
+                            full.append(n)
+        assert not todo and not full

@@ -36,6 +36,19 @@ AHEAD = (4, 5)
 QH_FIRST = False
 SPLIT = 12
 SERIAL = 12
+JOBS_FIRST = 6
+JOBS_ALL = 6
+GU = ()
+EV2_S = True
+HEAD_EV = 9
+Q1_AT = 8
+SQ_V = ()
+NB = 4
+LOOK = 2
+LOOK_AT = 4
+LOOK2 = 3
+WARM = ()
+LAST = (4, 4, 2, 2, 2, 2)
 
 
 def tile_bcs_gap_step_s13_kernel(tc, phi, coef_bytes, coef_scale, energy, v_words, v_scales, out):
@@ -74,6 +87,13 @@ def tile_bcs_gap_step_s13_kernel(tc, phi, coef_bytes, coef_scale, energy, v_word
         make_identity(nc, ident[:])
         nc.vector.memset(vs[:].rearrange("p g n -> p (g n)").bitcast(I32), 0)
 
+        def load_scales(g0=0, g1=G):
+            for quad in range(4):
+                nc.sync.dma_start(
+                    out=vs[32 * quad : 32 * quad + 4, g0:g1, :].bitcast(I32),
+                    in_=v_scales[g0:g1, 4 * quad : 4 * quad + 4, :].rearrange("g r n -> r g n").bitcast(I32),
+                )
+
         nc.sync.dma_start(out=cs[:], in_=cs_v)
         nc.sync.dma_start(out=cb[0][:], in_=cb_v[0])
         load_en(0, 0, 2)
@@ -84,15 +104,18 @@ def tile_bcs_gap_step_s13_kernel(tc, phi, coef_bytes, coef_scale, energy, v_word
         load_en(2, 0, 4)
         load_phi(1)
         load_en(3, 0, 4)
-        for j in range(2, 2 * G):
-            load_phi(j)
-        for quad in range(4):
-            nc.sync.dma_start(
-                out=vs[32 * quad : 32 * quad + 4, :, :].bitcast(I32),
-                in_=v_scales[:, 4 * quad : 4 * quad + 4, :].rearrange("g r n -> r g n").bitcast(I32),
-            )
-        for g in range(G):
-            load_v(g)
+        load_phi(2)
+        load_phi(3)
+        load_phi(4)
+        load_phi(5)
+        load_phi(6)
+        load_phi(7)
+        load_scales(0, 2)
+        load_v(0)
+        load_v(1)
+        load_scales(2, 4)
+        load_v(2)
+        load_v(3)
 
         cc = keep.tile([P, PASSES, B], U32, name="cc", align_bytes=64)
         csc = keep.tile([P, PASSES, B], U8, name="csc", align_bytes=64)
@@ -140,7 +163,7 @@ def tile_bcs_gap_step_s13_kernel(tc, phi, coef_bytes, coef_scale, energy, v_word
         grouped = {}
 
         def transposes(j):
-            bank = psum.tile([P, PASSES, 2, P], F32, name="tbank", tag="bank%d" % (2 + (j + 4) % 6), bufs=1)
+            bank = psum.tile([P, PASSES, 2, P], F32, name="tbank", tag="bank%d" % (2 + (j + 4) % 6 if j < TILES - 2 else j - 8), bufs=1)
             words = ph[j // 2][:, j % 2, :].bitcast(F32)
             for k in range(PASSES):
                 for u in range(2):
@@ -189,7 +212,8 @@ def tile_bcs_gap_step_s13_kernel(tc, phi, coef_bytes, coef_scale, energy, v_word
         def divide(u):
             g, c = order[u]
             cols = slice(c * NC, (c + 1) * NC)
-            nc.vector.tensor_tensor(out=weight[g][:, :, cols], in0=weight[g][:, :, cols], in1=inv[u][:], op=MULT)
+            eng = nc.gpsimd if u in GU else nc.vector
+            eng.tensor_tensor(out=weight[g][:, :, cols], in0=weight[g][:, :, cols], in1=inv[u][:], op=MULT)
 
         def make_h(u):
             g, c = order[u]
@@ -212,13 +236,13 @@ def tile_bcs_gap_step_s13_kernel(tc, phi, coef_bytes, coef_scale, energy, v_word
             )
 
         parts = [(c, i0, QUAD) for c in range(CH) for i0 in range(0, TILES, QUAD)]
-        parts = parts[:-1] + [(CH - 1, TILES - QUAD, 2), (CH - 1, TILES - 2, 2)]
+        parts = parts[:-QUAD] + [(CH - 1, sum(LAST[:n]), count) for n, count in enumerate(LAST)]
         sums = {}
 
         def mm2(n, g):
             c, i0, count = parts[n]
             if g == 0:
-                sums[n] = psum.tile([P, count, NC], F32, name="obank", tag="bank%d" % (2 + (2 + n) % 6), bufs=1)
+                sums[n] = psum.tile([P, count, NC], F32, name="obank", tag="bank%d" % (2 + n % 6), bufs=1)
             cols = slice(c * NC, (c + 1) * NC)
             for k in range(count):
                 i = i0 + k
@@ -287,8 +311,8 @@ def tile_bcs_gap_step_s13_kernel(tc, phi, coef_bytes, coef_scale, energy, v_word
                 evacuate(j, j not in EV_V)
                 emptied = j + 1
             for j in pair:
-                if j + 6 < TILES:
-                    transposes(j + 6)
+                if TILES - 4 <= j < TILES - 2:
+                    transposes(j + 2)
             for n in range(2 if u in AHEAD else 1):
                 if roots < UNITS:
                     inv_sqrt(roots)
@@ -297,7 +321,9 @@ def tile_bcs_gap_step_s13_kernel(tc, phi, coef_bytes, coef_scale, energy, v_word
                 roots = roots + 1
             if u > 0 and QH_FIRST:
                 quant_h(u - 1)
-            if u + 1 < UNITS:
+            if u + 2 in GU:
+                divide(u + 2)
+            if u + 1 < UNITS and u + 1 not in GU:
                 divide(u + 1)
             if u > 0 and not QH_FIRST:
                 quant_h(u - 1)
@@ -306,16 +332,16 @@ def tile_bcs_gap_step_s13_kernel(tc, phi, coef_bytes, coef_scale, energy, v_word
             for g in range(2, G):
                 if u == QUANT_AT[g]:
                     quant_phi(g)
-            if u + 2 < UNITS:
+            if u + 2 < UNITS and u >= JOBS_FIRST:
                 mm1(u + 2)
             for n in full:
                 store(n, n not in ST_V)
                 stored.append(n)
             full = []
-            left = JOBS if u < UNITS else len(todo)
+            left = JOBS if JOBS_ALL <= u < UNITS else len(todo)
             for n, g in list(todo):
                 c = parts[n][0]
-                free = emptied > TILES - 6 + n if n < 6 else n - 6 in stored
+                free = emptied > 8 + n if n < 4 else emptied > 10 + n if n < 6 else n - 6 in stored
                 turn = n <= SERIAL or (n - 1, G - 1) not in todo
                 if left and order.index((g, c)) < u and free and turn and (g == 0 or (n, g - 1) not in todo):
                     mm2(n, g)
@@ -327,4 +353,6 @@ def tile_bcs_gap_step_s13_kernel(tc, phi, coef_bytes, coef_scale, energy, v_word
                             stored.append(n)
                         else:
                             full.append(n)
+            if u + 2 < UNITS and u < JOBS_FIRST:
+                mm1(u + 2)
         assert not todo and not full

@@ -28,27 +28,29 @@ QUAD = 4
 UNITS = G * CH
 IL = 4
 ORDER = [(0, 0), (1, 0), (0, 1), (2, 0), (1, 1), (3, 0), (2, 1), (3, 1)] + [(g, c) for c in (2, 3) for g in range(G)]
-EV_V = (8, 12)
+EV_V = ()
 QUANT_AT = {2: 1, 3: 3}
 ST_V = ()
 JOBS = 4
-AHEAD = (4, 5)
-QH_FIRST = False
+AHEAD = (0,4,5)
 SPLIT = 12
 SERIAL = 12
-JOBS_FIRST = 6
-JOBS_ALL = 6
+JOBS_FIRST = 7
+JOBS_ALL = 7
 GU = ()
 EV2_S = True
-HEAD_EV = 9
+HEAD_EV = 12
 Q1_AT = 8
 SQ_V = ()
 NB = 4
 LOOK = 2
 LOOK_AT = 4
 LOOK2 = 3
-WARM = ()
 LAST = (4, 4, 2, 2, 2, 2)
+QH_AT = (2,4)
+SQUARED = 3
+EV_FROM = 0
+MM0 = 8
 
 
 def tile_bcs_gap_step_s13_kernel(tc, phi, coef_bytes, coef_scale, energy, v_words, v_scales, out):
@@ -101,11 +103,11 @@ def tile_bcs_gap_step_s13_kernel(tc, phi, coef_bytes, coef_scale, energy, v_word
         load_en(0, 2, 4)
         load_en(1, 0, 4)
         load_phi(0)
-        load_en(2, 0, 4)
         load_phi(1)
-        load_en(3, 0, 4)
+        load_en(2, 0, 4)
         load_phi(2)
         load_phi(3)
+        load_en(3, 0, 4)
         load_phi(4)
         load_phi(5)
         load_phi(6)
@@ -120,7 +122,7 @@ def tile_bcs_gap_step_s13_kernel(tc, phi, coef_bytes, coef_scale, energy, v_word
         cc = keep.tile([P, PASSES, B], U32, name="cc", align_bytes=64)
         csc = keep.tile([P, PASSES, B], U8, name="csc", align_bytes=64)
         wide = [keep.tile([P, PACK, B], BF16, name="wide%d" % k, align_bytes=64) for k in range(PASSES)]
-        cgrp = [keep.tile([P, B, PACK], BF16, name="cgrp%d" % k, align_bytes=64) for k in range(PASSES)]
+        cgrp = [keep.tile([P, B, PACK], BF16, name="cgrp%d" % k, tag="cgrp%d" % k, align_bytes=64) for k in range(PASSES)]
         weight = [keep.tile([P, PACK, B], F32, name="weight%d" % g, align_bytes=64) for g in range(G)]
         pc = [keep.tile([P, PACK, PASSES, P], U32, name="pc%d" % g, align_bytes=64) for g in range(G)]
         psc = [keep.tile([P, PACK, PASSES, P], U8, name="psc%d" % g, align_bytes=64) for g in range(G)]
@@ -150,20 +152,30 @@ def tile_bcs_gap_step_s13_kernel(tc, phi, coef_bytes, coef_scale, energy, v_word
             nc.scalar.activation(out=weight[g][:, t0:t1, :], in_=en[g][:, t0:t1, :], func=ACT.Tanh)
 
         inv = {}
+        squared = {}
+
+        def square_energy(u, pool, tag):
+            if u < SQUARED:
+                g, c = order[u]
+                cols = slice(c * NC, (c + 1) * NC)
+                squared[u] = pool.tile([P, PACK, NC], F32, name="esq", tag=tag, bufs=1, align_bytes=64)
+                nc.gpsimd.tensor_tensor(out=squared[u][:], in0=en[g][:, :, cols], in1=en[g][:, :, cols], op=MULT)
 
         def inv_sqrt(u):
             g, c = order[u]
             inv[u] = stage.tile([P, PACK, NC], F32, name="inv", tag="inv", bufs=6, align_bytes=64)
-            nc.scalar.activation(out=inv[u][:], in_=en[g][:, :, c * NC : (c + 1) * NC], func=ACT.Abs_reciprocal_sqrt)
+            src = squared[u][:] if u < SQUARED else en[g][:, :, c * NC : (c + 1) * NC]
+            nc.scalar.activation(out=inv[u][:], in_=src, func=ACT.Abs_reciprocal_sqrt)
 
         def square(u):
-            nc.scalar.activation(out=inv[u][:], in_=inv[u][:], func=ACT.Square)
+            if u >= SQUARED:
+                nc.scalar.activation(out=inv[u][:], in_=inv[u][:], func=ACT.Square)
 
         turned = {}
         grouped = {}
 
         def transposes(j):
-            bank = psum.tile([P, PASSES, 2, P], F32, name="tbank", tag="bank%d" % (2 + (j + 4) % 6 if j < TILES - 2 else j - 8), bufs=1)
+            bank = psum.tile([P, PASSES, 2, P], F32, name="tbank", tag="bank%d" % (2 + (j + 4) % 6), bufs=1)
             words = ph[j // 2][:, j % 2, :].bitcast(F32)
             for k in range(PASSES):
                 for u in range(2):
@@ -173,7 +185,7 @@ def tile_bcs_gap_step_s13_kernel(tc, phi, coef_bytes, coef_scale, energy, v_word
         def evacuate(j, on_scalar):
             g, t = divmod(j, PACK)
             if t == 0:
-                grouped[g] = stage.tile([P, PACK, PASSES * P * PACK], BF16, name="grp", tag="grp", bufs=2, align_bytes=64)
+                grouped[g] = stage.tile([P, PACK, PASSES * P * PACK], BF16, name="grp", tag="grp%d" % g, bufs=1, align_bytes=64)
             dst = grouped[g][:, t, :].bitcast(F32).rearrange("p (k r u) -> p k r u", k=PASSES, u=2)
             src = turned[j][:].rearrange("p k u r -> p k r u")
             if on_scalar:
@@ -242,7 +254,7 @@ def tile_bcs_gap_step_s13_kernel(tc, phi, coef_bytes, coef_scale, energy, v_word
         def mm2(n, g):
             c, i0, count = parts[n]
             if g == 0:
-                sums[n] = psum.tile([P, count, NC], F32, name="obank", tag="bank%d" % (2 + n % 6), bufs=1)
+                sums[n] = psum.tile([P, count, NC], F32, name="obank", tag="bank%d" % (2 + (2 + n) % 6), bufs=1)
             cols = slice(c * NC, (c + 1) * NC)
             for k in range(count):
                 i = i0 + k
@@ -265,67 +277,84 @@ def tile_bcs_gap_step_s13_kernel(tc, phi, coef_bytes, coef_scale, energy, v_word
                 nc.vector.tensor_copy(out=o[:], in_=sums[n][:])
             nc.sync.dma_start(out=out_v[c][:, i0 : i0 + count, :], in_=o[:])
 
-        tanh(0, 0, 2)
-        tanh(0, 2, 4)
-        for g in range(1, G):
-            tanh(g, 0, 4)
         for k in range(PASSES):
             coef_widen(k)
         for k in range(PASSES):
             coef_interleave(k)
+        for k in range(PASSES):
+            coef_quant(k)
+        square_energy(0, keep, "cgrp1")
         for j in range(6):
             transposes(j)
-        coef_quant(0)
-        for j in range(PACK):
-            evacuate(j, False)
-        coef_quant(1)
-        quant_phi(0)
-        transposes(6)
-        transposes(7)
-        transposes(8)
-        transposes(9)
-        for j in range(PACK, 2 * PACK):
-            evacuate(j, False)
-            if j + 6 < SPLIT:
-                transposes(j + 6)
+        tanh(0, 0, 2)
+        tanh(0, 2, 4)
+        tanh(1, 0, 4)
+        for g in range(2):
+            for j in range(PACK * g, PACK * g + PACK):
+                evacuate(j, j % PACK < 2)
+                if j % PACK == 1:
+                    tanh(2 + g, 0, 4)
+            quant_phi(g)
+            square_energy(g + 1, stage, "grp%d" % g)
+            if g == 0:
+                transposes(6)
+                transposes(7)
+                if MM0 == 8:
+                    mm1(0)
+                transposes(8)
+                transposes(9)
+                if MM0 == 10:
+                    mm1(0)
+        for j in range(10, SPLIT):
+            transposes(j)
+        if MM0 == 12:
+            mm1(0)
+        mm1(1)
+        for j in range(SPLIT, 14):
+            transposes(j)
         inv_sqrt(0)
         inv_sqrt(1)
         square(0)
         inv_sqrt(2)
         square(1)
-        quant_phi(1)
-        mm1(0)
-        mm1(1)
-        for j in range(SPLIT, 2 * PACK + 6):
-            transposes(j)
+        for j in range(2 * PACK, HEAD_EV):
+            evacuate(j, False)
+            if j + 6 < TILES:
+                transposes(j + 6)
+        if QUANT_AT[2] < 0:
+            quant_phi(2)
         divide(0)
 
         todo = [(n, g) for n in range(len(parts)) for g in range(G)]
         full = []
         stored = []
-        emptied = 2 * PACK
+        emptied = HEAD_EV
         roots = 3
         for u in range(UNITS + 1):
-            pair = range(emptied, min(emptied + 2, TILES))
-            for j in pair:
-                evacuate(j, j not in EV_V)
-                emptied = j + 1
-            for j in pair:
-                if TILES - 4 <= j < TILES - 2:
-                    transposes(j + 2)
+            if u in QH_AT:
+                quant_h(u - 1)
+            for n in full:
+                store(n, n not in ST_V)
+                stored.append(n)
+            full = []
             for n in range(2 if u in AHEAD else 1):
                 if roots < UNITS:
                     inv_sqrt(roots)
                 if roots - 1 < UNITS:
                     square(roots - 1)
                 roots = roots + 1
-            if u > 0 and QH_FIRST:
-                quant_h(u - 1)
+            pair = range(emptied, min(emptied + (2 if u >= EV_FROM else 0), TILES))
+            for j in pair:
+                evacuate(j, j not in EV_V)
+                emptied = j + 1
+            for j in pair:
+                if j + 6 < TILES:
+                    transposes(j + 6)
             if u + 2 in GU:
                 divide(u + 2)
             if u + 1 < UNITS and u + 1 not in GU:
                 divide(u + 1)
-            if u > 0 and not QH_FIRST:
+            if u > 0 and u not in QH_AT:
                 quant_h(u - 1)
             if u < UNITS:
                 make_h(u)
@@ -334,14 +363,10 @@ def tile_bcs_gap_step_s13_kernel(tc, phi, coef_bytes, coef_scale, energy, v_word
                     quant_phi(g)
             if u + 2 < UNITS and u >= JOBS_FIRST:
                 mm1(u + 2)
-            for n in full:
-                store(n, n not in ST_V)
-                stored.append(n)
-            full = []
             left = JOBS if JOBS_ALL <= u < UNITS else len(todo)
             for n, g in list(todo):
                 c = parts[n][0]
-                free = emptied > 8 + n if n < 4 else emptied > 10 + n if n < 6 else n - 6 in stored
+                free = emptied > TILES - 6 + n if n < 6 else n - 6 in stored
                 turn = n <= SERIAL or (n - 1, G - 1) not in todo
                 if left and order.index((g, c)) < u and free and turn and (g == 0 or (n, g - 1) not in todo):
                     mm2(n, g)

@@ -32,14 +32,14 @@ EV_V = ()
 QUANT_AT = {2: 1, 3: 3}
 ST_V = ()
 JOBS = 4
-AHEAD = (0,4,5)
+AHEAD = (4,5)
 SPLIT = 12
 SERIAL = 12
 JOBS_FIRST = 7
 JOBS_ALL = 7
 GU = ()
 EV2_S = True
-HEAD_EV = 12
+HEAD_EV = 10
 Q1_AT = 8
 SQ_V = ()
 NB = 4
@@ -51,6 +51,9 @@ QH_AT = (2,4)
 SQUARED = 3
 EV_FROM = 0
 MM0 = 8
+S_HEAD = (0,1)
+TANH_AT = {1: (2,3)}
+G_AT = {0: (1,2), 1: ()}
 
 
 def tile_bcs_gap_step_s13_kernel(tc, phi, coef_bytes, coef_scale, energy, v_words, v_scales, out):
@@ -106,8 +109,8 @@ def tile_bcs_gap_step_s13_kernel(tc, phi, coef_bytes, coef_scale, energy, v_word
         load_phi(1)
         load_en(2, 0, 4)
         load_phi(2)
-        load_phi(3)
         load_en(3, 0, 4)
+        load_phi(3)
         load_phi(4)
         load_phi(5)
         load_phi(6)
@@ -291,11 +294,13 @@ def tile_bcs_gap_step_s13_kernel(tc, phi, coef_bytes, coef_scale, energy, v_word
         tanh(1, 0, 4)
         for g in range(2):
             for j in range(PACK * g, PACK * g + PACK):
-                evacuate(j, j % PACK < 2)
-                if j % PACK == 1:
-                    tanh(2 + g, 0, 4)
+                evacuate(j, j in S_HEAD)
+                if j in TANH_AT:
+                    for gg in TANH_AT[j]:
+                        tanh(gg, 0, 4)
             quant_phi(g)
-            square_energy(g + 1, stage, "grp%d" % g)
+            for u in G_AT[g]:
+                square_energy(u, stage, "grp%d" % g if u == G_AT[g][0] else "esq")
             if g == 0:
                 transposes(6)
                 transposes(7)
@@ -305,11 +310,10 @@ def tile_bcs_gap_step_s13_kernel(tc, phi, coef_bytes, coef_scale, energy, v_word
                 transposes(9)
                 if MM0 == 10:
                     mm1(0)
-        for j in range(10, SPLIT):
+        for j in range(10, min(SPLIT, 14)):
             transposes(j)
-        if MM0 == 12:
-            mm1(0)
-        mm1(1)
+        if SPLIT < TILES:
+            mm1(1)
         for j in range(SPLIT, 14):
             transposes(j)
         inv_sqrt(0)
@@ -321,8 +325,8 @@ def tile_bcs_gap_step_s13_kernel(tc, phi, coef_bytes, coef_scale, energy, v_word
             evacuate(j, False)
             if j + 6 < TILES:
                 transposes(j + 6)
-        if QUANT_AT[2] < 0:
-            quant_phi(2)
+        if SPLIT == TILES:
+            mm1(1)
         divide(0)
 
         todo = [(n, g) for n in range(len(parts)) for g in range(G)]

@@ -19,118 +19,96 @@ MULT = mybir.AluOpType.mult
 
 P = 128
 PACK = 4
-G = M // 512
-PASSES = R // 512
+GROUPS = M // (P * PACK)
+PASSES = R // (P * PACK)
 NC = 128
-CH = B // NC
+CHUNKS = B // NC
+UNITS = GROUPS * CHUNKS
 TILES = M // P
-QUAD = 4
-UNITS = G * CH
-IL = 4
-ORDER = [(0, 0), (1, 0), (0, 1), (2, 0), (1, 1), (3, 0), (2, 1), (3, 1)] + [(g, c) for c in (2, 3) for g in range(G)]
-EV_V = ()
-QUANT_AT = {2: 1, 3: 3}
-ST_V = ()
-JOBS = 4
-AHEAD = (4,5)
-SPLIT = 12
-SERIAL = 12
-JOBS_FIRST = 7
-JOBS_ALL = 7
-GU = ()
-EV2_S = True
-HEAD_EV = 10
-Q1_AT = 8
-SQ_V = ()
-NB = 4
-LOOK = 2
-LOOK_AT = 4
-LOOK2 = 3
-LAST = (4, 4, 2, 2, 2, 2)
-QH_AT = (2,4)
-SQUARED = 3
-EV_FROM = 0
-MM0 = 8
-S_HEAD = (0,1)
-TANH_AT = {1: (2,3)}
-G_AT = {0: (1,2), 1: ()}
+RUN = 4
+
+GAP_BANKS = 2
+WORK_BANKS = 6
+PART = 4
+LAST_PARTS = (4, 4, 2, 2, 2, 2)
+PASSES_A_STEP = 4
+AHEAD = (4, 5)
+FILL_STEPS = 7
 
 
 def tile_bcs_gap_step_s13_kernel(tc, phi, coef_bytes, coef_scale, energy, v_words, v_scales, out):
     nc = tc.nc
-    order = ORDER
+    order = sorted(((g, c) for g in range(GROUPS) for c in range(2)), key=lambda u: (u[0] + 2 * u[1], -u[1]))
+    order = order + [(g, c) for c in range(2, CHUNKS) for g in range(GROUPS)]
+    parts = [(c, i0, PART) for c in range(CHUNKS - 1) for i0 in range(0, TILES, PART)]
+    parts = parts + [(CHUNKS - 1, sum(LAST_PARTS[:n]), count) for n, count in enumerate(LAST_PARTS)]
+    first_of_last_chunk = len(parts) - len(LAST_PARTS)
+
     with ExitStack() as ctx:
         keep = ctx.enter_context(tc.tile_pool(name="keep", bufs=1))
         stage = ctx.enter_context(tc.tile_pool(name="stage", bufs=2))
-        psum = ctx.enter_context(tc.psum_pool(name="psum", bufs=2))
+        psum = ctx.enter_context(tc.psum_pool(name="psum", bufs=1))
         ctx.enter_context(tc.manual_schedule())
 
-        en = [keep.tile([P, PACK, B], BF16, name="en%d" % g, align_bytes=64) for g in range(G)]
-        ph = [keep.tile([P, 2, R], BF16, name="ph%d" % j, align_bytes=64) for j in range(2 * G)]
+        def bank_tile(shape, bank):
+            return psum.tile(shape, F32, name="bank", tag="bank%d" % bank, bufs=1)
+
+        en = [keep.tile([P, PACK, B], BF16, name="en%d" % g, align_bytes=64) for g in range(GROUPS)]
+        ph = [keep.tile([P, 2, R], BF16, name="ph%d" % j, align_bytes=64) for j in range(TILES // 2)]
         cb = [keep.tile([P, PACK * B], U8, name="cb%d" % k, align_bytes=64) for k in range(PASSES)]
         cs = keep.tile([P, PASSES, PACK], F32, name="cs", align_bytes=64)
-        vw = [keep.tile([P, 2 * M], U8, name="vw%d" % g, align_bytes=64) for g in range(G)]
-        vs = keep.tile([P, G, M], U8, name="vs", align_bytes=64)
+        vw = [keep.tile([P, 2 * M], U8, name="vw%d" % g, align_bytes=64) for g in range(GROUPS)]
+        vs = keep.tile([P, GROUPS, M], U8, name="vs", align_bytes=64)
         ident = keep.tile([P, P], F32, name="ident", align_bytes=64)
 
         phi_v = phi.rearrange("(g p t) k -> g p t k", p=P, t=PACK)
         en_v = energy.rearrange("(g p t) n -> g p t n", p=P, t=PACK)
-        cb_v = coef_bytes.rearrange("(g p t) n -> g p (t n)", p=P, t=PACK)
-        cs_v = coef_scale.rearrange("(g p t) o -> p g (t o)", p=P, t=PACK)
+        cb_v = coef_bytes.rearrange("(k p t) n -> k p (t n)", p=P, t=PACK)
+        cs_v = coef_scale.rearrange("(k p t) o -> p k (t o)", p=P, t=PACK)
         out_v = out.rearrange("(i p) (c n) -> c p i n", p=P, n=NC)
 
-        def load_en(g, t0, t1):
+        def load_coef(k):
+            nc.sync.dma_start(out=cb[k][:], in_=cb_v[k])
+
+        def load_energy(g, t0=0, t1=PACK):
             nc.sync.dma_start(out=en[g][:, t0:t1, :], in_=en_v[g][:, t0:t1, :])
 
-        def load_phi(j):
-            g, half = divmod(j, 2)
-            nc.sync.dma_start(out=ph[j][:], in_=phi_v[g][:, 2 * half : 2 * half + 2, :])
+        def load_phi(pair):
+            g, half = divmod(pair, 2)
+            nc.sync.dma_start(out=ph[pair][:], in_=phi_v[g][:, 2 * half : 2 * half + 2, :])
 
-        def load_v(g):
-            nc.sync.dma_start(out=vw[g][:], in_=v_words[g])
-
-        make_identity(nc, ident[:])
-        nc.vector.memset(vs[:].rearrange("p g n -> p (g n)").bitcast(I32), 0)
-
-        def load_scales(g0=0, g1=G):
+        def load_v(g0, g1):
             for quad in range(4):
                 nc.sync.dma_start(
                     out=vs[32 * quad : 32 * quad + 4, g0:g1, :].bitcast(I32),
                     in_=v_scales[g0:g1, 4 * quad : 4 * quad + 4, :].rearrange("g r n -> r g n").bitcast(I32),
                 )
+            for g in range(g0, g1):
+                nc.sync.dma_start(out=vw[g][:], in_=v_words[g])
+
+        make_identity(nc, ident[:])
+        nc.vector.memset(vs[:].rearrange("p g n -> p (g n)").bitcast(I32), 0)
 
         nc.sync.dma_start(out=cs[:], in_=cs_v)
-        nc.sync.dma_start(out=cb[0][:], in_=cb_v[0])
-        load_en(0, 0, 2)
-        nc.sync.dma_start(out=cb[1][:], in_=cb_v[1])
-        load_en(0, 2, 4)
-        load_en(1, 0, 4)
+        load_coef(0)
+        load_energy(0, 0, 2)
+        load_coef(1)
+        load_energy(0, 2, PACK)
+        load_energy(1)
         load_phi(0)
         load_phi(1)
-        load_en(2, 0, 4)
+        load_energy(2)
         load_phi(2)
-        load_en(3, 0, 4)
-        load_phi(3)
-        load_phi(4)
-        load_phi(5)
-        load_phi(6)
-        load_phi(7)
-        load_scales(0, 2)
-        load_v(0)
-        load_v(1)
-        load_scales(2, 4)
-        load_v(2)
-        load_v(3)
+        load_energy(3)
+        for pair in range(3, TILES // 2):
+            load_phi(pair)
+        load_v(0, 2)
+        load_v(2, GROUPS)
 
         cc = keep.tile([P, PASSES, B], U32, name="cc", align_bytes=64)
         csc = keep.tile([P, PASSES, B], U8, name="csc", align_bytes=64)
         wide = [keep.tile([P, PACK, B], BF16, name="wide%d" % k, align_bytes=64) for k in range(PASSES)]
         cgrp = [keep.tile([P, B, PACK], BF16, name="cgrp%d" % k, tag="cgrp%d" % k, align_bytes=64) for k in range(PASSES)]
-        weight = [keep.tile([P, PACK, B], F32, name="weight%d" % g, align_bytes=64) for g in range(G)]
-        pc = [keep.tile([P, PACK, PASSES, P], U32, name="pc%d" % g, align_bytes=64) for g in range(G)]
-        psc = [keep.tile([P, PACK, PASSES, P], U8, name="psc%d" % g, align_bytes=64) for g in range(G)]
-        hc = [keep.tile([P, B], U32, name="hc%d" % g, align_bytes=64) for g in range(G)]
-        hs = [keep.tile([P, B], U8, name="hs%d" % g, align_bytes=64) for g in range(G)]
 
         def coef_widen(k):
             for t in range(PACK):
@@ -144,41 +122,23 @@ def tile_bcs_gap_step_s13_kernel(tc, phi, coef_bytes, coef_scale, energy, v_word
 
         def coef_interleave(k):
             nc.vector.tensor_copy(
-                out=cgrp[k][:].rearrange("p (c i) t -> p c t i", i=4),
-                in_=wide[k][:].rearrange("p t (c i) -> p c t i", i=4),
+                out=cgrp[k][:].rearrange("p (c i) t -> p c t i", i=RUN),
+                in_=wide[k][:].rearrange("p t (c i) -> p c t i", i=RUN),
             )
 
         def coef_quant(k):
             nc.vector.quantize_mx(out=cc[:, k, :].bitcast(FP8X4), scales=csc[:, k, :], in_=cgrp[k][:].rearrange("p n t -> p (n t)"))
 
-        def tanh(g, t0, t1):
-            nc.scalar.activation(out=weight[g][:, t0:t1, :], in_=en[g][:, t0:t1, :], func=ACT.Tanh)
-
-        inv = {}
-        squared = {}
-
-        def square_energy(u, pool, tag):
-            if u < SQUARED:
-                g, c = order[u]
-                cols = slice(c * NC, (c + 1) * NC)
-                squared[u] = pool.tile([P, PACK, NC], F32, name="esq", tag=tag, bufs=1, align_bytes=64)
-                nc.gpsimd.tensor_tensor(out=squared[u][:], in0=en[g][:, :, cols], in1=en[g][:, :, cols], op=MULT)
-
-        def inv_sqrt(u):
-            g, c = order[u]
-            inv[u] = stage.tile([P, PACK, NC], F32, name="inv", tag="inv", bufs=6, align_bytes=64)
-            src = squared[u][:] if u < SQUARED else en[g][:, :, c * NC : (c + 1) * NC]
-            nc.scalar.activation(out=inv[u][:], in_=src, func=ACT.Abs_reciprocal_sqrt)
-
-        def square(u):
-            if u >= SQUARED:
-                nc.scalar.activation(out=inv[u][:], in_=inv[u][:], func=ACT.Square)
-
+        pc = [keep.tile([P, PACK, PASSES, P], U32, name="pc%d" % g, align_bytes=64) for g in range(GROUPS)]
+        psc = [keep.tile([P, PACK, PASSES, P], U8, name="psc%d" % g, align_bytes=64) for g in range(GROUPS)]
         turned = {}
         grouped = {}
 
+        def turn_bank(j):
+            return GAP_BANKS + (j + PART) % WORK_BANKS
+
         def transposes(j):
-            bank = psum.tile([P, PASSES, 2, P], F32, name="tbank", tag="bank%d" % (2 + (j + 4) % 6), bufs=1)
+            bank = bank_tile([P, PASSES, 2, P], turn_bank(j))
             words = ph[j // 2][:, j % 2, :].bitcast(F32)
             for k in range(PASSES):
                 for u in range(2):
@@ -203,11 +163,43 @@ def tile_bcs_gap_step_s13_kernel(tc, phi, coef_bytes, coef_scale, energy, v_word
                 in_=grouped[g][:].rearrange("p t x -> p (t x)"),
             )
 
-        gaps = {}
+        weight = [keep.tile([P, PACK, B], F32, name="weight%d" % g, align_bytes=64) for g in range(GROUPS)]
+        squared = {}
+        inv = {}
 
-        def mm1(u):
+        def tanh(g, t0=0, t1=PACK):
+            nc.scalar.activation(out=weight[g][:, t0:t1, :], in_=en[g][:, t0:t1, :], func=ACT.Tanh)
+
+        def square_energy(eng, g, chunks, pool, tag):
+            width = chunks * NC
+            esq = pool.tile([P, PACK, width], F32, name="esq", tag=tag, bufs=1, align_bytes=64)
+            eng.tensor_tensor(out=esq[:], in0=en[g][:, :, :width], in1=en[g][:, :, :width], op=MULT)
+            for c in range(chunks):
+                squared[g, c] = esq[:, :, c * NC : (c + 1) * NC]
+
+        def inv_sqrt(u):
             g, c = order[u]
-            bank = psum.tile([P, PACK, NC], F32, name="gbank", tag="bank%d" % (u % 2), bufs=1)
+            inv[u] = stage.tile([P, PACK, NC], F32, name="inv", tag="inv", bufs=6, align_bytes=64)
+            src = squared[g, c] if (g, c) in squared else en[g][:, :, c * NC : (c + 1) * NC]
+            nc.scalar.activation(out=inv[u][:], in_=src, func=ACT.Abs_reciprocal_sqrt)
+
+        def square_root(u):
+            if order[u] not in squared:
+                nc.scalar.activation(out=inv[u][:], in_=inv[u][:], func=ACT.Square)
+
+        def divide(u):
+            g, c = order[u]
+            w = weight[g][:, :, c * NC : (c + 1) * NC]
+            nc.vector.tensor_tensor(out=w, in0=w, in1=inv[u][:], op=MULT)
+
+        hc = [keep.tile([P, B], U32, name="hc%d" % g, align_bytes=64) for g in range(GROUPS)]
+        hs = [keep.tile([P, B], U8, name="hs%d" % g, align_bytes=64) for g in range(GROUPS)]
+        gaps = {}
+        hgrp = {}
+
+        def first_product(u):
+            g, c = order[u]
+            bank = bank_tile([P, PACK, NC], u % GAP_BANKS)
             cols = slice(c * NC, (c + 1) * NC)
             for t in range(PACK):
                 for k in range(PASSES):
@@ -222,53 +214,41 @@ def tile_bcs_gap_step_s13_kernel(tc, phi, coef_bytes, coef_scale, energy, v_word
                     )
             gaps[u] = bank
 
-        hgrp = {}
-
-        def divide(u):
-            g, c = order[u]
-            cols = slice(c * NC, (c + 1) * NC)
-            eng = nc.gpsimd if u in GU else nc.vector
-            eng.tensor_tensor(out=weight[g][:, :, cols], in0=weight[g][:, :, cols], in1=inv[u][:], op=MULT)
-
         def make_h(u):
             g, c = order[u]
             hgrp[u] = stage.tile([P, NC, PACK], BF16, name="hg", tag="hg", bufs=3, align_bytes=64)
-            cols = slice(c * NC, (c + 1) * NC)
             nc.vector.tensor_tensor(
-                out=hgrp[u][:].rearrange("p (c i) t -> p c t i", i=IL),
-                in0=gaps[u][:].rearrange("p t (c i) -> p c t i", i=IL),
-                in1=weight[g][:, :, cols].rearrange("p t (c i) -> p c t i", i=IL),
+                out=hgrp[u][:].rearrange("p (c i) t -> p c t i", i=RUN),
+                in0=gaps[u][:].rearrange("p t (c i) -> p c t i", i=RUN),
+                in1=weight[g][:, :, c * NC : (c + 1) * NC].rearrange("p t (c i) -> p c t i", i=RUN),
                 op=MULT,
             )
 
         def quant_h(u):
             g, c = order[u]
             cols = slice(c * NC, (c + 1) * NC)
-            nc.vector.quantize_mx(
-                out=hc[g][:, cols].bitcast(FP8X4),
-                scales=hs[g][:, cols],
-                in_=hgrp[u][:].rearrange("p n t -> p (n t)"),
-            )
+            nc.vector.quantize_mx(out=hc[g][:, cols].bitcast(FP8X4), scales=hs[g][:, cols], in_=hgrp[u][:].rearrange("p n t -> p (n t)"))
 
-        parts = [(c, i0, QUAD) for c in range(CH) for i0 in range(0, TILES, QUAD)]
-        parts = parts[:-QUAD] + [(CH - 1, sum(LAST[:n]), count) for n, count in enumerate(LAST)]
         sums = {}
 
-        def mm2(n, g):
+        def part_bank(n):
+            return turn_bank(TILES - WORK_BANKS + n)
+
+        def part_pass(n, g):
             c, i0, count = parts[n]
             if g == 0:
-                sums[n] = psum.tile([P, count, NC], F32, name="obank", tag="bank%d" % (2 + (2 + n) % 6), bufs=1)
+                sums[n] = bank_tile([P, count, NC], part_bank(n))
             cols = slice(c * NC, (c + 1) * NC)
-            for k in range(count):
-                i = i0 + k
+            for i in range(count):
+                tile_i = i0 + i
                 nc.tensor.matmul_mx(
-                    out=sums[n][:, k, :],
-                    lhsT=vw[g][:, 2 * P * i : 2 * P * (i + 1)].bitcast(FP4X4),
-                    lhsT_scale=vs[:, g, P * i : P * (i + 1)],
+                    out=sums[n][:, i, :],
+                    lhsT=vw[g][:, 2 * P * tile_i : 2 * P * (tile_i + 1)].bitcast(FP4X4),
+                    lhsT_scale=vs[:, g, P * tile_i : P * (tile_i + 1)],
                     rhs=hc[g][:, cols].bitcast(FP8X4),
                     rhs_scale=hs[g][:, cols],
-                    start=(g == 0 and k == 0),
-                    stop=(g == G - 1 and k == count - 1),
+                    start=(g == 0 and i == 0),
+                    stop=(g == GROUPS - 1 and i == count - 1),
                 )
 
         def store(n, on_scalar):
@@ -286,102 +266,82 @@ def tile_bcs_gap_step_s13_kernel(tc, phi, coef_bytes, coef_scale, energy, v_word
             coef_interleave(k)
         for k in range(PASSES):
             coef_quant(k)
-        square_energy(0, keep, "cgrp1")
-        for j in range(6):
+        square_energy(nc.gpsimd, 2, 1, keep, "cgrp0")
+        for j in range(WORK_BANKS):
             transposes(j)
         tanh(0, 0, 2)
-        tanh(0, 2, 4)
-        tanh(1, 0, 4)
-        for g in range(2):
-            for j in range(PACK * g, PACK * g + PACK):
-                evacuate(j, j in S_HEAD)
-                if j in TANH_AT:
-                    for gg in TANH_AT[j]:
-                        tanh(gg, 0, 4)
-            quant_phi(g)
-            for u in G_AT[g]:
-                square_energy(u, stage, "grp%d" % g if u == G_AT[g][0] else "esq")
-            if g == 0:
-                transposes(6)
-                transposes(7)
-                if MM0 == 8:
-                    mm1(0)
-                transposes(8)
-                transposes(9)
-                if MM0 == 10:
-                    mm1(0)
-        for j in range(10, min(SPLIT, 14)):
+        tanh(0, 2, PACK)
+        tanh(1)
+        evacuate(0, True)
+        evacuate(1, True)
+        tanh(2)
+        tanh(3)
+        evacuate(2, False)
+        evacuate(3, False)
+        quant_phi(0)
+        square_energy(nc.vector, 0, 2, keep, "esq")
+        square_energy(nc.gpsimd, 1, 2, stage, "grp0")
+        first_product(0)
+        for j in range(WORK_BANKS, WORK_BANKS + PACK):
             transposes(j)
-        if SPLIT < TILES:
-            mm1(1)
-        for j in range(SPLIT, 14):
+        for j in range(PACK, 2 * PACK):
+            evacuate(j, False)
+        quant_phi(1)
+        for j in range(WORK_BANKS + PACK, WORK_BANKS + 2 * PACK):
             transposes(j)
+        first_product(1)
         inv_sqrt(0)
         inv_sqrt(1)
-        square(0)
         inv_sqrt(2)
-        square(1)
-        for j in range(2 * PACK, HEAD_EV):
-            evacuate(j, False)
-            if j + 6 < TILES:
-                transposes(j + 6)
-        if SPLIT == TILES:
-            mm1(1)
         divide(0)
 
-        todo = [(n, g) for n in range(len(parts)) for g in range(G)]
+        todo = [(n, g) for n in range(len(parts)) for g in range(GROUPS)]
         full = []
         stored = []
-        emptied = HEAD_EV
+        emptied = 2 * PACK
         roots = 3
         for u in range(UNITS + 1):
-            if u in QH_AT:
-                quant_h(u - 1)
             for n in full:
-                store(n, n not in ST_V)
+                store(n, True)
                 stored.append(n)
             full = []
-            for n in range(2 if u in AHEAD else 1):
+            for j in range(emptied, min(emptied + (PACK if u == 0 else 2), TILES)):
+                evacuate(j, True)
+                emptied = j + 1
+                if j + WORK_BANKS < TILES:
+                    transposes(j + WORK_BANKS)
+            for ahead in range(2 if u in AHEAD else 1):
                 if roots < UNITS:
                     inv_sqrt(roots)
                 if roots - 1 < UNITS:
-                    square(roots - 1)
+                    square_root(roots - 1)
                 roots = roots + 1
-            pair = range(emptied, min(emptied + (2 if u >= EV_FROM else 0), TILES))
-            for j in pair:
-                evacuate(j, j not in EV_V)
-                emptied = j + 1
-            for j in pair:
-                if j + 6 < TILES:
-                    transposes(j + 6)
-            if u + 2 in GU:
-                divide(u + 2)
-            if u + 1 < UNITS and u + 1 not in GU:
+            after_phi = u in (2, 4)
+            if after_phi:
+                quant_h(u - 1)
+            if u + 1 < UNITS:
                 divide(u + 1)
-            if u > 0 and u not in QH_AT:
+            if u > 0 and not after_phi:
                 quant_h(u - 1)
             if u < UNITS:
                 make_h(u)
-            for g in range(2, G):
-                if u == QUANT_AT[g]:
-                    quant_phi(g)
-            if u + 2 < UNITS and u >= JOBS_FIRST:
-                mm1(u + 2)
-            left = JOBS if JOBS_ALL <= u < UNITS else len(todo)
+            if u in (1, 3):
+                quant_phi(2 + u // 2)
+            if FILL_STEPS <= u < UNITS - 2:
+                first_product(u + 2)
+            left = PASSES_A_STEP if FILL_STEPS <= u < UNITS else len(todo)
             for n, g in list(todo):
-                c = parts[n][0]
-                free = emptied > TILES - 6 + n if n < 6 else n - 6 in stored
-                turn = n <= SERIAL or (n - 1, G - 1) not in todo
-                if left and order.index((g, c)) < u and free and turn and (g == 0 or (n, g - 1) not in todo):
-                    mm2(n, g)
+                has_h = order.index((g, parts[n][0])) < u
+                has_bank = emptied > TILES - WORK_BANKS + n if n < WORK_BANKS else n - WORK_BANKS in stored
+                in_turn = n <= first_of_last_chunk or (n - 1, GROUPS - 1) not in todo
+                if left and has_h and has_bank and in_turn and (n, g - 1) not in todo:
+                    part_pass(n, g)
                     todo.remove((n, g))
                     left = left - 1
-                    if g == G - 1:
-                        if u == UNITS:
-                            store(n, n % 2 == 0)
-                            stored.append(n)
-                        else:
-                            full.append(n)
-            if u + 2 < UNITS and u < JOBS_FIRST:
-                mm1(u + 2)
-        assert not todo and not full
+                    if g == GROUPS - 1 and u == UNITS:
+                        store(n, n % 2 == 0)
+                        stored.append(n)
+                    elif g == GROUPS - 1:
+                        full.append(n)
+            if u < FILL_STEPS:
+                first_product(u + 2)

@@ -57,8 +57,8 @@ def tile_bcs_gap_step_s13_kernel(tc, phi, coef_bytes, coef_scale, energy, v_word
         ph = [keep.tile([P, 2, R], BF16, name="ph%d" % j, align_bytes=64) for j in range(TILES // 2)]
         cb = [keep.tile([P, PACK * B], U8, name="cb%d" % k, align_bytes=64) for k in range(PASSES)]
         cs = keep.tile([P, PASSES, PACK], F32, name="cs", align_bytes=64)
-        vw = [keep.tile([P, 2 * M], U8, name="vw%d" % g, align_bytes=64) for g in range(GROUPS)]
-        vs = keep.tile([P, GROUPS, M], U8, name="vs", align_bytes=64)
+        vw = [keep.tile([P, 2 * M], U8, name="vw%d" % g, align_bytes=256) for g in range(GROUPS)]
+        vs = keep.tile([P, GROUPS, M], U8, name="vs", align_bytes=256)
         ident = keep.tile([P, P], F32, name="ident", align_bytes=64)
 
         phi_v = phi.rearrange("(g p t) k -> g p t k", p=P, t=PACK)
@@ -105,8 +105,8 @@ def tile_bcs_gap_step_s13_kernel(tc, phi, coef_bytes, coef_scale, energy, v_word
         load_v(0, 2)
         load_v(2, GROUPS)
 
-        cc = keep.tile([P, PASSES, B], U32, name="cc", align_bytes=64)
-        csc = keep.tile([P, PASSES, B], U8, name="csc", align_bytes=64)
+        cc = keep.tile([P, PASSES, B], U32, name="cc", align_bytes=256)
+        csc = keep.tile([P, PASSES, B], U8, name="csc", align_bytes=256)
         wide = [keep.tile([P, PACK, B], BF16, name="wide%d" % k, align_bytes=64) for k in range(PASSES)]
         cgrp = [keep.tile([P, B, PACK], BF16, name="cgrp%d" % k, tag="cgrp%d" % k, align_bytes=64) for k in range(PASSES)]
 
@@ -129,8 +129,8 @@ def tile_bcs_gap_step_s13_kernel(tc, phi, coef_bytes, coef_scale, energy, v_word
         def coef_quant(k):
             nc.vector.quantize_mx(out=cc[:, k, :].bitcast(FP8X4), scales=csc[:, k, :], in_=cgrp[k][:].rearrange("p n t -> p (n t)"))
 
-        pc = [keep.tile([P, PACK, PASSES, P], U32, name="pc%d" % g, align_bytes=64) for g in range(GROUPS)]
-        psc = [keep.tile([P, PACK, PASSES, P], U8, name="psc%d" % g, align_bytes=64) for g in range(GROUPS)]
+        pc = [keep.tile([P, PACK, PASSES, P], U32, name="pc%d" % g, align_bytes=256) for g in range(GROUPS)]
+        psc = [keep.tile([P, PACK, PASSES, P], U8, name="psc%d" % g, align_bytes=256) for g in range(GROUPS)]
         turned = {}
         grouped = {}
 
@@ -192,8 +192,8 @@ def tile_bcs_gap_step_s13_kernel(tc, phi, coef_bytes, coef_scale, energy, v_word
             w = weight[g][:, :, c * NC : (c + 1) * NC]
             nc.vector.tensor_tensor(out=w, in0=w, in1=inv[u][:], op=MULT)
 
-        hc = [keep.tile([P, B], U32, name="hc%d" % g, align_bytes=64) for g in range(GROUPS)]
-        hs = [keep.tile([P, B], U8, name="hs%d" % g, align_bytes=64) for g in range(GROUPS)]
+        hc = [keep.tile([P, B], U32, name="hc%d" % g, align_bytes=256) for g in range(GROUPS)]
+        hs = [keep.tile([P, B], U8, name="hs%d" % g, align_bytes=256) for g in range(GROUPS)]
         gaps = {}
         hgrp = {}
 
@@ -266,7 +266,6 @@ def tile_bcs_gap_step_s13_kernel(tc, phi, coef_bytes, coef_scale, energy, v_word
             coef_interleave(k)
         for k in range(PASSES):
             coef_quant(k)
-        square_energy(nc.gpsimd, 2, 1, keep, "cgrp0")
         for j in range(WORK_BANKS):
             transposes(j)
         tanh(0, 0, 2)
@@ -278,6 +277,7 @@ def tile_bcs_gap_step_s13_kernel(tc, phi, coef_bytes, coef_scale, energy, v_word
         tanh(3)
         evacuate(2, False)
         evacuate(3, False)
+        square_energy(nc.vector, 2, 1, keep, "esq2")
         quant_phi(0)
         square_energy(nc.vector, 0, 2, keep, "esq")
         square_energy(nc.gpsimd, 1, 2, stage, "grp0")

@@ -163,6 +163,11 @@ def tile_bcs_gap_step_s13_kernel(tc, phi, coef_bytes, coef_scale, energy, v_word
                 in_=grouped[g][:].rearrange("p t x -> p (t x)"),
             )
 
+        def warm_up():
+            bank = bank_tile([P, B], 1)
+            for n in range(2):
+                nc.tensor.matmul(bank[:], lhsT=en[1][:, n, :P], rhs=en[1][:, n, :], start=True, stop=True)
+
         weight = [keep.tile([P, PACK, B], F32, name="weight%d" % g, align_bytes=64) for g in range(GROUPS)]
         squared = {}
         inv = {}
@@ -267,6 +272,8 @@ def tile_bcs_gap_step_s13_kernel(tc, phi, coef_bytes, coef_scale, energy, v_word
         for k in range(PASSES):
             coef_quant(k)
         for j in range(WORK_BANKS):
+            if j % PACK == 0:
+                warm_up()
             transposes(j)
         tanh(0, 0, 2)
         tanh(0, 2, PACK)

@@ -97,9 +97,11 @@ def tile_bcs_gap_step_s13_kernel(tc, phi, coef_bytes, coef_scale, energy, v_word
         load_energy(1)
         load_phi(0)
         load_phi(1)
-        load_energy(2)
+        load_energy(2, 0, 2)
+        load_energy(2, 2, PACK)
         load_phi(2)
-        load_energy(3)
+        load_energy(3, 0, 2)
+        load_energy(3, 2, PACK)
         for pair in range(3, TILES // 2):
             load_phi(pair)
         load_v(0, 2)
@@ -163,9 +165,9 @@ def tile_bcs_gap_step_s13_kernel(tc, phi, coef_bytes, coef_scale, energy, v_word
                 in_=grouped[g][:].rearrange("p t x -> p (t x)"),
             )
 
-        def warm_up():
+        def warm_up(count):
             bank = bank_tile([P, B], 1)
-            for n in range(2):
+            for n in range(count):
                 nc.tensor.matmul(bank[:], lhsT=en[1][:, n, :P], rhs=en[1][:, n, :], start=True, stop=True)
 
         weight = [keep.tile([P, PACK, B], F32, name="weight%d" % g, align_bytes=64) for g in range(GROUPS)]
@@ -273,15 +275,18 @@ def tile_bcs_gap_step_s13_kernel(tc, phi, coef_bytes, coef_scale, energy, v_word
             coef_quant(k)
         for j in range(WORK_BANKS):
             if j % PACK == 0:
-                warm_up()
+                warm_up(2)
             transposes(j)
+        warm_up(1)
         tanh(0, 0, 2)
         tanh(0, 2, PACK)
         tanh(1)
         evacuate(0, True)
         evacuate(1, True)
-        tanh(2)
-        tanh(3)
+        tanh(2, 0, 2)
+        tanh(2, 2, PACK)
+        tanh(3, 0, 2)
+        tanh(3, 2, PACK)
         evacuate(2, False)
         evacuate(3, False)
         square_energy(nc.vector, 2, 1, keep, "esq2")

@@ -21,28 +21,25 @@ P = 128
 PACK = 4
 GROUPS = M // (P * PACK)
 PASSES = R // (P * PACK)
-NC = 128
-CHUNKS = B // NC
-UNITS = GROUPS * CHUNKS
 TILES = M // P
 RUN = 4
 
+CHUNKS = ((0, 128), (128, 256), (384, 128))
 GAP_BANKS = 2
 WORK_BANKS = 6
-PART = 4
+BANKS = GAP_BANKS + WORK_BANKS
+BANK_COLS = 512
 LAST_PARTS = (4, 4, 2, 2, 2, 2)
-PASSES_A_STEP = 4
-AHEAD = (4, 5)
-FILL_STEPS = 7
+RING = (3, 4, 6, 7, 0, 1, 3, 2, 4, 5, 6, 7, 0, 1, 3, 2, 4, 5)
+TURN = (0, 1, 2, 3, 4, 5, 6, 7, 4, 5, 0, 1, 3, 4, 6, 7)
 
 
 def tile_bcs_gap_step_s13_kernel(tc, phi, coef_bytes, coef_scale, energy, v_words, v_scales, out):
     nc = tc.nc
-    order = sorted(((g, c) for g in range(GROUPS) for c in range(2)), key=lambda u: (u[0] + 2 * u[1], -u[1]))
-    order = order + [(g, c) for c in range(2, CHUNKS) for g in range(GROUPS)]
-    parts = [(c, i0, PART) for c in range(CHUNKS - 1) for i0 in range(0, TILES, PART)]
-    parts = parts + [(CHUNKS - 1, sum(LAST_PARTS[:n]), count) for n, count in enumerate(LAST_PARTS)]
-    first_of_last_chunk = len(parts) - len(LAST_PARTS)
+    parts = []
+    for c, (first, width) in enumerate(CHUNKS[:-1]):
+        parts.extend((c, i0, BANK_COLS // width) for i0 in range(0, TILES, BANK_COLS // width))
+    parts.extend((len(CHUNKS) - 1, sum(LAST_PARTS[:n]), count) for n, count in enumerate(LAST_PARTS))
 
     with ExitStack() as ctx:
         keep = ctx.enter_context(tc.tile_pool(name="keep", bufs=1))
@@ -65,7 +62,8 @@ def tile_bcs_gap_step_s13_kernel(tc, phi, coef_bytes, coef_scale, energy, v_word
         en_v = energy.rearrange("(g p t) n -> g p t n", p=P, t=PACK)
         cb_v = coef_bytes.rearrange("(k p t) n -> k p (t n)", p=P, t=PACK)
         cs_v = coef_scale.rearrange("(k p t) o -> p k (t o)", p=P, t=PACK)
-        out_v = out.rearrange("(i p) (c n) -> c p i n", p=P, n=NC)
+        vs_v = v_scales.rearrange("g (q r) n -> r q g n", r=4)
+        out_v = out.rearrange("(i p) n -> p i n", p=P)
 
         def load_coef(k):
             nc.sync.dma_start(out=cb[k][:], in_=cb_v[k])
@@ -77,50 +75,49 @@ def tile_bcs_gap_step_s13_kernel(tc, phi, coef_bytes, coef_scale, energy, v_word
             g, half = divmod(pair, 2)
             nc.sync.dma_start(out=ph[pair][:], in_=phi_v[g][:, 2 * half : 2 * half + 2, :])
 
-        def load_v(g0, g1):
-            for quad in range(4):
-                nc.sync.dma_start(
-                    out=vs[32 * quad : 32 * quad + 4, g0:g1, :].bitcast(I32),
-                    in_=v_scales[g0:g1, 4 * quad : 4 * quad + 4, :].rearrange("g r n -> r g n").bitcast(I32),
-                )
-            for g in range(g0, g1):
-                nc.sync.dma_start(out=vw[g][:], in_=v_words[g])
+        def load_scales(g0, g1):
+            for r in range(4):
+                nc.sync.dma_start(out=vs[r:P:32, g0:g1, :].bitcast(I32), in_=vs_v[r][:, g0:g1, :].bitcast(I32))
+
+        def load_words(g):
+            nc.sync.dma_start(out=vw[g][:], in_=v_words[g])
 
         make_identity(nc, ident[:])
         nc.vector.memset(vs[:].rearrange("p g n -> p (g n)").bitcast(I32), 0)
 
         nc.sync.dma_start(out=cs[:], in_=cs_v)
+        load_energy(0, 0, 1)
         load_coef(0)
-        load_energy(0, 0, 2)
         load_coef(1)
-        load_energy(0, 2, PACK)
-        load_energy(1)
-        load_phi(0)
-        load_phi(1)
-        load_energy(2, 0, 2)
-        load_energy(2, 2, PACK)
-        load_phi(2)
-        load_energy(3, 0, 2)
-        load_energy(3, 2, PACK)
-        for pair in range(3, TILES // 2):
+        for pair in range(4):
             load_phi(pair)
-        load_v(0, 2)
-        load_v(2, GROUPS)
+        load_energy(0, 1, PACK)
+        load_energy(1)
+        load_phi(4)
+        load_energy(2)
+        load_phi(5)
+        load_energy(3)
+        load_phi(6)
+        load_phi(7)
+        load_scales(0, 2)
+        load_words(0)
+        load_words(1)
+        load_scales(2, 4)
+        load_words(2)
+        load_words(3)
 
         cc = keep.tile([P, PASSES, B], U32, name="cc", align_bytes=256)
         csc = keep.tile([P, PASSES, B], U8, name="csc", align_bytes=256)
-        wide = [keep.tile([P, PACK, B], BF16, name="wide%d" % k, align_bytes=64) for k in range(PASSES)]
-        cgrp = [keep.tile([P, B, PACK], BF16, name="cgrp%d" % k, tag="cgrp%d" % k, align_bytes=64) for k in range(PASSES)]
+        wide = [stage.tile([P, PACK, B], BF16, name="wide", tag="wide", bufs=4, align_bytes=64) for k in range(PASSES)]
+        cgrp = [stage.tile([P, B, PACK], BF16, name="cgrp", tag="wide", bufs=4, align_bytes=64) for k in range(PASSES)]
 
-        def coef_widen(k):
-            for t in range(PACK):
-                nc.vector.tensor_scalar(
-                    out=wide[k][:, t, :],
-                    in0=cb[k][:, t * B : (t + 1) * B].bitcast(FP8),
-                    scalar1=cs[:, k, t : t + 1],
-                    scalar2=None,
-                    op0=MULT,
-                )
+        def coef_widen(k, t0=0, t1=PACK, on_scalar=False):
+            for t in range(t0, t1):
+                codes = cb[k][:, t * B : (t + 1) * B].bitcast(FP8)
+                if on_scalar:
+                    nc.scalar.activation(out=wide[k][:, t, :], in_=codes, func=ACT.Copy, scale=cs[:, k, t : t + 1])
+                else:
+                    nc.vector.tensor_scalar(out=wide[k][:, t, :], in0=codes, scalar1=cs[:, k, t : t + 1], scalar2=None, op0=MULT)
 
         def coef_interleave(k):
             nc.vector.tensor_copy(
@@ -137,7 +134,7 @@ def tile_bcs_gap_step_s13_kernel(tc, phi, coef_bytes, coef_scale, energy, v_word
         grouped = {}
 
         def turn_bank(j):
-            return GAP_BANKS + (j + PART) % WORK_BANKS
+            return TURN[j]
 
         def transposes(j):
             bank = bank_tile([P, PASSES, 2, P], turn_bank(j))
@@ -158,60 +155,74 @@ def tile_bcs_gap_step_s13_kernel(tc, phi, coef_bytes, coef_scale, energy, v_word
             else:
                 nc.vector.tensor_copy(out=dst, in_=src)
 
-        def quant_phi(g):
+        def quant_phi(g, t0=0, t1=PACK):
             nc.vector.quantize_mx(
-                out=pc[g][:].rearrange("p t k r -> p (t k r)").bitcast(FP8X4),
-                scales=psc[g][:].rearrange("p t k r -> p (t k r)"),
-                in_=grouped[g][:].rearrange("p t x -> p (t x)"),
+                out=pc[g][:, t0:t1].rearrange("p t k r -> p (t k r)").bitcast(FP8X4),
+                scales=psc[g][:, t0:t1].rearrange("p t k r -> p (t k r)"),
+                in_=grouped[g][:, t0:t1].rearrange("p t x -> p (t x)"),
             )
 
-        def warm_up(count):
-            bank = bank_tile([P, B], 1)
-            for n in range(count):
-                nc.tensor.matmul(bank[:], lhsT=en[1][:, n, :P], rhs=en[1][:, n, :], start=True, stop=True)
-
-        weight = [keep.tile([P, PACK, B], F32, name="weight%d" % g, align_bytes=64) for g in range(GROUPS)]
+        num = [keep.tile([P, B // RUN, PACK, RUN], F32, name="num%d" % g, align_bytes=64) for g in range(GROUPS)]
         squared = {}
         inv = {}
 
+        def energies(g, c):
+            first, width = CHUNKS[c]
+            return en[g][:, :, first : first + width].rearrange("p t (c i) -> p t c i", i=RUN)
+
         def tanh(g, t0=0, t1=PACK):
-            nc.scalar.activation(out=weight[g][:, t0:t1, :], in_=en[g][:, t0:t1, :], func=ACT.Tanh)
+            nc.scalar.activation(
+                out=num[g][:, :, t0:t1, :].rearrange("p c t i -> p t c i"),
+                in_=en[g][:, t0:t1, :].rearrange("p t (c i) -> p t c i", i=RUN),
+                func=ACT.Tanh,
+            )
 
-        def square_energy(eng, g, chunks, pool, tag):
-            width = chunks * NC
-            esq = pool.tile([P, PACK, width], F32, name="esq", tag=tag, bufs=1, align_bytes=64)
-            eng.tensor_tensor(out=esq[:], in0=en[g][:, :, :width], in1=en[g][:, :, :width], op=MULT)
-            for c in range(chunks):
-                squared[g, c] = esq[:, :, c * NC : (c + 1) * NC]
+        def new_inv(g, c):
+            width = CHUNKS[c][1]
+            inv[g, c] = stage.tile([P, width // RUN, PACK, RUN], F32, name="inv", tag="wide" if width > P else "inv", bufs=4, align_bytes=64)
+            return inv[g, c]
 
-        def inv_sqrt(u):
-            g, c = order[u]
-            inv[u] = stage.tile([P, PACK, NC], F32, name="inv", tag="inv", bufs=6, align_bytes=64)
-            src = squared[g, c] if (g, c) in squared else en[g][:, :, c * NC : (c + 1) * NC]
-            nc.scalar.activation(out=inv[u][:], in_=src, func=ACT.Abs_reciprocal_sqrt)
+        def square_energy(eng, g, c):
+            esq = inv[g, c] if (g, c) in inv else new_inv(g, c)
+            eng.tensor_tensor(out=esq[:].rearrange("p c t i -> p t c i"), in0=energies(g, c), in1=energies(g, c), op=MULT)
+            squared[g, c] = esq
 
-        def square_root(u):
-            if order[u] not in squared:
-                nc.scalar.activation(out=inv[u][:], in_=inv[u][:], func=ACT.Square)
+        def square_aside(slot, units):
+            room = stage.tile([P, B // RUN, PACK, RUN], F32, name="esq", tag="grp%d" % slot, bufs=1, align_bytes=64)
+            used = 0
+            for g, c in units:
+                runs = CHUNKS[c][1] // RUN
+                inv[g, c] = room[:, used : used + runs]
+                used = used + runs
+                square_energy(nc.gpsimd, g, c)
 
-        def divide(u):
-            g, c = order[u]
-            w = weight[g][:, :, c * NC : (c + 1) * NC]
-            nc.vector.tensor_tensor(out=w, in0=w, in1=inv[u][:], op=MULT)
+        def inv_sqrt(g, c):
+            if (g, c) in squared:
+                nc.scalar.activation(out=inv[g, c][:], in_=inv[g, c][:], func=ACT.Abs_reciprocal_sqrt)
+            else:
+                root = new_inv(g, c)
+                nc.scalar.activation(out=root[:].rearrange("p c t i -> p t c i"), in_=energies(g, c), func=ACT.Abs_reciprocal_sqrt)
+
+        def square_root(g, c, on_scalar=True):
+            if on_scalar:
+                nc.scalar.activation(out=inv[g, c][:], in_=inv[g, c][:], func=ACT.Square)
+            else:
+                nc.vector.tensor_tensor(out=inv[g, c][:], in0=inv[g, c][:], in1=inv[g, c][:], op=MULT)
 
         hc = [keep.tile([P, B], U32, name="hc%d" % g, align_bytes=256) for g in range(GROUPS)]
         hs = [keep.tile([P, B], U8, name="hs%d" % g, align_bytes=256) for g in range(GROUPS)]
         gaps = {}
         hgrp = {}
 
-        def first_product(u):
-            g, c = order[u]
-            bank = bank_tile([P, PACK, NC], u % GAP_BANKS)
-            cols = slice(c * NC, (c + 1) * NC)
-            for t in range(PACK):
+        def first_product(g, n, first=0, width=B, at=None):
+            count = BANK_COLS // width
+            bank = bank_tile([P, count, width], len(gaps) % GAP_BANKS if at is None else at)
+            cols = slice(first, first + width)
+            for i in range(count):
+                t = n * count + i
                 for k in range(PASSES):
                     nc.tensor.matmul_mx(
-                        out=bank[:, t, :],
+                        out=bank[:, i, :],
                         lhsT=pc[g][:, t, k, :].bitcast(FP8X4),
                         lhsT_scale=psc[g][:, t, k, :],
                         rhs=cc[:, k, cols].bitcast(FP8X4),
@@ -219,33 +230,39 @@ def tile_bcs_gap_step_s13_kernel(tc, phi, coef_bytes, coef_scale, energy, v_word
                         start=(k == 0),
                         stop=(k == PASSES - 1),
                     )
-            gaps[u] = bank
+            gaps[g, n, first] = bank
 
-        def make_h(u):
-            g, c = order[u]
-            hgrp[u] = stage.tile([P, NC, PACK], BF16, name="hg", tag="hg", bufs=3, align_bytes=64)
+        def times_gap(g, n, first=0, width=B):
+            count = BANK_COLS // width
+            w = num[g][:, first // RUN : (first + width) // RUN, n * count : (n + 1) * count, :].rearrange("p c t i -> p t c i")
+            nc.vector.tensor_tensor(out=w, in0=gaps[g, n, first][:].rearrange("p t (c i) -> p t c i", i=RUN), in1=w, op=MULT)
+
+        def make_h(g, c):
+            first, width = CHUNKS[c]
+            hgrp[g, c] = stage.tile([P, width, PACK], BF16, name="hg", tag="hg", bufs=3, align_bytes=64)
             nc.vector.tensor_tensor(
-                out=hgrp[u][:].rearrange("p (c i) t -> p c t i", i=RUN),
-                in0=gaps[u][:].rearrange("p t (c i) -> p c t i", i=RUN),
-                in1=weight[g][:, :, c * NC : (c + 1) * NC].rearrange("p t (c i) -> p c t i", i=RUN),
+                out=hgrp[g, c][:].rearrange("p (c i) t -> p c t i", i=RUN),
+                in0=num[g][:, first // RUN : (first + width) // RUN],
+                in1=inv[g, c][:],
                 op=MULT,
             )
 
-        def quant_h(u):
-            g, c = order[u]
-            cols = slice(c * NC, (c + 1) * NC)
-            nc.vector.quantize_mx(out=hc[g][:, cols].bitcast(FP8X4), scales=hs[g][:, cols], in_=hgrp[u][:].rearrange("p n t -> p (n t)"))
+        def quant_h(g, c):
+            first, width = CHUNKS[c]
+            cols = slice(first, first + width)
+            nc.vector.quantize_mx(out=hc[g][:, cols].bitcast(FP8X4), scales=hs[g][:, cols], in_=hgrp[g, c][:].rearrange("p n t -> p (n t)"))
 
         sums = {}
 
         def part_bank(n):
-            return turn_bank(TILES - WORK_BANKS + n)
+            return RING[n]
 
         def part_pass(n, g):
             c, i0, count = parts[n]
+            first, width = CHUNKS[c]
             if g == 0:
-                sums[n] = bank_tile([P, count, NC], part_bank(n))
-            cols = slice(c * NC, (c + 1) * NC)
+                sums[n] = bank_tile([P, count, width], part_bank(n))
+            cols = slice(first, first + width)
             for i in range(count):
                 tile_i = i0 + i
                 nc.tensor.matmul_mx(
@@ -258,102 +275,149 @@ def tile_bcs_gap_step_s13_kernel(tc, phi, coef_bytes, coef_scale, energy, v_word
                     stop=(g == GROUPS - 1 and i == count - 1),
                 )
 
+        def passes(n0, n1, g0, g1):
+            for n in range(n0, n1):
+                for g in range(g0, g1):
+                    part_pass(n, g)
+
         def store(n, on_scalar):
             c, i0, count = parts[n]
-            o = stage.tile([P, count, NC], F32, name="o", tag="o", bufs=6, align_bytes=64)
+            first, width = CHUNKS[c]
+            o = stage.tile([P, count, width], F32, name="o", tag="o", bufs=8, align_bytes=64)
             if on_scalar:
                 nc.scalar.copy(out=o[:], in_=sums[n][:])
             else:
                 nc.vector.tensor_copy(out=o[:], in_=sums[n][:])
-            nc.sync.dma_start(out=out_v[c][:, i0 : i0 + count, :], in_=o[:])
+            nc.sync.dma_start(out=out_v[:, i0 : i0 + count, first : first + width], in_=o[:])
 
+        tanh(0, 0, 1)
         for k in range(PASSES):
-            coef_widen(k)
+            coef_widen(k, 0, 2)
+            coef_widen(k, 2, 4, True)
         for k in range(PASSES):
             coef_interleave(k)
         for k in range(PASSES):
             coef_quant(k)
-        for j in range(WORK_BANKS):
-            if j % PACK == 0:
-                warm_up(2)
+        for j in range(8):
             transposes(j)
-        warm_up(1)
-        tanh(0, 0, 2)
+        for j in range(6):
+            evacuate(j, True)
+        tanh(0, 1, 2)
         tanh(0, 2, PACK)
         tanh(1)
-        evacuate(0, True)
-        evacuate(1, True)
-        tanh(2, 0, 2)
-        tanh(2, 2, PACK)
-        tanh(3, 0, 2)
-        tanh(3, 2, PACK)
-        evacuate(2, False)
-        evacuate(3, False)
-        square_energy(nc.vector, 2, 1, keep, "esq2")
-        quant_phi(0)
-        square_energy(nc.vector, 0, 2, keep, "esq")
-        square_energy(nc.gpsimd, 1, 2, stage, "grp0")
-        first_product(0)
-        for j in range(WORK_BANKS, WORK_BANKS + PACK):
-            transposes(j)
-        for j in range(PACK, 2 * PACK):
-            evacuate(j, False)
+        tanh(2)
+        tanh(3)
+        quant_phi(0, 0, 2)
+        quant_phi(0, 2, 4)
+        evacuate(6, False)
+        evacuate(7, False)
+        for t in range(PACK):
+            first_product(0, t, at=t)
         quant_phi(1)
-        for j in range(WORK_BANKS + PACK, WORK_BANKS + 2 * PACK):
-            transposes(j)
-        first_product(1)
-        inv_sqrt(0)
-        inv_sqrt(1)
-        inv_sqrt(2)
-        divide(0)
-
-        todo = [(n, g) for n in range(len(parts)) for g in range(GROUPS)]
-        full = []
-        stored = []
-        emptied = 2 * PACK
-        roots = 3
-        for u in range(UNITS + 1):
-            for n in full:
-                store(n, True)
-                stored.append(n)
-            full = []
-            for j in range(emptied, min(emptied + (PACK if u == 0 else 2), TILES)):
-                evacuate(j, True)
-                emptied = j + 1
-                if j + WORK_BANKS < TILES:
-                    transposes(j + WORK_BANKS)
-            for ahead in range(2 if u in AHEAD else 1):
-                if roots < UNITS:
-                    inv_sqrt(roots)
-                if roots - 1 < UNITS:
-                    square_root(roots - 1)
-                roots = roots + 1
-            after_phi = u in (2, 4)
-            if after_phi:
-                quant_h(u - 1)
-            if u + 1 < UNITS:
-                divide(u + 1)
-            if u > 0 and not after_phi:
-                quant_h(u - 1)
-            if u < UNITS:
-                make_h(u)
-            if u in (1, 3):
-                quant_phi(2 + u // 2)
-            if FILL_STEPS <= u < UNITS - 2:
-                first_product(u + 2)
-            left = PASSES_A_STEP if FILL_STEPS <= u < UNITS else len(todo)
-            for n, g in list(todo):
-                has_h = order.index((g, parts[n][0])) < u
-                has_bank = emptied > TILES - WORK_BANKS + n if n < WORK_BANKS else n - WORK_BANKS in stored
-                in_turn = n <= first_of_last_chunk or (n - 1, GROUPS - 1) not in todo
-                if left and has_h and has_bank and in_turn and (n, g - 1) not in todo:
-                    part_pass(n, g)
-                    todo.remove((n, g))
-                    left = left - 1
-                    if g == GROUPS - 1 and u == UNITS:
-                        store(n, n % 2 == 0)
-                        stored.append(n)
-                    elif g == GROUPS - 1:
-                        full.append(n)
-            if u < FILL_STEPS:
-                first_product(u + 2)
+        square_aside(1, [(0, 0), (1, 0), (2, 0), (3, 0)])
+        transposes(8)
+        transposes(9)
+        first_product(1, 0, at=6)
+        first_product(1, 1, at=7)
+        for t in range(PACK):
+            times_gap(0, t)
+        transposes(10)
+        transposes(11)
+        first_product(1, 2, at=2)
+        evacuate(8, False)
+        evacuate(9, False)
+        times_gap(1, 0)
+        times_gap(1, 1)
+        transposes(12)
+        transposes(13)
+        first_product(1, 3, at=5)
+        transposes(14)
+        transposes(15)
+        evacuate(10, False)
+        evacuate(11, False)
+        quant_phi(2)
+        square_aside(2, [(0, 2)])
+        first_product(2, 0, 0, 128, at=0)
+        first_product(2, 0, 128, 256, at=1)
+        times_gap(1, 2)
+        times_gap(1, 3)
+        evacuate(12, False)
+        first_product(2, 1, 128, 256, at=2)
+        first_product(2, 0, 384, 128, at=5)
+        inv_sqrt(0, 0)
+        inv_sqrt(1, 0)
+        for j in range(13, 16):
+            evacuate(j, True)
+        inv_sqrt(2, 0)
+        inv_sqrt(3, 0)
+        make_h(0, 0)
+        make_h(1, 0)
+        quant_h(0, 0)
+        times_gap(2, 0, 0, 128)
+        quant_h(1, 0)
+        quant_phi(3)
+        passes(0, 4, 0, 1)
+        passes(0, 2, 1, 2)
+        first_product(3, 0, 0, 128, at=0)
+        passes(2, 4, 1, 2)
+        make_h(2, 0)
+        times_gap(2, 0, 128, 256)
+        quant_h(2, 0)
+        times_gap(3, 0, 0, 128)
+        times_gap(2, 1, 128, 256)
+        make_h(3, 0)
+        times_gap(2, 0, 384, 128)
+        quant_h(3, 0)
+        passes(0, 4, 2, 3)
+        first_product(3, 0, 128, 256, at=1)
+        first_product(3, 1, 128, 256, at=2)
+        passes(0, 4, 3, 4)
+        first_product(3, 0, 384, 128, at=5)
+        inv_sqrt(0, 1)
+        inv_sqrt(1, 1)
+        square_root(0, 1)
+        inv_sqrt(2, 1)
+        square_root(1, 1)
+        square_root(2, 1)
+        store(0, True)
+        inv_sqrt(3, 1)
+        store(1, True)
+        square_root(3, 1)
+        store(2, True)
+        store(3, True)
+        make_h(0, 1)
+        times_gap(3, 0, 128, 256)
+        quant_h(0, 1)
+        make_h(1, 1)
+        times_gap(3, 1, 128, 256)
+        quant_h(1, 1)
+        passes(4, 8, 0, 1)
+        passes(4, 8, 1, 2)
+        passes(8, 9, 0, 2)
+        make_h(2, 1)
+        times_gap(3, 0, 384, 128)
+        quant_h(2, 1)
+        passes(9, 10, 0, 2)
+        passes(4, 10, 2, 3)
+        for g in range(4):
+            inv_sqrt(g, 2)
+        make_h(3, 1)
+        quant_h(3, 1)
+        make_h(0, 2)
+        passes(4, 10, 3, 4)
+        passes(10, 12, 0, 4)
+        square_root(1, 2, False)
+        quant_h(0, 2)
+        square_root(2, 2, False)
+        make_h(1, 2)
+        square_root(3, 2, False)
+        quant_h(1, 2)
+        make_h(2, 2)
+        make_h(3, 2)
+        quant_h(2, 2)
+        quant_h(3, 2)
+        for n in range(4, 12):
+            store(n, True)
+        for n in range(12, 18):
+            passes(n, n + 1, 0, 4)
+            store(n, n % 2 == 1)

@@ -50,7 +50,8 @@ def tile_bcs_gap_step_s13_kernel(tc, phi, coef_bytes, coef_scale, energy, v_word
         def bank_tile(shape, bank):
             return psum.tile(shape, F32, name="bank", tag="bank%d" % bank, bufs=1)
 
-        en = [keep.tile([P, PACK, B], BF16, name="en%d" % g, align_bytes=64) for g in range(GROUPS)]
+        en_all = keep.tile([P, GROUPS * PACK, B], BF16, name="en", align_bytes=64)
+        en = [en_all[:, PACK * g : PACK * (g + 1), :] for g in range(GROUPS)]
         ph = [keep.tile([P, 2, R], BF16, name="ph%d" % j, align_bytes=64) for j in range(TILES // 2)]
         cb = [keep.tile([P, PACK * B], U8, name="cb%d" % k, align_bytes=64) for k in range(PASSES)]
         cs = keep.tile([P, PASSES, PACK], F32, name="cs", align_bytes=64)
@@ -182,26 +183,17 @@ def tile_bcs_gap_step_s13_kernel(tc, phi, coef_bytes, coef_scale, energy, v_word
             inv[g, c] = stage.tile([P, width // RUN, PACK, RUN], F32, name="inv", tag="wide" if width > P else "inv", bufs=4, align_bytes=64)
             return inv[g, c]
 
-        def square_energy(eng, g, c):
-            esq = inv[g, c] if (g, c) in inv else new_inv(g, c)
-            eng.tensor_tensor(out=esq[:].rearrange("p c t i -> p t c i"), in0=energies(g, c), in1=energies(g, c), op=MULT)
-            squared[g, c] = esq
-
-        def square_aside(slot, units):
-            room = stage.tile([P, B // RUN, PACK, RUN], F32, name="esq", tag="grp%d" % slot, bufs=1, align_bytes=64)
-            used = 0
-            for g, c in units:
-                runs = CHUNKS[c][1] // RUN
-                inv[g, c] = room[:, used : used + runs]
-                used = used + runs
-                square_energy(nc.gpsimd, g, c)
+        def square_aside(slot, g0, g1, c):
+            first, width = CHUNKS[c]
+            esq = stage.tile([P, (g1 - g0) * PACK, width], F32, name="esq", tag="grp%d" % slot, bufs=1, align_bytes=64)
+            src = en_all[:, PACK * g0 : PACK * g1, first : first + width]
+            nc.gpsimd.tensor_tensor(out=esq[:], in0=src, in1=src, op=MULT)
+            for g in range(g0, g1):
+                squared[g, c] = esq[:, PACK * (g - g0) : PACK * (g - g0 + 1), :].rearrange("p t (c i) -> p t c i", i=RUN)
 
         def inv_sqrt(g, c):
-            if (g, c) in squared:
-                nc.scalar.activation(out=inv[g, c][:], in_=inv[g, c][:], func=ACT.Abs_reciprocal_sqrt)
-            else:
-                root = new_inv(g, c)
-                nc.scalar.activation(out=root[:].rearrange("p c t i -> p t c i"), in_=energies(g, c), func=ACT.Abs_reciprocal_sqrt)
+            src = squared[g, c] if (g, c) in squared else energies(g, c)
+            nc.scalar.activation(out=new_inv(g, c)[:].rearrange("p c t i -> p t c i"), in_=src, func=ACT.Abs_reciprocal_sqrt)
 
         def square_root(g, c, on_scalar=True):
             if on_scalar:
@@ -314,7 +306,7 @@ def tile_bcs_gap_step_s13_kernel(tc, phi, coef_bytes, coef_scale, energy, v_word
         for t in range(PACK):
             first_product(0, t, at=t)
         quant_phi(1)
-        square_aside(1, [(0, 0), (1, 0), (2, 0), (3, 0)])
+        square_aside(1, 0, 3, 0)
         transposes(8)
         transposes(9)
         first_product(1, 0, at=6)
@@ -336,17 +328,18 @@ def tile_bcs_gap_step_s13_kernel(tc, phi, coef_bytes, coef_scale, energy, v_word
         evacuate(10, False)
         evacuate(11, False)
         quant_phi(2)
-        square_aside(2, [(0, 2)])
+        square_aside(2, 3, 4, 0)
         first_product(2, 0, 0, 128, at=0)
         first_product(2, 0, 128, 256, at=1)
         times_gap(1, 2)
         times_gap(1, 3)
         evacuate(12, False)
+        evacuate(13, False)
         first_product(2, 1, 128, 256, at=2)
         first_product(2, 0, 384, 128, at=5)
         inv_sqrt(0, 0)
         inv_sqrt(1, 0)
-        for j in range(13, 16):
+        for j in range(14, 16):
             evacuate(j, True)
         inv_sqrt(2, 0)
         inv_sqrt(3, 0)
@@ -403,12 +396,13 @@ def tile_bcs_gap_step_s13_kernel(tc, phi, coef_bytes, coef_scale, energy, v_word
             inv_sqrt(g, 2)
         make_h(3, 1)
         quant_h(3, 1)
+        square_root(0, 2, False)
+        square_root(1, 2, False)
         make_h(0, 2)
         passes(4, 10, 3, 4)
         passes(10, 12, 0, 4)
-        square_root(1, 2, False)
-        quant_h(0, 2)
         square_root(2, 2, False)
+        quant_h(0, 2)
         make_h(1, 2)
         square_root(3, 2, False)
         quant_h(1, 2)

@@ -24,14 +24,14 @@ PASSES = R // (P * PACK)
 TILES = M // P
 RUN = 4
 
-CHUNKS = ((0, 128), (128, 256), (384, 128))
+CHUNKS = ((0, 128), (128, 128), (256, 128), (384, 128))
 GAP_BANKS = 2
 WORK_BANKS = 6
 BANKS = GAP_BANKS + WORK_BANKS
 BANK_COLS = 512
 LAST_PARTS = (4, 4, 2, 2, 2, 2)
-RING = (3, 4, 6, 7, 0, 1, 3, 2, 4, 5, 6, 7, 0, 1, 3, 2, 4, 5)
-TURN = (0, 1, 2, 3, 4, 5, 6, 7, 4, 5, 0, 1, 3, 4, 6, 7)
+RING = (3, 4, 6, 7, 5, 2, 1, 0, 4, 6, 7, 3, 5, 2, 1, 0, 4, 6)
+TURN = (0, 1, 2, 3, 4, 5, 6, 7, 6, 7, 0, 1, 3, 4, 6, 7)
 
 
 def tile_bcs_gap_step_s13_kernel(tc, phi, coef_bytes, coef_scale, energy, v_words, v_scales, out):
@@ -66,8 +66,8 @@ def tile_bcs_gap_step_s13_kernel(tc, phi, coef_bytes, coef_scale, energy, v_word
         vs_v = v_scales.rearrange("g (q r) n -> r q g n", r=4)
         out_v = out.rearrange("(i p) n -> p i n", p=P)
 
-        def load_coef(k):
-            nc.sync.dma_start(out=cb[k][:], in_=cb_v[k])
+        def load_coef(k, t0=0, t1=PACK):
+            nc.sync.dma_start(out=cb[k][:, t0 * B : t1 * B], in_=cb_v[k][:, t0 * B : t1 * B])
 
         def load_energy(g, t0=0, t1=PACK):
             nc.sync.dma_start(out=en[g][:, t0:t1, :], in_=en_v[g][:, t0:t1, :])
@@ -163,46 +163,64 @@ def tile_bcs_gap_step_s13_kernel(tc, phi, coef_bytes, coef_scale, energy, v_word
                 in_=grouped[g][:, t0:t1].rearrange("p t x -> p (t x)"),
             )
 
-        num = [keep.tile([P, B // RUN, PACK, RUN], F32, name="num%d" % g, align_bytes=64) for g in range(GROUPS)]
+        num = keep.tile([P, GROUPS, B // RUN, PACK, RUN], F32, name="num", align_bytes=64)
         squared = {}
+        rooms = {}
         inv = {}
-
-        def energies(g, c):
-            first, width = CHUNKS[c]
-            return en[g][:, :, first : first + width].rearrange("p t (c i) -> p t c i", i=RUN)
 
         def tanh(g, t0=0, t1=PACK):
             nc.scalar.activation(
-                out=num[g][:, :, t0:t1, :].rearrange("p c t i -> p t c i"),
+                out=num[:, g, :, t0:t1, :].rearrange("p c t i -> p t c i"),
                 in_=en[g][:, t0:t1, :].rearrange("p t (c i) -> p t c i", i=RUN),
                 func=ACT.Tanh,
             )
 
-        def new_inv(g, c):
-            width = CHUNKS[c][1]
-            inv[g, c] = stage.tile([P, width // RUN, PACK, RUN], F32, name="inv", tag="wide" if width > P else "inv", bufs=4, align_bytes=64)
-            return inv[g, c]
-
-        def square_aside(slot, g0, g1, c):
+        def square_aside(tag, g0, g1, c, part=0):
+            if part == 0:
+                rooms[tag] = stage.tile([P, PACK * B], F32, name="esq", tag=tag, bufs=1, align_bytes=64)
             first, width = CHUNKS[c]
-            esq = stage.tile([P, (g1 - g0) * PACK, width], F32, name="esq", tag="grp%d" % slot, bufs=1, align_bytes=64)
+            size = (g1 - g0) * PACK * width
+            esq = rooms[tag][:, part * size : (part + 1) * size].rearrange("p (r n) -> p r n", n=width)
             src = en_all[:, PACK * g0 : PACK * g1, first : first + width]
-            nc.gpsimd.tensor_tensor(out=esq[:], in0=src, in1=src, op=MULT)
+            nc.gpsimd.tensor_tensor(out=esq, in0=src, in1=src, op=MULT)
             for g in range(g0, g1):
-                squared[g, c] = esq[:, PACK * (g - g0) : PACK * (g - g0 + 1), :].rearrange("p t (c i) -> p t c i", i=RUN)
+                squared[g, c] = (esq, g0)
 
-        def inv_sqrt(g, c):
-            src = squared[g, c] if (g, c) in squared else energies(g, c)
-            nc.scalar.activation(out=new_inv(g, c)[:].rearrange("p c t i -> p t c i"), in_=src, func=ACT.Abs_reciprocal_sqrt)
+        def new_inv(g0, g1, c):
+            width = CHUNKS[c][1]
+            tag = "wide" if (g1 - g0) * width > P else "inv"
+            room = stage.tile([P, g1 - g0, width // RUN, PACK, RUN], F32, name="inv", tag=tag, bufs=4, align_bytes=64)
+            for g in range(g0, g1):
+                inv[g, c] = (room, g0)
 
-        def square_root(g, c, on_scalar=True):
-            if on_scalar:
-                nc.scalar.activation(out=inv[g, c][:], in_=inv[g, c][:], func=ACT.Square)
+        def inv_of(g0, g1, c):
+            room, base = inv[g0, c]
+            return room[:, g0 - base : g1 - base]
+
+        def inv_sqrt(g0, g1, c):
+            first, width = CHUNKS[c]
+            if (g0, c) not in inv:
+                new_inv(g0, g1, c)
+            if (g0, c) in squared:
+                esq, base = squared[g0, c]
+                src = esq[:, PACK * (g0 - base) : PACK * (g1 - base), :]
             else:
-                nc.vector.tensor_tensor(out=inv[g, c][:], in0=inv[g, c][:], in1=inv[g, c][:], op=MULT)
+                src = en_all[:, PACK * g0 : PACK * g1, first : first + width]
+            nc.scalar.activation(
+                out=inv_of(g0, g1, c).rearrange("p g c t i -> p t g c i"),
+                in_=src.rearrange("p (g t) (c i) -> p t g c i", t=PACK, i=RUN),
+                func=ACT.Abs_reciprocal_sqrt,
+            )
 
-        hc = [keep.tile([P, B], U32, name="hc%d" % g, align_bytes=256) for g in range(GROUPS)]
-        hs = [keep.tile([P, B], U8, name="hs%d" % g, align_bytes=256) for g in range(GROUPS)]
+        def square_root(g0, g1, c, on_scalar=True):
+            root = inv_of(g0, g1, c).rearrange("p g c t i -> p (g c t i)")
+            if on_scalar:
+                nc.scalar.activation(out=root, in_=root, func=ACT.Square)
+            else:
+                nc.vector.tensor_tensor(out=root, in0=root, in1=root, op=MULT)
+
+        hc = [keep.tile([P, GROUPS, width], U32, name="hc%d" % c, align_bytes=256) for c, (first, width) in enumerate(CHUNKS)]
+        hs = [keep.tile([P, GROUPS, width], U8, name="hs%d" % c, align_bytes=256) for c, (first, width) in enumerate(CHUNKS)]
         gaps = {}
         hgrp = {}
 
@@ -226,23 +244,25 @@ def tile_bcs_gap_step_s13_kernel(tc, phi, coef_bytes, coef_scale, energy, v_word
 
         def times_gap(g, n, first=0, width=B):
             count = BANK_COLS // width
-            w = num[g][:, first // RUN : (first + width) // RUN, n * count : (n + 1) * count, :].rearrange("p c t i -> p t c i")
+            w = num[:, g, first // RUN : (first + width) // RUN, n * count : (n + 1) * count, :].rearrange("p c t i -> p t c i")
             nc.vector.tensor_tensor(out=w, in0=gaps[g, n, first][:].rearrange("p t (c i) -> p t c i", i=RUN), in1=w, op=MULT)
 
-        def make_h(g, c):
+        def make_h(g0, g1, c):
             first, width = CHUNKS[c]
-            hgrp[g, c] = stage.tile([P, width, PACK], BF16, name="hg", tag="hg", bufs=3, align_bytes=64)
+            hgrp[g0, c] = stage.tile([P, g1 - g0, width, PACK], BF16, name="hg", tag="hg", bufs=3, align_bytes=64)
             nc.vector.tensor_tensor(
-                out=hgrp[g, c][:].rearrange("p (c i) t -> p c t i", i=RUN),
-                in0=num[g][:, first // RUN : (first + width) // RUN],
-                in1=inv[g, c][:],
+                out=hgrp[g0, c][:].rearrange("p g (c i) t -> p g c t i", i=RUN),
+                in0=num[:, g0:g1, first // RUN : (first + width) // RUN],
+                in1=inv_of(g0, g1, c),
                 op=MULT,
             )
 
-        def quant_h(g, c):
-            first, width = CHUNKS[c]
-            cols = slice(first, first + width)
-            nc.vector.quantize_mx(out=hc[g][:, cols].bitcast(FP8X4), scales=hs[g][:, cols], in_=hgrp[g, c][:].rearrange("p n t -> p (n t)"))
+        def quant_h(g0, g1, c):
+            nc.vector.quantize_mx(
+                out=hc[c][:, g0:g1, :].rearrange("p g n -> p (g n)").bitcast(FP8X4),
+                scales=hs[c][:, g0:g1, :].rearrange("p g n -> p (g n)"),
+                in_=hgrp[g0, c][:].rearrange("p g n t -> p (g n t)"),
+            )
 
         sums = {}
 
@@ -251,18 +271,16 @@ def tile_bcs_gap_step_s13_kernel(tc, phi, coef_bytes, coef_scale, energy, v_word
 
         def part_pass(n, g):
             c, i0, count = parts[n]
-            first, width = CHUNKS[c]
             if g == 0:
-                sums[n] = bank_tile([P, count, width], part_bank(n))
-            cols = slice(first, first + width)
+                sums[n] = bank_tile([P, count, CHUNKS[c][1]], part_bank(n))
             for i in range(count):
                 tile_i = i0 + i
                 nc.tensor.matmul_mx(
                     out=sums[n][:, i, :],
                     lhsT=vw[g][:, 2 * P * tile_i : 2 * P * (tile_i + 1)].bitcast(FP4X4),
                     lhsT_scale=vs[:, g, P * tile_i : P * (tile_i + 1)],
-                    rhs=hc[g][:, cols].bitcast(FP8X4),
-                    rhs_scale=hs[g][:, cols],
+                    rhs=hc[c][:, g, :].bitcast(FP8X4),
+                    rhs_scale=hs[c][:, g, :],
                     start=(g == 0 and i == 0),
                     stop=(g == GROUPS - 1 and i == count - 1),
                 )
@@ -294,8 +312,7 @@ def tile_bcs_gap_step_s13_kernel(tc, phi, coef_bytes, coef_scale, energy, v_word
             transposes(j)
         for j in range(6):
             evacuate(j, True)
-        tanh(0, 1, 2)
-        tanh(0, 2, PACK)
+        tanh(0, 1, PACK)
         tanh(1)
         tanh(2)
         tanh(3)
@@ -306,112 +323,109 @@ def tile_bcs_gap_step_s13_kernel(tc, phi, coef_bytes, coef_scale, energy, v_word
         for t in range(PACK):
             first_product(0, t, at=t)
         quant_phi(1)
-        square_aside(1, 0, 3, 0)
-        transposes(8)
-        transposes(9)
-        first_product(1, 0, at=6)
-        first_product(1, 1, at=7)
+        square_aside("grp1", 0, 2, 0)
+        square_aside("grp1", 2, 4, 0, 1)
+        first_product(1, 0, at=4)
+        first_product(1, 1, at=5)
         for t in range(PACK):
             times_gap(0, t)
-        transposes(10)
-        transposes(11)
+        for j in range(8, 12):
+            transposes(j)
         first_product(1, 2, at=2)
-        evacuate(8, False)
-        evacuate(9, False)
         times_gap(1, 0)
         times_gap(1, 1)
+        for j in range(8, 12):
+            evacuate(j, False)
         transposes(12)
         transposes(13)
         first_product(1, 3, at=5)
         transposes(14)
         transposes(15)
-        evacuate(10, False)
-        evacuate(11, False)
         quant_phi(2)
-        square_aside(2, 3, 4, 0)
         first_product(2, 0, 0, 128, at=0)
         first_product(2, 0, 128, 256, at=1)
         times_gap(1, 2)
         times_gap(1, 3)
-        evacuate(12, False)
-        evacuate(13, False)
         first_product(2, 1, 128, 256, at=2)
         first_product(2, 0, 384, 128, at=5)
-        inv_sqrt(0, 0)
-        inv_sqrt(1, 0)
-        for j in range(14, 16):
+        inv_sqrt(0, 1, 0)
+        inv_sqrt(1, 2, 0)
+        evacuate(12, False)
+        for j in range(13, 16):
             evacuate(j, True)
-        inv_sqrt(2, 0)
-        inv_sqrt(3, 0)
-        make_h(0, 0)
-        make_h(1, 0)
-        quant_h(0, 0)
+        inv_sqrt(2, 3, 0)
+        inv_sqrt(3, 4, 0)
+        make_h(0, 1, 0)
+        make_h(1, 2, 0)
+        quant_h(0, 1, 0)
         times_gap(2, 0, 0, 128)
-        quant_h(1, 0)
+        quant_h(1, 2, 0)
         quant_phi(3)
         passes(0, 4, 0, 1)
         passes(0, 2, 1, 2)
         first_product(3, 0, 0, 128, at=0)
         passes(2, 4, 1, 2)
-        make_h(2, 0)
+        make_h(2, 3, 0)
         times_gap(2, 0, 128, 256)
-        quant_h(2, 0)
+        quant_h(2, 3, 0)
         times_gap(3, 0, 0, 128)
         times_gap(2, 1, 128, 256)
-        make_h(3, 0)
-        times_gap(2, 0, 384, 128)
-        quant_h(3, 0)
-        passes(0, 4, 2, 3)
+        make_h(3, 4, 0)
         first_product(3, 0, 128, 256, at=1)
-        first_product(3, 1, 128, 256, at=2)
+        passes(0, 4, 2, 3)
+        first_product(3, 1, 128, 256, at=0)
+        times_gap(2, 0, 384, 128)
+        quant_h(3, 4, 0)
         passes(0, 4, 3, 4)
-        first_product(3, 0, 384, 128, at=5)
-        inv_sqrt(0, 1)
-        inv_sqrt(1, 1)
-        square_root(0, 1)
-        inv_sqrt(2, 1)
-        square_root(1, 1)
-        square_root(2, 1)
+        inv_sqrt(0, 2, 1)
+        inv_sqrt(2, 4, 1)
+        square_root(0, 2, 1)
+        square_root(2, 4, 1)
+        inv_sqrt(0, 2, 2)
         store(0, True)
-        inv_sqrt(3, 1)
+        square_root(0, 2, 2)
         store(1, True)
-        square_root(3, 1)
-        store(2, True)
-        store(3, True)
-        make_h(0, 1)
+        make_h(0, 1, 1)
         times_gap(3, 0, 128, 256)
-        quant_h(0, 1)
-        make_h(1, 1)
+        quant_h(0, 1, 1)
+        make_h(1, 2, 1)
         times_gap(3, 1, 128, 256)
-        quant_h(1, 1)
-        passes(4, 8, 0, 1)
-        passes(4, 8, 1, 2)
-        passes(8, 9, 0, 2)
-        make_h(2, 1)
+        quant_h(1, 2, 1)
+        passes(4, 7, 0, 1)
+        first_product(3, 0, 384, 128, at=3)
+        passes(4, 7, 1, 2)
+        passes(7, 8, 0, 2)
+        inv_sqrt(2, 4, 2)
+        store(2, True)
+        square_root(2, 4, 2)
+        make_h(2, 4, 1)
+        store(3, False)
+        quant_h(2, 4, 1)
+        passes(4, 8, 2, 4)
+        make_h(0, 2, 2)
         times_gap(3, 0, 384, 128)
-        quant_h(2, 1)
-        passes(9, 10, 0, 2)
-        passes(4, 10, 2, 3)
-        for g in range(4):
-            inv_sqrt(g, 2)
-        make_h(3, 1)
-        quant_h(3, 1)
-        square_root(0, 2, False)
-        square_root(1, 2, False)
-        make_h(0, 2)
-        passes(4, 10, 3, 4)
-        passes(10, 12, 0, 4)
-        square_root(2, 2, False)
-        quant_h(0, 2)
-        make_h(1, 2)
-        square_root(3, 2, False)
-        quant_h(1, 2)
-        make_h(2, 2)
-        make_h(3, 2)
-        quant_h(2, 2)
-        quant_h(3, 2)
-        for n in range(4, 12):
-            store(n, True)
+        quant_h(0, 2, 2)
+        inv_sqrt(0, 2, 3)
+        store(4, True)
+        square_root(0, 2, 3)
+        make_h(2, 4, 2)
+        store(5, False)
+        quant_h(2, 4, 2)
+        passes(8, 12, 0, 2)
+        store(6, False)
+        store(7, False)
+        inv_sqrt(2, 4, 3)
+        passes(8, 12, 2, 4)
+        square_root(2, 4, 3)
+        store(8, True)
+        store(9, True)
+        store(10, True)
+        make_h(0, 2, 3)
+        quant_h(0, 2, 3)
+        make_h(2, 4, 3)
+        store(11, False)
+        quant_h(2, 4, 3)
+        passes(12, 14, 0, 2)
         for n in range(12, 18):
-            passes(n, n + 1, 0, 4)
+            passes(n, n + 1, 2 if n < 14 else 0, 4)
             store(n, n % 2 == 1)

@@ -29,9 +29,9 @@ GAP_BANKS = 2
 WORK_BANKS = 6
 BANKS = GAP_BANKS + WORK_BANKS
 BANK_COLS = 512
-LAST_PARTS = (4, 4, 2, 2, 2, 2)
-RING = (3, 4, 6, 7, 5, 2, 1, 0, 4, 6, 7, 3, 5, 2, 1, 0, 4, 6)
-TURN = (0, 1, 2, 3, 4, 5, 6, 7, 6, 7, 0, 1, 3, 4, 6, 7)
+LAST_PARTS = (2, 2, 2, 2, 2, 2, 2, 2)
+RING = (4, 5, 6, 7, 2, 3, 1, 0, 5, 6, 7, 4, 2, 3, 1, 0, 5, 6, 7, 4)
+TURN = (0, 1, 2, 3, 4, 5, 6, 7, 6, 7, 0, 1, 4, 5, 6, 7)
 
 
 def tile_bcs_gap_step_s13_kernel(tc, phi, coef_bytes, coef_scale, energy, v_words, v_scales, out):
@@ -338,7 +338,7 @@ def tile_bcs_gap_step_s13_kernel(tc, phi, coef_bytes, coef_scale, energy, v_word
             evacuate(j, False)
         transposes(12)
         transposes(13)
-        first_product(1, 3, at=5)
+        first_product(1, 3, at=3)
         transposes(14)
         transposes(15)
         quant_phi(2)
@@ -347,11 +347,10 @@ def tile_bcs_gap_step_s13_kernel(tc, phi, coef_bytes, coef_scale, energy, v_word
         times_gap(1, 2)
         times_gap(1, 3)
         first_product(2, 1, 128, 256, at=2)
-        first_product(2, 0, 384, 128, at=5)
+        first_product(2, 0, 384, 128, at=3)
         inv_sqrt(0, 1, 0)
         inv_sqrt(1, 2, 0)
-        evacuate(12, False)
-        for j in range(13, 16):
+        for j in range(12, 16):
             evacuate(j, True)
         inv_sqrt(2, 3, 0)
         inv_sqrt(3, 4, 0)
@@ -360,21 +359,22 @@ def tile_bcs_gap_step_s13_kernel(tc, phi, coef_bytes, coef_scale, energy, v_word
         quant_h(0, 1, 0)
         times_gap(2, 0, 0, 128)
         quant_h(1, 2, 0)
+        times_gap(2, 0, 128, 256)
         quant_phi(3)
         passes(0, 4, 0, 1)
         passes(0, 2, 1, 2)
         first_product(3, 0, 0, 128, at=0)
         passes(2, 4, 1, 2)
         make_h(2, 3, 0)
-        times_gap(2, 0, 128, 256)
+        times_gap(2, 1, 128, 256)
         quant_h(2, 3, 0)
         times_gap(3, 0, 0, 128)
-        times_gap(2, 1, 128, 256)
+        times_gap(2, 0, 384, 128)
         make_h(3, 4, 0)
         first_product(3, 0, 128, 256, at=1)
         passes(0, 4, 2, 3)
         first_product(3, 1, 128, 256, at=0)
-        times_gap(2, 0, 384, 128)
+        times_gap(3, 0, 128, 256)
         quant_h(3, 4, 0)
         passes(0, 4, 3, 4)
         inv_sqrt(0, 2, 1)
@@ -386,46 +386,45 @@ def tile_bcs_gap_step_s13_kernel(tc, phi, coef_bytes, coef_scale, energy, v_word
         square_root(0, 2, 2)
         store(1, True)
         make_h(0, 1, 1)
-        times_gap(3, 0, 128, 256)
+        times_gap(3, 1, 128, 256)
         quant_h(0, 1, 1)
         make_h(1, 2, 1)
-        times_gap(3, 1, 128, 256)
+        store(2, False)
         quant_h(1, 2, 1)
-        passes(4, 7, 0, 1)
-        first_product(3, 0, 384, 128, at=3)
-        passes(4, 7, 1, 2)
-        passes(7, 8, 0, 2)
+        passes(4, 8, 0, 1)
+        first_product(3, 0, 384, 128, at=4)
+        passes(4, 8, 1, 2)
         inv_sqrt(2, 4, 2)
-        store(2, True)
         square_root(2, 4, 2)
         make_h(2, 4, 1)
         store(3, False)
         quant_h(2, 4, 1)
         passes(4, 8, 2, 4)
         make_h(0, 2, 2)
-        times_gap(3, 0, 384, 128)
+        store(4, False)
         quant_h(0, 2, 2)
         inv_sqrt(0, 2, 3)
-        store(4, True)
+        store(5, True)
         square_root(0, 2, 3)
         make_h(2, 4, 2)
-        store(5, False)
+        times_gap(3, 0, 384, 128)
         quant_h(2, 4, 2)
-        passes(8, 12, 0, 2)
+        passes(8, 11, 0, 2)
         store(6, False)
         store(7, False)
         inv_sqrt(2, 4, 3)
-        passes(8, 12, 2, 4)
-        square_root(2, 4, 3)
+        passes(8, 11, 2, 4)
+        passes(11, 12, 0, 4)
         store(8, True)
-        store(9, True)
-        store(10, True)
+        square_root(2, 4, 3)
         make_h(0, 2, 3)
+        store(9, False)
+        store(10, True)
         quant_h(0, 2, 3)
         make_h(2, 4, 3)
-        store(11, False)
+        store(11, True)
         quant_h(2, 4, 3)
-        passes(12, 14, 0, 2)
-        for n in range(12, 18):
-            passes(n, n + 1, 2 if n < 14 else 0, 4)
+        passes(12, 17, 0, 2)
+        for n in range(12, 20):
+            passes(n, n + 1, 2 if n < 17 else 0, 4)
             store(n, n % 2 == 1)

@@ -20,26 +20,33 @@ MULT = mybir.AluOpType.mult
 P = 128
 PACK = 4
 GROUPS = M // (P * PACK)
+HALF = GROUPS // 2
 PASSES = R // (P * PACK)
 TILES = M // P
 RUN = 4
-
-CHUNKS = ((0, 128), (128, 128), (256, 128), (384, 128))
-GAP_BANKS = 2
-WORK_BANKS = 6
-BANKS = GAP_BANKS + WORK_BANKS
+BANKS = 8
 BANK_COLS = 512
-LAST_PARTS = (2, 2, 2, 2, 2, 2, 2, 2)
-RING = (4, 5, 6, 7, 2, 3, 1, 0, 5, 6, 7, 4, 2, 3, 1, 0, 5, 6, 7, 4)
-TURN = (0, 1, 2, 3, 4, 5, 6, 7, 6, 7, 0, 1, 4, 5, 6, 7)
+NC = 128
+CHUNKS = B // NC
+PART = BANK_COLS // NC
+LAST_PART = 2
+PARTS = TILES // PART
+
+WHOLE = [(0, B, t) for t in range(PACK)]
+FIRST = (0, NC, 0)
+MIDDLE = [(NC, 2 * NC, n) for n in range(2)]
+LAST = (B - NC, NC, 0)
+
+SLOTS_WIDENED_BY_VECTOR = 2
+TILES_EMPTIED_BEFORE_TANH = 6
+AHEAD_IN_THIRD_CHUNK = 3
+AHEAD_IN_LAST_CHUNK = 5
 
 
 def tile_bcs_gap_step_s13_kernel(tc, phi, coef_bytes, coef_scale, energy, v_words, v_scales, out):
     nc = tc.nc
-    parts = []
-    for c, (first, width) in enumerate(CHUNKS[:-1]):
-        parts.extend((c, i0, BANK_COLS // width) for i0 in range(0, TILES, BANK_COLS // width))
-    parts.extend((len(CHUNKS) - 1, sum(LAST_PARTS[:n]), count) for n, count in enumerate(LAST_PARTS))
+    parts = [(c, i0, PART) for c in range(CHUNKS - 1) for i0 in range(0, TILES, PART)]
+    parts = parts + [(CHUNKS - 1, i0, LAST_PART) for i0 in range(0, TILES, LAST_PART)]
 
     with ExitStack() as ctx:
         keep = ctx.enter_context(tc.tile_pool(name="keep", bufs=1))
@@ -47,12 +54,18 @@ def tile_bcs_gap_step_s13_kernel(tc, phi, coef_bytes, coef_scale, energy, v_word
         psum = ctx.enter_context(tc.psum_pool(name="psum", bufs=1))
         ctx.enter_context(tc.manual_schedule())
 
-        def bank_tile(shape, bank):
-            return psum.tile(shape, F32, name="bank", tag="bank%d" % bank, bufs=1)
+        free_banks = list(range(BANKS))
+        bank_of = {}
 
-        en_all = keep.tile([P, GROUPS * PACK, B], BF16, name="en", align_bytes=64)
-        en = [en_all[:, PACK * g : PACK * (g + 1), :] for g in range(GROUPS)]
-        ph = [keep.tile([P, 2, R], BF16, name="ph%d" % j, align_bytes=64) for j in range(TILES // 2)]
+        def take_bank(user, shape):
+            bank_of[user] = free_banks.pop(0)
+            return psum.tile(shape, F32, name="bank", tag="bank%d" % bank_of[user], bufs=1)
+
+        def give_back(user):
+            free_banks.append(bank_of[user])
+
+        en = keep.tile([P, GROUPS * PACK, B], BF16, name="en", align_bytes=64)
+        ph = [keep.tile([P, 2, R], BF16, name="ph%d" % pair, align_bytes=64) for pair in range(TILES // 2)]
         cb = [keep.tile([P, PACK * B], U8, name="cb%d" % k, align_bytes=64) for k in range(PASSES)]
         cs = keep.tile([P, PASSES, PACK], F32, name="cs", align_bytes=64)
         vw = [keep.tile([P, 2 * M], U8, name="vw%d" % g, align_bytes=256) for g in range(GROUPS)]
@@ -66,59 +79,49 @@ def tile_bcs_gap_step_s13_kernel(tc, phi, coef_bytes, coef_scale, energy, v_word
         vs_v = v_scales.rearrange("g (q r) n -> r q g n", r=4)
         out_v = out.rearrange("(i p) n -> p i n", p=P)
 
-        def load_coef(k, t0=0, t1=PACK):
-            nc.sync.dma_start(out=cb[k][:, t0 * B : t1 * B], in_=cb_v[k][:, t0 * B : t1 * B])
-
         def load_energy(g, t0=0, t1=PACK):
-            nc.sync.dma_start(out=en[g][:, t0:t1, :], in_=en_v[g][:, t0:t1, :])
+            nc.sync.dma_start(out=en[:, PACK * g + t0 : PACK * g + t1, :], in_=en_v[g][:, t0:t1, :])
 
         def load_phi(pair):
             g, half = divmod(pair, 2)
             nc.sync.dma_start(out=ph[pair][:], in_=phi_v[g][:, 2 * half : 2 * half + 2, :])
 
-        def load_scales(g0, g1):
+        def load_v(g0, g1):
             for r in range(4):
                 nc.sync.dma_start(out=vs[r:P:32, g0:g1, :].bitcast(I32), in_=vs_v[r][:, g0:g1, :].bitcast(I32))
-
-        def load_words(g):
-            nc.sync.dma_start(out=vw[g][:], in_=v_words[g])
+            for g in range(g0, g1):
+                nc.sync.dma_start(out=vw[g][:], in_=v_words[g])
 
         make_identity(nc, ident[:])
         nc.vector.memset(vs[:].rearrange("p g n -> p (g n)").bitcast(I32), 0)
 
         nc.sync.dma_start(out=cs[:], in_=cs_v)
         load_energy(0, 0, 1)
-        load_coef(0)
-        load_coef(1)
-        for pair in range(4):
+        for k in range(PASSES):
+            nc.sync.dma_start(out=cb[k][:], in_=cb_v[k])
+        for pair in range(BANKS // 2):
             load_phi(pair)
         load_energy(0, 1, PACK)
-        load_energy(1)
-        load_phi(4)
-        load_energy(2)
-        load_phi(5)
-        load_energy(3)
-        load_phi(6)
-        load_phi(7)
-        load_scales(0, 2)
-        load_words(0)
-        load_words(1)
-        load_scales(2, 4)
-        load_words(2)
-        load_words(3)
+        for g in range(1, GROUPS):
+            load_energy(g)
+            load_phi(BANKS // 2 + g - 1)
+        load_phi(TILES // 2 - 1)
+        load_v(0, HALF)
+        load_v(HALF, GROUPS)
 
         cc = keep.tile([P, PASSES, B], U32, name="cc", align_bytes=256)
         csc = keep.tile([P, PASSES, B], U8, name="csc", align_bytes=256)
         wide = [stage.tile([P, PACK, B], BF16, name="wide", tag="wide", bufs=4, align_bytes=64) for k in range(PASSES)]
         cgrp = [stage.tile([P, B, PACK], BF16, name="cgrp", tag="wide", bufs=4, align_bytes=64) for k in range(PASSES)]
 
-        def coef_widen(k, t0=0, t1=PACK, on_scalar=False):
-            for t in range(t0, t1):
+        def coef_widen(k):
+            for t in range(PACK):
                 codes = cb[k][:, t * B : (t + 1) * B].bitcast(FP8)
-                if on_scalar:
-                    nc.scalar.activation(out=wide[k][:, t, :], in_=codes, func=ACT.Copy, scale=cs[:, k, t : t + 1])
+                scale = cs[:, k, t : t + 1]
+                if t < SLOTS_WIDENED_BY_VECTOR:
+                    nc.vector.tensor_scalar(out=wide[k][:, t, :], in0=codes, scalar1=scale, scalar2=None, op0=MULT)
                 else:
-                    nc.vector.tensor_scalar(out=wide[k][:, t, :], in0=codes, scalar1=cs[:, k, t : t + 1], scalar2=None, op0=MULT)
+                    nc.scalar.activation(out=wide[k][:, t, :], in_=codes, func=ACT.Copy, scale=scale)
 
         def coef_interleave(k):
             nc.vector.tensor_copy(
@@ -134,27 +137,26 @@ def tile_bcs_gap_step_s13_kernel(tc, phi, coef_bytes, coef_scale, energy, v_word
         turned = {}
         grouped = {}
 
-        def turn_bank(j):
-            return TURN[j]
+        def transposes(j0, j1):
+            for j in range(j0, j1):
+                turned[j] = take_bank(("turned", j), [P, PASSES, 2, P])
+                words = ph[j // 2][:, j % 2, :].bitcast(F32)
+                for k in range(PASSES):
+                    for u in range(2):
+                        nc.tensor.transpose(turned[j][:, k, u, :], words[:, 256 * k + u : 256 * (k + 1) : 2], ident[:])
 
-        def transposes(j):
-            bank = bank_tile([P, PASSES, 2, P], turn_bank(j))
-            words = ph[j // 2][:, j % 2, :].bitcast(F32)
-            for k in range(PASSES):
-                for u in range(2):
-                    nc.tensor.transpose(bank[:, k, u, :], words[:, 256 * k + u : 256 * (k + 1) : 2], ident[:])
-            turned[j] = bank
-
-        def evacuate(j, on_scalar):
-            g, t = divmod(j, PACK)
-            if t == 0:
-                grouped[g] = stage.tile([P, PACK, PASSES * P * PACK], BF16, name="grp", tag="grp%d" % g, bufs=1, align_bytes=64)
-            dst = grouped[g][:, t, :].bitcast(F32).rearrange("p (k r u) -> p k r u", k=PASSES, u=2)
-            src = turned[j][:].rearrange("p k u r -> p k r u")
-            if on_scalar:
-                nc.scalar.copy(out=dst, in_=src)
-            else:
-                nc.vector.tensor_copy(out=dst, in_=src)
+        def empty_turned(j0, j1, on_scalar):
+            for j in range(j0, j1):
+                g, t = divmod(j, PACK)
+                if t == 0:
+                    grouped[g] = stage.tile([P, PACK, PASSES * P * PACK], BF16, name="grp", tag="grp%d" % g, bufs=1, align_bytes=64)
+                dst = grouped[g][:, t, :].bitcast(F32).rearrange("p (k r u) -> p k r u", k=PASSES, u=2)
+                src = turned[j][:].rearrange("p k u r -> p k r u")
+                if on_scalar:
+                    nc.scalar.copy(out=dst, in_=src)
+                else:
+                    nc.vector.tensor_copy(out=dst, in_=src)
+                give_back(("turned", j))
 
         def quant_phi(g, t0=0, t1=PACK):
             nc.vector.quantize_mx(
@@ -164,75 +166,61 @@ def tile_bcs_gap_step_s13_kernel(tc, phi, coef_bytes, coef_scale, energy, v_word
             )
 
         num = keep.tile([P, GROUPS, B // RUN, PACK, RUN], F32, name="num", align_bytes=64)
-        squared = {}
-        rooms = {}
         inv = {}
 
         def tanh(g, t0=0, t1=PACK):
             nc.scalar.activation(
                 out=num[:, g, :, t0:t1, :].rearrange("p c t i -> p t c i"),
-                in_=en[g][:, t0:t1, :].rearrange("p t (c i) -> p t c i", i=RUN),
+                in_=en[:, PACK * g + t0 : PACK * g + t1, :].rearrange("p t (c i) -> p t c i", i=RUN),
                 func=ACT.Tanh,
             )
 
-        def square_aside(tag, g0, g1, c, part=0):
-            if part == 0:
-                rooms[tag] = stage.tile([P, PACK * B], F32, name="esq", tag=tag, bufs=1, align_bytes=64)
-            first, width = CHUNKS[c]
-            size = (g1 - g0) * PACK * width
-            esq = rooms[tag][:, part * size : (part + 1) * size].rearrange("p (r n) -> p r n", n=width)
-            src = en_all[:, PACK * g0 : PACK * g1, first : first + width]
-            nc.gpsimd.tensor_tensor(out=esq, in0=src, in1=src, op=MULT)
-            for g in range(g0, g1):
-                squared[g, c] = (esq, g0)
+        def energies(g0, g1, c):
+            return en[:, PACK * g0 : PACK * g1, c * NC : (c + 1) * NC]
 
-        def new_inv(g0, g1, c):
-            width = CHUNKS[c][1]
-            tag = "wide" if (g1 - g0) * width > P else "inv"
-            room = stage.tile([P, g1 - g0, width // RUN, PACK, RUN], F32, name="inv", tag=tag, bufs=4, align_bytes=64)
+        def square_first_chunk():
+            squares = stage.tile([P, GROUPS * PACK, NC], F32, name="esq", tag="grp1", bufs=1, align_bytes=64)
+            for g0 in (0, HALF):
+                src = energies(g0, g0 + HALF, 0)
+                nc.gpsimd.tensor_tensor(out=squares[:, PACK * g0 : PACK * (g0 + HALF), :], in0=src, in1=src, op=MULT)
+            return squares
+
+        def inv_sqrt(g0, g1, c, src):
+            tag = "inv" if g1 - g0 == 1 else "wide"
+            room = stage.tile([P, g1 - g0, NC // RUN, PACK, RUN], F32, name="inv", tag=tag, bufs=4, align_bytes=64)
             for g in range(g0, g1):
                 inv[g, c] = (room, g0)
-
-        def inv_of(g0, g1, c):
-            room, base = inv[g0, c]
-            return room[:, g0 - base : g1 - base]
-
-        def inv_sqrt(g0, g1, c):
-            first, width = CHUNKS[c]
-            if (g0, c) not in inv:
-                new_inv(g0, g1, c)
-            if (g0, c) in squared:
-                esq, base = squared[g0, c]
-                src = esq[:, PACK * (g0 - base) : PACK * (g1 - base), :]
-            else:
-                src = en_all[:, PACK * g0 : PACK * g1, first : first + width]
             nc.scalar.activation(
-                out=inv_of(g0, g1, c).rearrange("p g c t i -> p t g c i"),
+                out=room[:].rearrange("p g c t i -> p t g c i"),
                 in_=src.rearrange("p (g t) (c i) -> p t g c i", t=PACK, i=RUN),
                 func=ACT.Abs_reciprocal_sqrt,
             )
 
-        def square_root(g0, g1, c, on_scalar=True):
-            root = inv_of(g0, g1, c).rearrange("p g c t i -> p (g c t i)")
-            if on_scalar:
-                nc.scalar.activation(out=root, in_=root, func=ACT.Square)
-            else:
-                nc.vector.tensor_tensor(out=root, in0=root, in1=root, op=MULT)
+        def inv_from_square(g):
+            inv_sqrt(g, g + 1, 0, squares[:, PACK * g : PACK * (g + 1), :])
 
-        hc = [keep.tile([P, GROUPS, width], U32, name="hc%d" % c, align_bytes=256) for c, (first, width) in enumerate(CHUNKS)]
-        hs = [keep.tile([P, GROUPS, width], U8, name="hs%d" % c, align_bytes=256) for c, (first, width) in enumerate(CHUNKS)]
+        def root(g0, c):
+            inv_sqrt(g0, g0 + HALF, c, energies(g0, g0 + HALF, c))
+
+        def square_root(g0, c):
+            values = inv[g0, c][0][:].rearrange("p g c t i -> p (g c t i)")
+            nc.scalar.activation(out=values, in_=values, func=ACT.Square)
+
+        hc = [keep.tile([P, GROUPS, NC], U32, name="hc%d" % c, align_bytes=256) for c in range(CHUNKS)]
+        hs = [keep.tile([P, GROUPS, NC], U8, name="hs%d" % c, align_bytes=256) for c in range(CHUNKS)]
         gaps = {}
         hgrp = {}
 
-        def first_product(g, n, first=0, width=B, at=None):
+        def first_product(g, piece):
+            first, width, n = piece
             count = BANK_COLS // width
-            bank = bank_tile([P, count, width], len(gaps) % GAP_BANKS if at is None else at)
+            gaps[g, piece] = take_bank(("gap", g, piece), [P, count, width])
             cols = slice(first, first + width)
             for i in range(count):
                 t = n * count + i
                 for k in range(PASSES):
                     nc.tensor.matmul_mx(
-                        out=bank[:, i, :],
+                        out=gaps[g, piece][:, i, :],
                         lhsT=pc[g][:, t, k, :].bitcast(FP8X4),
                         lhsT_scale=psc[g][:, t, k, :],
                         rhs=cc[:, k, cols].bitcast(FP8X4),
@@ -240,20 +228,22 @@ def tile_bcs_gap_step_s13_kernel(tc, phi, coef_bytes, coef_scale, energy, v_word
                         start=(k == 0),
                         stop=(k == PASSES - 1),
                     )
-            gaps[g, n, first] = bank
 
-        def times_gap(g, n, first=0, width=B):
+        def times_gap(g, piece):
+            first, width, n = piece
             count = BANK_COLS // width
             w = num[:, g, first // RUN : (first + width) // RUN, n * count : (n + 1) * count, :].rearrange("p c t i -> p t c i")
-            nc.vector.tensor_tensor(out=w, in0=gaps[g, n, first][:].rearrange("p t (c i) -> p t c i", i=RUN), in1=w, op=MULT)
+            nc.vector.tensor_tensor(out=w, in0=gaps[g, piece][:].rearrange("p t (c i) -> p t c i", i=RUN), in1=w, op=MULT)
+            give_back(("gap", g, piece))
 
         def make_h(g0, g1, c):
-            first, width = CHUNKS[c]
-            hgrp[g0, c] = stage.tile([P, g1 - g0, width, PACK], BF16, name="hg", tag="hg", bufs=3, align_bytes=64)
+            room, base = inv[g0, c]
+            runs = NC // RUN
+            hgrp[g0, c] = stage.tile([P, g1 - g0, NC, PACK], BF16, name="hg", tag="hg", bufs=3, align_bytes=64)
             nc.vector.tensor_tensor(
                 out=hgrp[g0, c][:].rearrange("p g (c i) t -> p g c t i", i=RUN),
-                in0=num[:, g0:g1, first // RUN : (first + width) // RUN],
-                in1=inv_of(g0, g1, c),
+                in0=num[:, g0:g1, c * runs : (c + 1) * runs],
+                in1=room[:, g0 - base : g1 - base],
                 op=MULT,
             )
 
@@ -265,166 +255,155 @@ def tile_bcs_gap_step_s13_kernel(tc, phi, coef_bytes, coef_scale, energy, v_word
             )
 
         sums = {}
-
-        def part_bank(n):
-            return RING[n]
-
-        def part_pass(n, g):
-            c, i0, count = parts[n]
-            if g == 0:
-                sums[n] = bank_tile([P, count, CHUNKS[c][1]], part_bank(n))
-            for i in range(count):
-                tile_i = i0 + i
-                nc.tensor.matmul_mx(
-                    out=sums[n][:, i, :],
-                    lhsT=vw[g][:, 2 * P * tile_i : 2 * P * (tile_i + 1)].bitcast(FP4X4),
-                    lhsT_scale=vs[:, g, P * tile_i : P * (tile_i + 1)],
-                    rhs=hc[c][:, g, :].bitcast(FP8X4),
-                    rhs_scale=hs[c][:, g, :],
-                    start=(g == 0 and i == 0),
-                    stop=(g == GROUPS - 1 and i == count - 1),
-                )
+        finished = []
 
         def passes(n0, n1, g0, g1):
             for n in range(n0, n1):
+                c, i0, count = parts[n]
+                if g0 == 0:
+                    sums[n] = take_bank(("part", n), [P, count, NC])
                 for g in range(g0, g1):
-                    part_pass(n, g)
+                    for i in range(count):
+                        tile_i = i0 + i
+                        nc.tensor.matmul_mx(
+                            out=sums[n][:, i, :],
+                            lhsT=vw[g][:, 2 * P * tile_i : 2 * P * (tile_i + 1)].bitcast(FP4X4),
+                            lhsT_scale=vs[:, g, P * tile_i : P * (tile_i + 1)],
+                            rhs=hc[c][:, g, :].bitcast(FP8X4),
+                            rhs_scale=hs[c][:, g, :],
+                            start=(g == 0 and i == 0),
+                            stop=(g == GROUPS - 1 and i == count - 1),
+                        )
+                if g1 == GROUPS:
+                    finished.append(n)
 
-        def store(n, on_scalar):
+        def chunk_passes(c, g0, g1):
+            passes(PARTS * c, PARTS * (c + 1), g0, g1)
+
+        def store(on_scalar):
+            n = finished.pop(0)
             c, i0, count = parts[n]
-            first, width = CHUNKS[c]
-            o = stage.tile([P, count, width], F32, name="o", tag="o", bufs=8, align_bytes=64)
+            o = stage.tile([P, count, NC], F32, name="o", tag="o", bufs=8, align_bytes=64)
             if on_scalar:
                 nc.scalar.copy(out=o[:], in_=sums[n][:])
             else:
                 nc.vector.tensor_copy(out=o[:], in_=sums[n][:])
-            nc.sync.dma_start(out=out_v[:, i0 : i0 + count, first : first + width], in_=o[:])
+            give_back(("part", n))
+            nc.sync.dma_start(out=out_v[:, i0 : i0 + count, c * NC : (c + 1) * NC], in_=o[:])
+
+        def h_with_piece(g0, g1, c, g, piece):
+            make_h(g0, g1, c)
+            times_gap(g, piece)
+            quant_h(g0, g1, c)
+
+        def h_with_store(g0, g1, c):
+            make_h(g0, g1, c)
+            store(on_scalar=False)
+            quant_h(g0, g1, c)
+
+        def inv_with_store(g0, c):
+            root(g0, c)
+            store(on_scalar=True)
+            square_root(g0, c)
 
         tanh(0, 0, 1)
         for k in range(PASSES):
-            coef_widen(k, 0, 2)
-            coef_widen(k, 2, 4, True)
+            coef_widen(k)
         for k in range(PASSES):
             coef_interleave(k)
         for k in range(PASSES):
             coef_quant(k)
-        for j in range(8):
-            transposes(j)
-        for j in range(6):
-            evacuate(j, True)
+        transposes(0, BANKS)
+        empty_turned(0, TILES_EMPTIED_BEFORE_TANH, on_scalar=True)
         tanh(0, 1, PACK)
-        tanh(1)
-        tanh(2)
-        tanh(3)
+        for g in range(1, GROUPS):
+            tanh(g)
         quant_phi(0, 0, 2)
-        quant_phi(0, 2, 4)
-        evacuate(6, False)
-        evacuate(7, False)
-        for t in range(PACK):
-            first_product(0, t, at=t)
+        quant_phi(0, 2, PACK)
+        empty_turned(TILES_EMPTIED_BEFORE_TANH, BANKS, on_scalar=False)
+        for piece in WHOLE:
+            first_product(0, piece)
         quant_phi(1)
-        square_aside("grp1", 0, 2, 0)
-        square_aside("grp1", 2, 4, 0, 1)
-        first_product(1, 0, at=4)
-        first_product(1, 1, at=5)
-        for t in range(PACK):
-            times_gap(0, t)
-        for j in range(8, 12):
-            transposes(j)
-        first_product(1, 2, at=2)
-        times_gap(1, 0)
-        times_gap(1, 1)
-        for j in range(8, 12):
-            evacuate(j, False)
-        transposes(12)
-        transposes(13)
-        first_product(1, 3, at=3)
-        transposes(14)
-        transposes(15)
+
+        squares = square_first_chunk()
+        first_product(1, WHOLE[0])
+        first_product(1, WHOLE[1])
+        for piece in WHOLE:
+            times_gap(0, piece)
+        transposes(2 * PACK, 3 * PACK)
+        first_product(1, WHOLE[2])
+        times_gap(1, WHOLE[0])
+        times_gap(1, WHOLE[1])
+        empty_turned(2 * PACK, 3 * PACK, on_scalar=False)
+        transposes(3 * PACK, TILES - 2)
+        first_product(1, WHOLE[3])
+        transposes(TILES - 2, TILES)
         quant_phi(2)
-        first_product(2, 0, 0, 128, at=0)
-        first_product(2, 0, 128, 256, at=1)
-        times_gap(1, 2)
-        times_gap(1, 3)
-        first_product(2, 1, 128, 256, at=2)
-        first_product(2, 0, 384, 128, at=3)
-        inv_sqrt(0, 1, 0)
-        inv_sqrt(1, 2, 0)
-        for j in range(12, 16):
-            evacuate(j, True)
-        inv_sqrt(2, 3, 0)
-        inv_sqrt(3, 4, 0)
+
+        first_product(2, FIRST)
+        first_product(2, MIDDLE[0])
+        times_gap(1, WHOLE[2])
+        times_gap(1, WHOLE[3])
+        first_product(2, MIDDLE[1])
+        first_product(2, LAST)
+        inv_from_square(0)
+        inv_from_square(1)
+        empty_turned(3 * PACK, TILES, on_scalar=True)
+        inv_from_square(2)
+        inv_from_square(3)
         make_h(0, 1, 0)
         make_h(1, 2, 0)
         quant_h(0, 1, 0)
-        times_gap(2, 0, 0, 128)
+        times_gap(2, FIRST)
         quant_h(1, 2, 0)
-        times_gap(2, 0, 128, 256)
+        times_gap(2, MIDDLE[0])
         quant_phi(3)
-        passes(0, 4, 0, 1)
-        passes(0, 2, 1, 2)
-        first_product(3, 0, 0, 128, at=0)
-        passes(2, 4, 1, 2)
-        make_h(2, 3, 0)
-        times_gap(2, 1, 128, 256)
-        quant_h(2, 3, 0)
-        times_gap(3, 0, 0, 128)
-        times_gap(2, 0, 384, 128)
-        make_h(3, 4, 0)
-        first_product(3, 0, 128, 256, at=1)
-        passes(0, 4, 2, 3)
-        first_product(3, 1, 128, 256, at=0)
-        times_gap(3, 0, 128, 256)
-        quant_h(3, 4, 0)
-        passes(0, 4, 3, 4)
-        inv_sqrt(0, 2, 1)
-        inv_sqrt(2, 4, 1)
-        square_root(0, 2, 1)
-        square_root(2, 4, 1)
-        inv_sqrt(0, 2, 2)
-        store(0, True)
-        square_root(0, 2, 2)
-        store(1, True)
-        make_h(0, 1, 1)
-        times_gap(3, 1, 128, 256)
-        quant_h(0, 1, 1)
-        make_h(1, 2, 1)
-        store(2, False)
-        quant_h(1, 2, 1)
-        passes(4, 8, 0, 1)
-        first_product(3, 0, 384, 128, at=4)
-        passes(4, 8, 1, 2)
-        inv_sqrt(2, 4, 2)
-        square_root(2, 4, 2)
-        make_h(2, 4, 1)
-        store(3, False)
-        quant_h(2, 4, 1)
-        passes(4, 8, 2, 4)
-        make_h(0, 2, 2)
-        store(4, False)
-        quant_h(0, 2, 2)
-        inv_sqrt(0, 2, 3)
-        store(5, True)
-        square_root(0, 2, 3)
-        make_h(2, 4, 2)
-        times_gap(3, 0, 384, 128)
-        quant_h(2, 4, 2)
-        passes(8, 11, 0, 2)
-        store(6, False)
-        store(7, False)
-        inv_sqrt(2, 4, 3)
-        passes(8, 11, 2, 4)
-        passes(11, 12, 0, 4)
-        store(8, True)
-        square_root(2, 4, 3)
-        make_h(0, 2, 3)
-        store(9, False)
-        store(10, True)
-        quant_h(0, 2, 3)
-        make_h(2, 4, 3)
-        store(11, True)
-        quant_h(2, 4, 3)
-        passes(12, 17, 0, 2)
-        for n in range(12, 20):
-            passes(n, n + 1, 2 if n < 17 else 0, 4)
-            store(n, n % 2 == 1)
+
+        chunk_passes(0, 0, 1)
+        passes(0, PARTS // 2, 1, 2)
+        first_product(3, FIRST)
+        passes(PARTS // 2, PARTS, 1, 2)
+        h_with_piece(2, 3, 0, 2, MIDDLE[1])
+        times_gap(3, FIRST)
+        times_gap(2, LAST)
+        first_product(3, MIDDLE[0])
+        chunk_passes(0, 2, 3)
+        first_product(3, MIDDLE[1])
+        h_with_piece(3, 4, 0, 3, MIDDLE[0])
+        chunk_passes(0, 3, 4)
+
+        for g0 in (0, HALF):
+            root(g0, 1)
+        for g0 in (0, HALF):
+            square_root(g0, 1)
+        h_with_piece(0, 1, 1, 3, MIDDLE[1])
+        chunk_passes(1, 0, 1)
+        inv_with_store(0, 2)
+        first_product(3, LAST)
+        h_with_store(1, 2, 1)
+        chunk_passes(1, 1, 2)
+        h_with_store(HALF, GROUPS, 1)
+        chunk_passes(1, HALF, GROUPS)
+        inv_with_store(HALF, 2)
+
+        third = 2 * PARTS
+        h_with_store(0, HALF, 2)
+        passes(third, third + AHEAD_IN_THIRD_CHUNK, 0, HALF)
+        inv_with_store(0, 3)
+        h_with_piece(HALF, GROUPS, 2, 3, LAST)
+        passes(third, third + AHEAD_IN_THIRD_CHUNK, HALF, GROUPS)
+        passes(third + AHEAD_IN_THIRD_CHUNK, third + PARTS, 0, GROUPS)
+        store(on_scalar=False)
+        store(on_scalar=False)
+        inv_with_store(HALF, 3)
+
+        last = 3 * PARTS
+        h_with_store(0, HALF, 3)
+        passes(last, last + AHEAD_IN_LAST_CHUNK, 0, HALF)
+        store(on_scalar=True)
+        store(on_scalar=True)
+        make_h(HALF, GROUPS, 3)
+        quant_h(HALF, GROUPS, 3)
+        for n in range(last, len(parts)):
+            passes(n, n + 1, HALF if n < last + AHEAD_IN_LAST_CHUNK else 0, GROUPS)
+            store(on_scalar=(n % 2 == 1))

@@ -332,12 +332,11 @@ def tile_bcs_gap_step_s13_kernel(tc, phi, coef_bytes, coef_scale, energy, v_word
             times_gap(0, piece)
         transposes(2 * PACK, 3 * PACK)
         first_product(1, WHOLE[2])
+        first_product(1, WHOLE[3])
         times_gap(1, WHOLE[0])
         times_gap(1, WHOLE[1])
         empty_turned(2 * PACK, 3 * PACK, on_scalar=False)
-        transposes(3 * PACK, TILES - 2)
-        first_product(1, WHOLE[3])
-        transposes(TILES - 2, TILES)
+        transposes(3 * PACK, TILES)
         quant_phi(2)
 
         first_product(2, FIRST)

@@ -39,14 +39,17 @@ LAST = (B - NC, NC, 0)
 
 SLOTS_WIDENED_BY_VECTOR = 2
 TILES_EMPTIED_BEFORE_TANH = 6
+CHUNK = [(0, 128, 4), (128, 128, 4), (256, 128, 4), (384, 128, 2)]
+WIDE = 8
+STEP = 2
 AHEAD_IN_THIRD_CHUNK = 3
-AHEAD_IN_LAST_CHUNK = 5
+AHEAD_IN_LAST_CHUNK = 4
 
 
 def tile_bcs_gap_step_s13_kernel(tc, phi, coef_bytes, coef_scale, energy, v_words, v_scales, out):
     nc = tc.nc
-    parts = [(c, i0, PART) for c in range(CHUNKS - 1) for i0 in range(0, TILES, PART)]
-    parts = parts + [(CHUNKS - 1, i0, LAST_PART) for i0 in range(0, TILES, LAST_PART)]
+    parts = [(c, i0, count) for c, (first, width, count) in enumerate(CHUNK) for i0 in range(0, TILES, count)]
+    first_part = [sum(TILES // count for first, width, count in CHUNK[:c]) for c in range(len(CHUNK) + 1)]
 
     with ExitStack() as ctx:
         keep = ctx.enter_context(tc.tile_pool(name="keep", bufs=1))
@@ -65,7 +68,7 @@ def tile_bcs_gap_step_s13_kernel(tc, phi, coef_bytes, coef_scale, energy, v_word
             free_banks.append(bank_of[user])
 
         en = keep.tile([P, GROUPS * PACK, B], BF16, name="en", align_bytes=64)
-        ph = [keep.tile([P, 2, R], BF16, name="ph%d" % pair, align_bytes=64) for pair in range(TILES // 2)]
+        ph = [stage.tile([P, 2, R], BF16, name="ph", tag="ph", bufs=8, align_bytes=64) for pair in range(TILES // 2)]
         cb = [keep.tile([P, PACK * B], U8, name="cb%d" % k, align_bytes=64) for k in range(PASSES)]
         cs = keep.tile([P, PASSES, PACK], F32, name="cs", align_bytes=64)
         vw = [keep.tile([P, 2 * M], U8, name="vw%d" % g, align_bytes=256) for g in range(GROUPS)]
@@ -111,8 +114,8 @@ def tile_bcs_gap_step_s13_kernel(tc, phi, coef_bytes, coef_scale, energy, v_word
 
         cc = keep.tile([P, PASSES, B], U32, name="cc", align_bytes=256)
         csc = keep.tile([P, PASSES, B], U8, name="csc", align_bytes=256)
-        wide = [stage.tile([P, PACK, B], BF16, name="wide", tag="wide", bufs=4, align_bytes=64) for k in range(PASSES)]
-        cgrp = [stage.tile([P, B, PACK], BF16, name="cgrp", tag="wide", bufs=4, align_bytes=64) for k in range(PASSES)]
+        wide = [stage.tile([P, PACK, B], BF16, name="wide", tag="wide", bufs=WIDE, align_bytes=64) for k in range(PASSES)]
+        cgrp = [stage.tile([P, B, PACK], BF16, name="cgrp", tag="wide", bufs=WIDE, align_bytes=64) for k in range(PASSES)]
 
         def coef_widen(k):
             for t in range(PACK):
@@ -176,18 +179,25 @@ def tile_bcs_gap_step_s13_kernel(tc, phi, coef_bytes, coef_scale, energy, v_word
             )
 
         def energies(g0, g1, c):
-            return en[:, PACK * g0 : PACK * g1, c * NC : (c + 1) * NC]
+            first, width, count = CHUNK[c]
+            return en[:, PACK * g0 : PACK * g1, first : first + width]
 
-        def square_first_chunk():
-            squares = stage.tile([P, GROUPS * PACK, NC], F32, name="esq", tag="grp1", bufs=1, align_bytes=64)
-            for g0 in (0, HALF):
-                src = energies(g0, g0 + HALF, 0)
-                nc.gpsimd.tensor_tensor(out=squares[:, PACK * g0 : PACK * (g0 + HALF), :], in0=src, in1=src, op=MULT)
-            return squares
+        squares = {}
+
+        def square_energies(g0, g1, c, after):
+            room = stage.tile([P, (g1 - g0) * PACK, CHUNK[c][1]], F32, name="esq", tag="grp%d" % after, bufs=1, align_bytes=64)
+            for g in range(g0, g1, STEP):
+                src = energies(g, g + STEP, c)
+                nc.gpsimd.tensor_tensor(out=room[:, PACK * (g - g0) : PACK * (g - g0 + STEP), :], in0=src, in1=src, op=MULT)
+            for g in range(g0, g1):
+                squares[g, c] = (room, g0)
+
+        def inv_from_square(g0, g1, c):
+            room, base = squares[g0, c]
+            inv_sqrt(g0, g1, c, room[:, PACK * (g0 - base) : PACK * (g1 - base), :])
 
         def inv_sqrt(g0, g1, c, src):
-            tag = "inv" if g1 - g0 == 1 else "wide"
-            room = stage.tile([P, g1 - g0, NC // RUN, PACK, RUN], F32, name="inv", tag=tag, bufs=4, align_bytes=64)
+            room = stage.tile([P, g1 - g0, CHUNK[c][1] // RUN, PACK, RUN], F32, name="inv", tag="wide", bufs=WIDE, align_bytes=64)
             for g in range(g0, g1):
                 inv[g, c] = (room, g0)
             nc.scalar.activation(
@@ -196,18 +206,16 @@ def tile_bcs_gap_step_s13_kernel(tc, phi, coef_bytes, coef_scale, energy, v_word
                 func=ACT.Abs_reciprocal_sqrt,
             )
 
-        def inv_from_square(g):
-            inv_sqrt(g, g + 1, 0, squares[:, PACK * g : PACK * (g + 1), :])
+        def root(g0, g1, c):
+            inv_sqrt(g0, g1, c, energies(g0, g1, c))
 
-        def root(g0, c):
-            inv_sqrt(g0, g0 + HALF, c, energies(g0, g0 + HALF, c))
-
-        def square_root(g0, c):
-            values = inv[g0, c][0][:].rearrange("p g c t i -> p (g c t i)")
+        def square_root(g0, g1, c):
+            room, base = inv[g0, c]
+            values = room[:, g0 - base : g1 - base].rearrange("p g c t i -> p (g c t i)")
             nc.scalar.activation(out=values, in_=values, func=ACT.Square)
 
-        hc = [keep.tile([P, GROUPS, NC], U32, name="hc%d" % c, align_bytes=256) for c in range(CHUNKS)]
-        hs = [keep.tile([P, GROUPS, NC], U8, name="hs%d" % c, align_bytes=256) for c in range(CHUNKS)]
+        hc = [keep.tile([P, GROUPS, CHUNK[c][1]], U32, name="hc%d" % c, align_bytes=256) for c in range(len(CHUNK))]
+        hs = [keep.tile([P, GROUPS, CHUNK[c][1]], U8, name="hs%d" % c, align_bytes=256) for c in range(len(CHUNK))]
         gaps = {}
         hgrp = {}
 
@@ -238,11 +246,11 @@ def tile_bcs_gap_step_s13_kernel(tc, phi, coef_bytes, coef_scale, energy, v_word
 
         def make_h(g0, g1, c):
             room, base = inv[g0, c]
-            runs = NC // RUN
-            hgrp[g0, c] = stage.tile([P, g1 - g0, NC, PACK], BF16, name="hg", tag="hg", bufs=3, align_bytes=64)
+            first, width, count = CHUNK[c]
+            hgrp[g0, c] = stage.tile([P, g1 - g0, width, PACK], BF16, name="hg", tag="hg", bufs=3, align_bytes=64)
             nc.vector.tensor_tensor(
                 out=hgrp[g0, c][:].rearrange("p g (c i) t -> p g c t i", i=RUN),
-                in0=num[:, g0:g1, c * runs : (c + 1) * runs],
+                in0=num[:, g0:g1, first // RUN : (first + width) // RUN],
                 in1=room[:, g0 - base : g1 - base],
                 op=MULT,
             )
@@ -261,7 +269,7 @@ def tile_bcs_gap_step_s13_kernel(tc, phi, coef_bytes, coef_scale, energy, v_word
             for n in range(n0, n1):
                 c, i0, count = parts[n]
                 if g0 == 0:
-                    sums[n] = take_bank(("part", n), [P, count, NC])
+                    sums[n] = take_bank(("part", n), [P, count, CHUNK[c][1]])
                 for g in range(g0, g1):
                     for i in range(count):
                         tile_i = i0 + i
@@ -278,18 +286,19 @@ def tile_bcs_gap_step_s13_kernel(tc, phi, coef_bytes, coef_scale, energy, v_word
                     finished.append(n)
 
         def chunk_passes(c, g0, g1):
-            passes(PARTS * c, PARTS * (c + 1), g0, g1)
+            passes(first_part[c], first_part[c + 1], g0, g1)
 
         def store(on_scalar):
             n = finished.pop(0)
             c, i0, count = parts[n]
-            o = stage.tile([P, count, NC], F32, name="o", tag="o", bufs=8, align_bytes=64)
+            first, width = CHUNK[c][:2]
+            o = stage.tile([P, count, width], F32, name="o", tag="ph", bufs=8, align_bytes=64)
             if on_scalar:
                 nc.scalar.copy(out=o[:], in_=sums[n][:])
             else:
                 nc.vector.tensor_copy(out=o[:], in_=sums[n][:])
             give_back(("part", n))
-            nc.sync.dma_start(out=out_v[:, i0 : i0 + count, c * NC : (c + 1) * NC], in_=o[:])
+            nc.sync.dma_start(out=out_v[:, i0 : i0 + count, first : first + width], in_=o[:])
 
         def h_with_piece(g0, g1, c, g, piece):
             make_h(g0, g1, c)
@@ -302,9 +311,9 @@ def tile_bcs_gap_step_s13_kernel(tc, phi, coef_bytes, coef_scale, energy, v_word
             quant_h(g0, g1, c)
 
         def inv_with_store(g0, c):
-            root(g0, c)
+            root(g0, g0 + HALF, c)
             store(on_scalar=True)
-            square_root(g0, c)
+            square_root(g0, g0 + HALF, c)
 
         tanh(0, 0, 1)
         for k in range(PASSES):
@@ -324,19 +333,21 @@ def tile_bcs_gap_step_s13_kernel(tc, phi, coef_bytes, coef_scale, energy, v_word
         for piece in WHOLE:
             first_product(0, piece)
         quant_phi(1)
-
-        squares = square_first_chunk()
+        square_energies(0, 4, 0, 1)
         first_product(1, WHOLE[0])
-        first_product(1, WHOLE[1])
         for piece in WHOLE:
             times_gap(0, piece)
-        transposes(2 * PACK, 3 * PACK)
-        first_product(1, WHOLE[2])
-        first_product(1, WHOLE[3])
+        transposes(8, 10)
+        first_product(1, WHOLE[1])
+        transposes(10, 12)
         times_gap(1, WHOLE[0])
+        first_product(1, WHOLE[2])
+        empty_turned(8, 10, on_scalar=False)
         times_gap(1, WHOLE[1])
-        empty_turned(2 * PACK, 3 * PACK, on_scalar=False)
-        transposes(3 * PACK, TILES)
+        transposes(12, 14)
+        empty_turned(10, 12, on_scalar=False)
+        first_product(1, WHOLE[3])
+        transposes(14, 16)
         quant_phi(2)
 
         first_product(2, FIRST)
@@ -345,11 +356,11 @@ def tile_bcs_gap_step_s13_kernel(tc, phi, coef_bytes, coef_scale, energy, v_word
         times_gap(1, WHOLE[3])
         first_product(2, MIDDLE[1])
         first_product(2, LAST)
-        inv_from_square(0)
-        inv_from_square(1)
-        empty_turned(3 * PACK, TILES, on_scalar=True)
-        inv_from_square(2)
-        inv_from_square(3)
+        inv_from_square(0, 1, 0)
+        inv_from_square(1, 2, 0)
+        empty_turned(12, 16, on_scalar=True)
+        inv_from_square(2, 3, 0)
+        inv_from_square(3, 4, 0)
         make_h(0, 1, 0)
         make_h(1, 2, 0)
         quant_h(0, 1, 0)
@@ -357,52 +368,55 @@ def tile_bcs_gap_step_s13_kernel(tc, phi, coef_bytes, coef_scale, energy, v_word
         quant_h(1, 2, 0)
         times_gap(2, MIDDLE[0])
         quant_phi(3)
-
-        chunk_passes(0, 0, 1)
-        passes(0, PARTS // 2, 1, 2)
-        first_product(3, FIRST)
-        passes(PARTS // 2, PARTS, 1, 2)
         h_with_piece(2, 3, 0, 2, MIDDLE[1])
+        chunk_passes(0, 0, 1)
+        passes(0, 2, 1, 2)
+        first_product(3, FIRST)
+        passes(2, 4, 1, 2)
         times_gap(3, FIRST)
         times_gap(2, LAST)
         first_product(3, MIDDLE[0])
         chunk_passes(0, 2, 3)
         first_product(3, MIDDLE[1])
+        root(0, 2, 1)
+        root(2, 4, 1)
+        square_root(0, 2, 1)
+        square_root(2, 4, 1)
         h_with_piece(3, 4, 0, 3, MIDDLE[0])
         chunk_passes(0, 3, 4)
-
-        for g0 in (0, HALF):
-            root(g0, 1)
-        for g0 in (0, HALF):
-            square_root(g0, 1)
         h_with_piece(0, 1, 1, 3, MIDDLE[1])
         chunk_passes(1, 0, 1)
         inv_with_store(0, 2)
         first_product(3, LAST)
         h_with_store(1, 2, 1)
         chunk_passes(1, 1, 2)
+        root(2, 4, 2)
+        store(True)
         h_with_store(HALF, GROUPS, 1)
         chunk_passes(1, HALF, GROUPS)
-        inv_with_store(HALF, 2)
-
+        square_root(2, 4, 2)
         third = 2 * PARTS
         h_with_store(0, HALF, 2)
         passes(third, third + AHEAD_IN_THIRD_CHUNK, 0, HALF)
         inv_with_store(0, 3)
-        h_with_piece(HALF, GROUPS, 2, 3, LAST)
+        h_with_store(HALF, GROUPS, 2)
         passes(third, third + AHEAD_IN_THIRD_CHUNK, HALF, GROUPS)
+        store(on_scalar=False)
+        root(HALF, GROUPS, 3)
         passes(third + AHEAD_IN_THIRD_CHUNK, third + PARTS, 0, GROUPS)
-        store(on_scalar=False)
-        store(on_scalar=False)
-        inv_with_store(HALF, 3)
-
+        times_gap(3, LAST)
+        store(True)
+        square_root(2, 3, 3)
+        square_root(3, 4, 3)
         last = 3 * PARTS
         h_with_store(0, HALF, 3)
+        store(on_scalar=True)
         passes(last, last + AHEAD_IN_LAST_CHUNK, 0, HALF)
+        make_h(2, 3, 3)
+        make_h(3, 4, 3)
+        quant_h(2, 3, 3)
+        quant_h(3, 4, 3)
         store(on_scalar=True)
-        store(on_scalar=True)
-        make_h(HALF, GROUPS, 3)
-        quant_h(HALF, GROUPS, 3)
         for n in range(last, len(parts)):
             passes(n, n + 1, HALF if n < last + AHEAD_IN_LAST_CHUNK else 0, GROUPS)
             store(on_scalar=(n % 2 == 1))

@@ -40,7 +40,7 @@ LAST = (B - NC, NC, 0)
 SLOTS_WIDENED_BY_VECTOR = 2
 TILES_EMPTIED_BEFORE_TANH = 6
 CHUNK = [(0, 128, 4), (128, 128, 4), (256, 128, 4), (384, 128, 2)]
-WIDE = 8
+WIDE = 10
 STEP = 2
 AHEAD_IN_THIRD_CHUNK = 3
 AHEAD_IN_LAST_CHUNK = 4
@@ -184,17 +184,16 @@ def tile_bcs_gap_step_s13_kernel(tc, phi, coef_bytes, coef_scale, energy, v_word
 
         squares = {}
 
-        def square_energies(g0, g1, c, after):
-            room = stage.tile([P, (g1 - g0) * PACK, CHUNK[c][1]], F32, name="esq", tag="grp%d" % after, bufs=1, align_bytes=64)
-            for g in range(g0, g1, STEP):
-                src = energies(g, g + STEP, c)
-                nc.gpsimd.tensor_tensor(out=room[:, PACK * (g - g0) : PACK * (g - g0 + STEP), :], in0=src, in1=src, op=MULT)
-            for g in range(g0, g1):
-                squares[g, c] = (room, g0)
+        def square_energies(room, g0, g1, c0, c1):
+            first, last = CHUNK[c0][0], CHUNK[c1 - 1][0] + CHUNK[c1 - 1][1]
+            src = en[:, PACK * g0 : PACK * g1, first:last]
+            dst = room.rearrange("p (r n) -> p r n", n=last - first)
+            nc.gpsimd.tensor_tensor(out=dst, in0=src, in1=src, op=MULT)
+            for c in range(c0, c1):
+                squares[c, g0] = dst[:, :, CHUNK[c][0] - first : CHUNK[c][0] - first + CHUNK[c][1]]
 
-        def inv_from_square(g0, g1, c):
-            room, base = squares[g0, c]
-            inv_sqrt(g0, g1, c, room[:, PACK * (g0 - base) : PACK * (g1 - base), :])
+        def inv_from_square(g0, g1, c, base):
+            inv_sqrt(g0, g1, c, squares[c, base][:, PACK * (g0 - base) : PACK * (g1 - base), :])
 
         def inv_sqrt(g0, g1, c, src):
             room = stage.tile([P, g1 - g0, CHUNK[c][1] // RUN, PACK, RUN], F32, name="inv", tag="wide", bufs=WIDE, align_bytes=64)
@@ -332,8 +331,11 @@ def tile_bcs_gap_step_s13_kernel(tc, phi, coef_bytes, coef_scale, energy, v_word
         empty_turned(TILES_EMPTIED_BEFORE_TANH, BANKS, on_scalar=False)
         for piece in WHOLE:
             first_product(0, piece)
-        quant_phi(1)
-        square_energies(0, 4, 0, 1)
+        quant_phi(1, 0, 2)
+        quant_phi(1, 2, 4)
+        room = stage.tile([P, 2, 1024], F32, name="esq", tag="grp1", bufs=1, align_bytes=64)
+        square_energies(room[:, 0], 0, 2, 0, 1)
+        square_energies(room[:, 1], 2, 3, 0, 2)
         first_product(1, WHOLE[0])
         for piece in WHOLE:
             times_gap(0, piece)
@@ -348,7 +350,8 @@ def tile_bcs_gap_step_s13_kernel(tc, phi, coef_bytes, coef_scale, energy, v_word
         empty_turned(10, 12, on_scalar=False)
         first_product(1, WHOLE[3])
         transposes(14, 16)
-        quant_phi(2)
+        quant_phi(2, 0, 2)
+        quant_phi(2, 2, 4)
 
         first_product(2, FIRST)
         first_product(2, MIDDLE[0])
@@ -356,18 +359,26 @@ def tile_bcs_gap_step_s13_kernel(tc, phi, coef_bytes, coef_scale, energy, v_word
         times_gap(1, WHOLE[3])
         first_product(2, MIDDLE[1])
         first_product(2, LAST)
-        inv_from_square(0, 1, 0)
-        inv_from_square(1, 2, 0)
-        empty_turned(12, 16, on_scalar=True)
-        inv_from_square(2, 3, 0)
-        inv_from_square(3, 4, 0)
+        empty_turned(12, 13, on_scalar=False)
+        inv_from_square(0, 1, 0, 0)
+        inv_from_square(1, 2, 0, 0)
+        empty_turned(13, 16, on_scalar=True)
+        inv_from_square(2, 3, 0, 2)
+        root(3, 4, 0)
+        root(0, 2, 1)
+        square_root(3, 4, 0)
+        square_root(0, 2, 1)
+        root(3, 4, 1)
+        inv_from_square(2, 3, 1, 2)
+        square_root(3, 4, 1)
         make_h(0, 1, 0)
         make_h(1, 2, 0)
         quant_h(0, 1, 0)
         times_gap(2, FIRST)
         quant_h(1, 2, 0)
         times_gap(2, MIDDLE[0])
-        quant_phi(3)
+        quant_phi(3, 0, 2)
+        quant_phi(3, 2, 4)
         h_with_piece(2, 3, 0, 2, MIDDLE[1])
         chunk_passes(0, 0, 1)
         passes(0, 2, 1, 2)
@@ -378,10 +389,6 @@ def tile_bcs_gap_step_s13_kernel(tc, phi, coef_bytes, coef_scale, energy, v_word
         first_product(3, MIDDLE[0])
         chunk_passes(0, 2, 3)
         first_product(3, MIDDLE[1])
-        root(0, 2, 1)
-        root(2, 4, 1)
-        square_root(0, 2, 1)
-        square_root(2, 4, 1)
         h_with_piece(3, 4, 0, 3, MIDDLE[0])
         chunk_passes(0, 3, 4)
         h_with_piece(0, 1, 1, 3, MIDDLE[1])
@@ -391,8 +398,12 @@ def tile_bcs_gap_step_s13_kernel(tc, phi, coef_bytes, coef_scale, energy, v_word
         h_with_store(1, 2, 1)
         chunk_passes(1, 1, 2)
         root(2, 4, 2)
+        make_h(2, 3, 1)
+        make_h(3, 4, 1)
+        quant_h(2, 3, 1)
+        store(False)
         store(True)
-        h_with_store(HALF, GROUPS, 1)
+        quant_h(3, 4, 1)
         chunk_passes(1, HALF, GROUPS)
         square_root(2, 4, 2)
         third = 2 * PARTS

@@ -40,7 +40,7 @@ LAST = (B - NC, NC, 0)
 SLOTS_WIDENED_BY_VECTOR = 2
 TILES_EMPTIED_BEFORE_TANH = 6
 CHUNK = [(0, 128, 4), (128, 128, 4), (256, 128, 4), (384, 128, 2)]
-WIDE = 10
+WIDE = 8
 STEP = 2
 AHEAD_IN_THIRD_CHUNK = 3
 AHEAD_IN_LAST_CHUNK = 4
@@ -291,7 +291,7 @@ def tile_bcs_gap_step_s13_kernel(tc, phi, coef_bytes, coef_scale, energy, v_word
             n = finished.pop(0)
             c, i0, count = parts[n]
             first, width = CHUNK[c][:2]
-            o = stage.tile([P, count, width], F32, name="o", tag="ph", bufs=8, align_bytes=64)
+            o = stage.tile([P, count, width], F32, name="o", tag="ph" if n < first_part[-2] else "last", bufs=8, align_bytes=64)
             if on_scalar:
                 nc.scalar.copy(out=o[:], in_=sums[n][:])
             else:
@@ -350,16 +350,16 @@ def tile_bcs_gap_step_s13_kernel(tc, phi, coef_bytes, coef_scale, energy, v_word
         empty_turned(10, 12, on_scalar=False)
         first_product(1, WHOLE[3])
         transposes(14, 16)
+        times_gap(1, WHOLE[2])
         quant_phi(2, 0, 2)
         quant_phi(2, 2, 4)
 
         first_product(2, FIRST)
         first_product(2, MIDDLE[0])
-        times_gap(1, WHOLE[2])
+        empty_turned(12, 13, on_scalar=False)
         times_gap(1, WHOLE[3])
         first_product(2, MIDDLE[1])
         first_product(2, LAST)
-        empty_turned(12, 13, on_scalar=False)
         inv_from_square(0, 1, 0, 0)
         inv_from_square(1, 2, 0, 0)
         empty_turned(13, 16, on_scalar=True)
@@ -389,12 +389,12 @@ def tile_bcs_gap_step_s13_kernel(tc, phi, coef_bytes, coef_scale, energy, v_word
         first_product(3, MIDDLE[0])
         chunk_passes(0, 2, 3)
         first_product(3, MIDDLE[1])
+        first_product(3, LAST)
         h_with_piece(3, 4, 0, 3, MIDDLE[0])
         chunk_passes(0, 3, 4)
         h_with_piece(0, 1, 1, 3, MIDDLE[1])
-        chunk_passes(1, 0, 1)
         inv_with_store(0, 2)
-        first_product(3, LAST)
+        chunk_passes(1, 0, 1)
         h_with_store(1, 2, 1)
         chunk_passes(1, 1, 2)
         root(2, 4, 2)

from contextlib import ExitStack

import concourse.mybir as mybir
from concourse.masks import make_identity

M, R, B = 2048, 1024, 512
FLOPS = 2 * M * R * B + 2 * M * M * B

F32 = mybir.dt.float32
BF16 = mybir.dt.bfloat16
U32 = mybir.dt.uint32
I32 = mybir.dt.int32
U8 = mybir.dt.uint8
FP8 = mybir.dt.float8_e4m3fn
FP8X4 = mybir.dt.float8_e4m3fn_x4
FP4X4 = mybir.dt.float4_e2m1fn_x4
ACT = mybir.ActivationFunctionType
MULT = mybir.AluOpType.mult

P = 128
PACK = 4
GROUPS = M // (P * PACK)
HALF = GROUPS // 2
PASSES = R // (P * PACK)
TILES = M // P
RUN = 4
BANKS = 8
BANK_COLS = 512
NC = 128
CHUNKS = B // NC
PART = BANK_COLS // NC
LAST_PART = 2
PARTS = TILES // PART

WHOLE = [(0, B, t) for t in range(PACK)]
FIRST = (0, NC, 0)
MIDDLE = [(NC, 2 * NC, n) for n in range(2)]
LAST = (B - NC, NC, 0)

SLOTS_WIDENED_BY_VECTOR = 2
TILES_EMPTIED_BEFORE_TANH = 6
CHUNK = [(0, 128, 4), (128, 128, 4), (256, 128, 4), (384, 128, 2)]
WIDE = 8
STEP = 2
AHEAD_IN_THIRD_CHUNK = 3
AHEAD_IN_LAST_CHUNK = 4


def tile_bcs_gap_step_s13_kernel(tc, phi, coef_bytes, coef_scale, energy, v_words, v_scales, out):
    nc = tc.nc
    parts = [(c, i0, count) for c, (first, width, count) in enumerate(CHUNK) for i0 in range(0, TILES, count)]
    first_part = [sum(TILES // count for first, width, count in CHUNK[:c]) for c in range(len(CHUNK) + 1)]

    with ExitStack() as ctx:
        keep = ctx.enter_context(tc.tile_pool(name="keep", bufs=1))
        stage = ctx.enter_context(tc.tile_pool(name="stage", bufs=2))
        psum = ctx.enter_context(tc.psum_pool(name="psum", bufs=1))
        ctx.enter_context(tc.manual_schedule())

        free_banks = list(range(BANKS))
        bank_of = {}

        def take_bank(user, shape):
            bank_of[user] = free_banks.pop(0)
            return psum.tile(shape, F32, name="bank", tag="bank%d" % bank_of[user], bufs=1)

        def give_back(user):
            free_banks.append(bank_of[user])

        en = keep.tile([P, GROUPS * PACK, B], BF16, name="en", align_bytes=64)
        ph = [stage.tile([P, 2, R], BF16, name="ph", tag="ph", bufs=8, align_bytes=64) for pair in range(TILES // 2)]
        cb = [keep.tile([P, PACK * B], U8, name="cb%d" % k, align_bytes=64) for k in range(PASSES)]
        cs = keep.tile([P, PASSES, PACK], F32, name="cs", align_bytes=64)
        vw = [keep.tile([P, 2 * M], U8, name="vw%d" % g, align_bytes=256) for g in range(GROUPS)]
        vs = keep.tile([P, GROUPS, M], U8, name="vs", align_bytes=256)
        ident = keep.tile([P, P], F32, name="ident", align_bytes=64)

        phi_v = phi.rearrange("(g p t) k -> g p t k", p=P, t=PACK)
        en_v = energy.rearrange("(g p t) n -> g p t n", p=P, t=PACK)
        cb_v = coef_bytes.rearrange("(k p t) n -> k p (t n)", p=P, t=PACK)
        cs_v = coef_scale.rearrange("(k p t) o -> p k (t o)", p=P, t=PACK)
        vs_v = v_scales.rearrange("g (q r) n -> r q g n", r=4)
        out_v = out.rearrange("(i p) n -> p i n", p=P)

        def load_energy(g, t0=0, t1=PACK):
            nc.sync.dma_start(out=en[:, PACK * g + t0 : PACK * g + t1, :], in_=en_v[g][:, t0:t1, :])

        def load_phi(pair):
            g, half = divmod(pair, 2)
            nc.sync.dma_start(out=ph[pair][:], in_=phi_v[g][:, 2 * half : 2 * half + 2, :])

        def load_v(g0, g1):
            for r in range(4):
                nc.sync.dma_start(out=vs[r:P:32, g0:g1, :].bitcast(I32), in_=vs_v[r][:, g0:g1, :].bitcast(I32))
            for g in range(g0, g1):
                nc.sync.dma_start(out=vw[g][:], in_=v_words[g])

        make_identity(nc, ident[:])
        nc.vector.memset(vs[:].rearrange("p g n -> p (g n)").bitcast(I32), 0)

        nc.sync.dma_start(out=cs[:], in_=cs_v)
        load_energy(0, 0, 1)
        for k in range(PASSES):
            nc.sync.dma_start(out=cb[k][:], in_=cb_v[k])
        for pair in range(BANKS // 2):
            load_phi(pair)
        load_energy(0, 1, PACK)
        for g in range(1, GROUPS):
            load_energy(g)
            load_phi(BANKS // 2 + g - 1)
        load_phi(TILES // 2 - 1)
        load_v(0, HALF)
        load_v(HALF, GROUPS)

        cc = keep.tile([P, PASSES, B], U32, name="cc", align_bytes=256)
        csc = keep.tile([P, PASSES, B], U8, name="csc", align_bytes=256)
        wide = [stage.tile([P, PACK, B], BF16, name="wide", tag="wide", bufs=WIDE, align_bytes=64) for k in range(PASSES)]
        cgrp = [stage.tile([P, B, PACK], BF16, name="cgrp", tag="wide", bufs=WIDE, align_bytes=64) for k in range(PASSES)]

        def coef_widen(k):
            for t in range(PACK):
                codes = cb[k][:, t * B : (t + 1) * B].bitcast(FP8)
                scale = cs[:, k, t : t + 1]
                if t < SLOTS_WIDENED_BY_VECTOR:
                    nc.vector.tensor_scalar(out=wide[k][:, t, :], in0=codes, scalar1=scale, scalar2=None, op0=MULT)
                else:
                    nc.scalar.activation(out=wide[k][:, t, :], in_=codes, func=ACT.Copy, scale=scale)

        def coef_interleave(k):
            nc.vector.tensor_copy(
                out=cgrp[k][:].rearrange("p (c i) t -> p c t i", i=RUN),
                in_=wide[k][:].rearrange("p t (c i) -> p c t i", i=RUN),
            )

        def coef_quant(k):
            nc.vector.quantize_mx(out=cc[:, k, :].bitcast(FP8X4), scales=csc[:, k, :], in_=cgrp[k][:].rearrange("p n t -> p (n t)"))

        pc = [keep.tile([P, PACK, PASSES, P], U32, name="pc%d" % g, align_bytes=256) for g in range(GROUPS)]
        psc = [keep.tile([P, PACK, PASSES, P], U8, name="psc%d" % g, align_bytes=256) for g in range(GROUPS)]
        turned = {}
        grouped = {}

        def transposes(j0, j1):
            for j in range(j0, j1):
                turned[j] = take_bank(("turned", j), [P, PASSES, 2, P])
                words = ph[j // 2][:, j % 2, :].bitcast(F32)
                for k in range(PASSES):
                    for u in range(2):
                        nc.tensor.transpose(turned[j][:, k, u, :], words[:, 256 * k + u : 256 * (k + 1) : 2], ident[:])

        def empty_turned(j0, j1, on_scalar):
            for j in range(j0, j1):
                g, t = divmod(j, PACK)
                if t == 0:
                    grouped[g] = stage.tile([P, PACK, PASSES * P * PACK], BF16, name="grp", tag="grp%d" % g, bufs=1, align_bytes=64)
                dst = grouped[g][:, t, :].bitcast(F32).rearrange("p (k r u) -> p k r u", k=PASSES, u=2)
                src = turned[j][:].rearrange("p k u r -> p k r u")
                if on_scalar:
                    nc.scalar.copy(out=dst, in_=src)
                else:
                    nc.vector.tensor_copy(out=dst, in_=src)
                give_back(("turned", j))

        def quant_phi(g, t0=0, t1=PACK):
            nc.vector.quantize_mx(
                out=pc[g][:, t0:t1].rearrange("p t k r -> p (t k r)").bitcast(FP8X4),
                scales=psc[g][:, t0:t1].rearrange("p t k r -> p (t k r)"),
                in_=grouped[g][:, t0:t1].rearrange("p t x -> p (t x)"),
            )

        num = keep.tile([P, GROUPS, B // RUN, PACK, RUN], F32, name="num", align_bytes=64)
        inv = {}

        def tanh(g, t0=0, t1=PACK):
            nc.scalar.activation(
                out=num[:, g, :, t0:t1, :].rearrange("p c t i -> p t c i"),
                in_=en[:, PACK * g + t0 : PACK * g + t1, :].rearrange("p t (c i) -> p t c i", i=RUN),
                func=ACT.Tanh,
            )

        def energies(g0, g1, c):
            first, width, count = CHUNK[c]
            return en[:, PACK * g0 : PACK * g1, first : first + width]

        squares = {}

        def square_energies(room, g0, g1, c0, c1):
            first, last = CHUNK[c0][0], CHUNK[c1 - 1][0] + CHUNK[c1 - 1][1]
            src = en[:, PACK * g0 : PACK * g1, first:last]
            dst = room.rearrange("p (r n) -> p r n", n=last - first)
            nc.gpsimd.tensor_tensor(out=dst, in0=src, in1=src, op=MULT)
            for c in range(c0, c1):
                squares[c, g0] = dst[:, :, CHUNK[c][0] - first : CHUNK[c][0] - first + CHUNK[c][1]]

        def inv_from_square(g0, g1, c, base):
            inv_sqrt(g0, g1, c, squares[c, base][:, PACK * (g0 - base) : PACK * (g1 - base), :])

        def inv_sqrt(g0, g1, c, src):
            room = stage.tile([P, g1 - g0, CHUNK[c][1] // RUN, PACK, RUN], F32, name="inv", tag="wide", bufs=WIDE, align_bytes=64)
            for g in range(g0, g1):
                inv[g, c] = (room, g0)
            nc.scalar.activation(
                out=room[:].rearrange("p g c t i -> p t g c i"),
                in_=src.rearrange("p (g t) (c i) -> p t g c i", t=PACK, i=RUN),
                func=ACT.Abs_reciprocal_sqrt,
            )

        def root(g0, g1, c):
            inv_sqrt(g0, g1, c, energies(g0, g1, c))

        def square_root(g0, g1, c):
            room, base = inv[g0, c]
            values = room[:, g0 - base : g1 - base].rearrange("p g c t i -> p (g c t i)")
            nc.scalar.activation(out=values, in_=values, func=ACT.Square)

        hc = [keep.tile([P, GROUPS, CHUNK[c][1]], U32, name="hc%d" % c, align_bytes=256) for c in range(len(CHUNK))]
        hs = [keep.tile([P, GROUPS, CHUNK[c][1]], U8, name="hs%d" % c, align_bytes=256) for c in range(len(CHUNK))]
        gaps = {}
        hgrp = {}

        def first_product(g, piece):
            first, width, n = piece
            count = BANK_COLS // width
            gaps[g, piece] = take_bank(("gap", g, piece), [P, count, width])
            cols = slice(first, first + width)
            for i in range(count):
                t = n * count + i
                for k in range(PASSES):
                    nc.tensor.matmul_mx(
                        out=gaps[g, piece][:, i, :],
                        lhsT=pc[g][:, t, k, :].bitcast(FP8X4),
                        lhsT_scale=psc[g][:, t, k, :],
                        rhs=cc[:, k, cols].bitcast(FP8X4),
                        rhs_scale=csc[:, k, cols],
                        start=(k == 0),
                        stop=(k == PASSES - 1),
                    )

        def times_gap(g, piece):
            first, width, n = piece
            count = BANK_COLS // width
            w = num[:, g, first // RUN : (first + width) // RUN, n * count : (n + 1) * count, :].rearrange("p c t i -> p t c i")
            nc.vector.tensor_tensor(out=w, in0=gaps[g, piece][:].rearrange("p t (c i) -> p t c i", i=RUN), in1=w, op=MULT)
            give_back(("gap", g, piece))

        def make_h(g0, g1, c):
            room, base = inv[g0, c]
            first, width, count = CHUNK[c]
            hgrp[g0, c] = stage.tile([P, g1 - g0, width, PACK], BF16, name="hg", tag="hg", bufs=3, align_bytes=64)
            nc.vector.tensor_tensor(
                out=hgrp[g0, c][:].rearrange("p g (c i) t -> p g c t i", i=RUN),
                in0=num[:, g0:g1, first // RUN : (first + width) // RUN],
                in1=room[:, g0 - base : g1 - base],
                op=MULT,
            )

        def quant_h(g0, g1, c):
            nc.vector.quantize_mx(
                out=hc[c][:, g0:g1, :].rearrange("p g n -> p (g n)").bitcast(FP8X4),
                scales=hs[c][:, g0:g1, :].rearrange("p g n -> p (g n)"),
                in_=hgrp[g0, c][:].rearrange("p g n t -> p (g n t)"),
            )

        sums = {}
        finished = []

        def passes(n0, n1, g0, g1):
            for n in range(n0, n1):
                c, i0, count = parts[n]
                if g0 == 0:
                    sums[n] = take_bank(("part", n), [P, count, CHUNK[c][1]])
                for g in range(g0, g1):
                    for i in range(count):
                        tile_i = i0 + i
                        nc.tensor.matmul_mx(
                            out=sums[n][:, i, :],
                            lhsT=vw[g][:, 2 * P * tile_i : 2 * P * (tile_i + 1)].bitcast(FP4X4),
                            lhsT_scale=vs[:, g, P * tile_i : P * (tile_i + 1)],
                            rhs=hc[c][:, g, :].bitcast(FP8X4),
                            rhs_scale=hs[c][:, g, :],
                            start=(g == 0 and i == 0),
                            stop=(g == GROUPS - 1 and i == count - 1),
                        )
                if g1 == GROUPS:
                    finished.append(n)

        def chunk_passes(c, g0, g1):
            passes(first_part[c], first_part[c + 1], g0, g1)

        def store(on_scalar):
            n = finished.pop(0)
            c, i0, count = parts[n]
            first, width = CHUNK[c][:2]
            o = stage.tile([P, count, width], F32, name="o", tag="ph" if n < first_part[-2] else "last", bufs=8, align_bytes=64)
            if on_scalar:
                nc.scalar.copy(out=o[:], in_=sums[n][:])
            else:
                nc.vector.tensor_copy(out=o[:], in_=sums[n][:])
            give_back(("part", n))
            nc.sync.dma_start(out=out_v[:, i0 : i0 + count, first : first + width], in_=o[:])

        def h_with_piece(g0, g1, c, g, piece):
            make_h(g0, g1, c)
            times_gap(g, piece)
            quant_h(g0, g1, c)

        def h_with_store(g0, g1, c):
            make_h(g0, g1, c)
            store(on_scalar=False)
            quant_h(g0, g1, c)

        def inv_with_store(g0, c):
            root(g0, g0 + HALF, c)
            store(on_scalar=True)
            square_root(g0, g0 + HALF, c)

        tanh(0, 0, 1)
        for k in range(PASSES):
            coef_widen(k)
        for k in range(PASSES):
            coef_interleave(k)
        for k in range(PASSES):
            coef_quant(k)
        transposes(0, BANKS)
        empty_turned(0, TILES_EMPTIED_BEFORE_TANH, on_scalar=True)
        tanh(0, 1, PACK)
        for g in range(1, GROUPS):
            tanh(g)
        quant_phi(0, 0, 2)
        quant_phi(0, 2, PACK)
        empty_turned(TILES_EMPTIED_BEFORE_TANH, BANKS, on_scalar=False)
        for piece in WHOLE:
            first_product(0, piece)
        quant_phi(1, 0, 2)
        quant_phi(1, 2, 4)
        room = stage.tile([P, 2, 1024], F32, name="esq", tag="grp1", bufs=1, align_bytes=64)
        square_energies(room[:, 0], 0, 2, 0, 1)
        square_energies(room[:, 1], 2, 3, 0, 2)
        first_product(1, WHOLE[0])
        for piece in WHOLE:
            times_gap(0, piece)
        transposes(8, 10)
        first_product(1, WHOLE[1])
        transposes(10, 12)
        times_gap(1, WHOLE[0])
        first_product(1, WHOLE[2])
        empty_turned(8, 10, on_scalar=False)
        times_gap(1, WHOLE[1])
        transposes(12, 14)
        empty_turned(10, 12, on_scalar=False)
        first_product(1, WHOLE[3])
        transposes(14, 16)
        times_gap(1, WHOLE[2])
        quant_phi(2, 0, 2)
        quant_phi(2, 2, 4)

        first_product(2, FIRST)
        first_product(2, MIDDLE[0])
        empty_turned(12, 13, on_scalar=False)
        times_gap(1, WHOLE[3])
        first_product(2, MIDDLE[1])
        first_product(2, LAST)
        inv_from_square(0, 1, 0, 0)
        inv_from_square(1, 2, 0, 0)
        empty_turned(13, 16, on_scalar=True)
        inv_from_square(2, 3, 0, 2)
        root(3, 4, 0)
        root(0, 2, 1)
        square_root(3, 4, 0)
        square_root(0, 2, 1)
        root(3, 4, 1)
        inv_from_square(2, 3, 1, 2)
        square_root(3, 4, 1)
        make_h(0, 1, 0)
        make_h(1, 2, 0)
        quant_h(0, 1, 0)
        times_gap(2, FIRST)
        quant_h(1, 2, 0)
        times_gap(2, MIDDLE[0])
        quant_phi(3, 0, 2)
        quant_phi(3, 2, 4)
        h_with_piece(2, 3, 0, 2, MIDDLE[1])
        chunk_passes(0, 0, 1)
        passes(0, 2, 1, 2)
        first_product(3, FIRST)
        passes(2, 4, 1, 2)
        times_gap(3, FIRST)
        times_gap(2, LAST)
        first_product(3, MIDDLE[0])
        chunk_passes(0, 2, 3)
        first_product(3, MIDDLE[1])
        first_product(3, LAST)
        h_with_piece(3, 4, 0, 3, MIDDLE[0])
        chunk_passes(0, 3, 4)
        h_with_piece(0, 1, 1, 3, MIDDLE[1])
        inv_with_store(0, 2)
        chunk_passes(1, 0, 1)
        h_with_store(1, 2, 1)
        chunk_passes(1, 1, 2)
        root(2, 4, 2)
        make_h(2, 3, 1)
        make_h(3, 4, 1)
        quant_h(2, 3, 1)
        store(False)
        store(True)
        quant_h(3, 4, 1)
        chunk_passes(1, HALF, GROUPS)
        square_root(2, 4, 2)
        third = 2 * PARTS
        h_with_store(0, HALF, 2)
        passes(third, third + AHEAD_IN_THIRD_CHUNK, 0, HALF)
        inv_with_store(0, 3)
        h_with_store(HALF, GROUPS, 2)
        passes(third, third + AHEAD_IN_THIRD_CHUNK, HALF, GROUPS)
        store(on_scalar=False)
        root(HALF, GROUPS, 3)
        passes(third + AHEAD_IN_THIRD_CHUNK, third + PARTS, 0, GROUPS)
        times_gap(3, LAST)
        store(True)
        square_root(2, 3, 3)
        square_root(3, 4, 3)
        last = 3 * PARTS
        h_with_store(0, HALF, 3)
        store(on_scalar=True)
        passes(last, last + AHEAD_IN_LAST_CHUNK, 0, HALF)
        make_h(2, 3, 3)
        make_h(3, 4, 3)
        quant_h(2, 3, 3)
        quant_h(3, 4, 3)
        store(on_scalar=True)
        for n in range(last, len(parts)):
            passes(n, n + 1, HALF if n < last + AHEAD_IN_LAST_CHUNK else 0, GROUPS)
            store(on_scalar=(n % 2 == 1))
